import numpy as np
import ml_dtypes


def mxq(x, axis, fmt="e4m3"):
    dtype, down = {"e4m3": (ml_dtypes.float8_e4m3fn, 7), "e5m2": (ml_dtypes.float8_e5m2, 14)}[fmt]
    v = np.moveaxis(np.asarray(x, np.float32).astype(ml_dtypes.bfloat16).astype(np.float64), axis, -1)
    blocks = v.reshape(v.shape[:-1] + (-1, 32))
    amax = np.abs(blocks).max(-1, keepdims=True)
    byte = np.maximum(np.where(amax > 0, np.frexp(amax)[1] - 1 + 127, 0) - down, 1)
    scale = np.exp2(byte - 127.0)
    codes = (blocks / scale).astype(np.float32).astype(dtype).astype(np.float64)
    return np.moveaxis((codes * scale).reshape(v.shape), -1, axis)


WIDE = False


def mx_kscale(k):
    if not WIDE:
        return np.ones(k)
    levels = np.array([24, -24, 12, -12, 0])
    if k % 512:
        return np.exp2(np.random.permutation(np.resize(levels, k // 32))).repeat(32)
    a = np.empty((k // 512, 16))
    for p in range(k // 512):
        a[p, :8] = np.random.permutation(np.resize(levels, 8))
        for g in range(8):
            far = levels[np.abs(levels - a[p, g]) >= 10]
            a[p, g + 8] = far[np.random.randint(len(far))]
    return np.exp2(a.ravel()).repeat(32)


def f64(x):
    return np.asarray(x).astype(np.float64)


def striped(idx):
    return np.tile(idx.reshape(-1, 16).T, (8, 1)).astype(np.uint16)


def unstriped(offs):
    return offs[:16].T.reshape(-1).astype(np.int64)


E2M1 = np.array([0.0, 0.5, 1.0, 1.5, 2.0, 3.0, 4.0, 6.0, -0.0, -0.5, -1.0, -1.5, -2.0, -3.0, -4.0, -6.0])


def pack_weight(w, fmt):
    k, n = w.shape
    w = f64(np.asarray(w, np.float32).astype(ml_dtypes.bfloat16)).reshape(k // 32, 32, n)
    amax = np.abs(w).max(1)
    if fmt == "e4m3":
        byte = np.frexp(amax)[1] - 1 + 127 - 7
    else:
        mant, ex = np.frexp(amax / 6.0)
        byte = np.where(mant > 0.5, ex, ex - 1) + 127
    byte = np.clip(np.where(amax > 0, byte, 1), 1, 254)
    scaled = (w * np.exp2(127.0 - byte)[:, None, :]).reshape(k, n).astype(np.float32)
    by_word = np.ascontiguousarray(scaled.reshape(k // 512, 128, 4, n).transpose(0, 1, 3, 2))
    if fmt == "e4m3":
        words = by_word.astype(ml_dtypes.float8_e4m3fn).view(np.uint8)
    else:
        c = by_word.astype(ml_dtypes.float4_e2m1fn).view(np.uint8) & 0xF
        words = (c[..., 0::2] | (c[..., 1::2] << 4)).reshape(k // 512, 128, 2 * n)
    return np.ascontiguousarray(words), np.ascontiguousarray(byte.astype(np.uint8).reshape(k // 512, 16, n))


def unpack_weight(words, scales, fmt):
    g, _, n = scales.shape
    words = np.ascontiguousarray(words).reshape(g, 128, n, -1)
    if fmt == "e4m3":
        vals = words.view(ml_dtypes.float8_e4m3fn).astype(np.float64)
    else:
        nib = np.empty((g, 128, n, 4), np.uint8)
        nib[..., 0::2] = words & 0xF
        nib[..., 1::2] = words >> 4
        vals = E2M1[nib]
    vals = vals * np.repeat(np.exp2(scales.astype(np.float64) - 127.0), 8, axis=1)[..., None]
    return vals.transpose(0, 1, 3, 2).reshape(g * 512, n)


K, R, N, T, J = 1024, 1024, 512, 2048, 1024


def setup_inputs():
    n = np.random.standard_normal
    s = mx_kscale(K)[:, None]
    u = mx_kscale(R)[:, None]
    p_tab = pack_weight(n((K, T)) * s, "e4m3")
    p_ws = pack_weight(n((K, R)) / np.sqrt(2 * K) / s * u.T, "e4m3")
    p_wt = pack_weight(n((K, R)) / np.sqrt(2 * K) / s * u.T, "e2m1")
    return {
        "tab_words": p_tab[0],
        "tab_scales": p_tab[1],
        "ws_words": p_ws[0],
        "ws_scales": p_ws[1],
        "wt_words": p_wt[0],
        "wt_scales": p_wt[1],
        "wd": (n((R, N)) / np.sqrt(R) / u).astype(np.float32),
        "rT": (n((N, T))).astype(np.float32),
        "wgo": np.tile(np.random.uniform(0.5, 2.0, J), (128, 1)).astype(np.float32),
        "offs": striped(np.random.permutation(T)[:J]),
        "offs2": striped(np.random.permutation(T)[:J]),
    }


def reference(tab_words, tab_scales, ws_words, ws_scales, wt_words, wt_scales, wd, rT, wgo, offs, offs2):
    idx = unstriped(offs)
    idx2 = unstriped(offs2)
    tab_ = unpack_weight(tab_words, tab_scales, "e4m3")[:, idx]
    tabb_ = unpack_weight(tab_words, tab_scales, "e4m3")[:, idx2]
    ws_ = unpack_weight(ws_words, ws_scales, "e4m3")
    wt_ = unpack_weight(wt_words, wt_scales, "e2m1")
    a = ws_.T @ tab_ + wt_.T @ tabb_
    h = a
    h_ = mxq(h, 0, "e4m3")
    wd_ = mxq(f64(wd), 0, "e4m3")
    y = wd_.T @ h_
    out = np.zeros((N, T))
    out[:, idx2] = f64(wgo)[0] * (y + f64(rT)[:, idx2])
    return out

@@ -1,0 +1,226 @@
+from contextlib import ExitStack
+
+import concourse.mybir as mybir
+from concourse.masks import make_identity
+
+K, R, N, T, J = 1024, 1024, 512, 2048, 1024
+FLOPS = 2 * (2 * K * R * J + R * N * J)
+
+F32 = mybir.dt.float32
+BF16 = mybir.dt.bfloat16
+I32 = mybir.dt.int32
+U32 = mybir.dt.uint32
+U16 = mybir.dt.uint16
+U8 = mybir.dt.uint8
+FP8X4 = mybir.dt.float8_e4m3fn_x4
+FP4X4 = mybir.dt.float4_e2m1fn_x4
+ADD = mybir.AluOpType.add
+MULT = mybir.AluOpType.mult
+
+P = 128
+PACK = 4
+PASSES = 2
+BANK = 512
+HALF = 512
+HALVES = J // HALF
+LIST_ROWS = 16
+QUADS = 4
+QUAD = 32
+ROWS = 4
+
+
+def tile_list_msg_none_resL_kernel(
+    tc, tab_words, tab_scales, ws_words, ws_scales, wt_words, wt_scales, wd, rT, wgo, offs, offs2, out
+):
+    nc = tc.nc
+    with ExitStack() as ctx:
+        keep = ctx.enter_context(tc.tile_pool(name="keep", bufs=1))
+        ring = ctx.enter_context(tc.tile_pool(name="ring", bufs=3))
+        psum = ctx.enter_context(tc.psum_pool(name="psum", bufs=2))
+
+        src = keep.tile([P, J // LIST_ROWS], U16, name="src")
+        dst = keep.tile([P, J // LIST_ROWS], U16, name="dst")
+        both_planes = keep.tile([P, T // 4], I32, name="both_planes", align_bytes=64)
+        second_plane = keep.tile([P, T // 4], I32, name="second_plane", align_bytes=64)
+        ws_sc = keep.tile([P, R // 4], I32, name="ws_sc", align_bytes=64)
+        wt_sc = keep.tile([P, PASSES, R // 4], I32, name="wt_sc", align_bytes=64)
+        table = [keep.tile([P, T], I32, name="table%d" % a, align_bytes=64) for a in range(PASSES)]
+        ws = keep.tile([P, PASSES, R], I32, name="ws", align_bytes=64)
+        wt = keep.tile([P, PASSES, R // 2], I32, name="wt", align_bytes=64)
+        ident = keep.tile([P, P], F32, name="ident")
+
+        nc.sync.dma_start(src[:], offs)
+        nc.vector.memset(both_planes[:], 0)
+        nc.vector.memset(second_plane[:], 0)
+        nc.vector.memset(ws_sc[:], 0)
+        nc.vector.memset(wt_sc[:], 0)
+        make_identity(nc, ident[:])
+
+        for q in range(QUADS):
+            nc.sync.dma_start(
+                both_planes[QUAD * q : QUAD * q + PASSES * ROWS, :],
+                tab_scales[:, ROWS * q : ROWS * (q + 1), :].bitcast(I32),
+            )
+        nc.sync.dma_start(dst[:], offs2)
+        for q in range(QUADS):
+            nc.sync.dma_start(
+                second_plane[QUAD * q : QUAD * q + ROWS, :],
+                tab_scales[1, ROWS * q : ROWS * (q + 1), :].bitcast(I32),
+            )
+        for a in range(PASSES):
+            nc.sync.dma_start(table[a][:], tab_words[a].rearrange("p t i -> p (t i)").bitcast(I32))
+        for q in range(QUADS):
+            nc.sync.dma_start(
+                ws_sc[QUAD * q : QUAD * q + PASSES * ROWS, :],
+                ws_scales[:, ROWS * q : ROWS * (q + 1), :].bitcast(I32),
+            )
+        for q in range(QUADS):
+            nc.sync.dma_start(
+                wt_sc[QUAD * q : QUAD * q + ROWS, :, :],
+                wt_scales[:, ROWS * q : ROWS * (q + 1), :].rearrange("a q r -> q a r").bitcast(I32),
+            )
+        nc.sync.dma_start(ws[:], ws_words.rearrange("a p r i -> p a (r i)").bitcast(I32))
+        nc.sync.dma_start(wt[:], wt_words.rearrange("a p c -> p a c").bitcast(I32))
+
+        wd_raw = [keep.tile([P, PACK, N], F32, name="wd_raw%d" % b) for b in range(PASSES)]
+        for b in range(PASSES):
+            nc.sync.dma_start(wd_raw[b][:], wd[BANK * b : BANK * (b + 1), :].rearrange("(p t) n -> p t n", t=PACK))
+        state = [keep.tile([P, T], F32, name="state%d" % i) for i in range(N // P)]
+        weight = keep.tile([P, J], F32, name="weight")
+        for i in range(N // P):
+            nc.sync.dma_start(state[i][:], rT[P * i : P * (i + 1), :])
+        nc.sync.dma_start(weight[:], wgo)
+
+        src_words = [keep.tile([P, J], U32, name="src_words%d" % a, align_bytes=64) for a in range(PASSES)]
+        dst_words = [keep.tile([P, J], U32, name="dst_words%d" % a, align_bytes=64) for a in range(PASSES)]
+        src_sc = keep.tile([P, J], U8, name="src_sc", align_bytes=64)
+        dst_sc = [keep.tile([P, J], U8, name="dst_sc%d" % a, align_bytes=64) for a in range(PASSES)]
+        h_bf = keep.tile([P, HALVES, PASSES, HALF, PACK], BF16, name="h_bf", align_bytes=64)
+        h_codes = keep.tile([P, HALVES, PASSES, HALF], U32, name="h_codes", align_bytes=64)
+        h_sc = keep.tile([P, HALVES, PASSES, HALF], U8, name="h_sc", align_bytes=64)
+        wd_bf = keep.tile([P, PASSES, N, PACK], BF16, name="wd_bf", align_bytes=64)
+        wd_codes = keep.tile([P, PASSES, N], U32, name="wd_codes", align_bytes=64)
+        wd_sc = keep.tile([P, PASSES, N], U8, name="wd_sc", align_bytes=64)
+        picked = [keep.tile([P, J], F32, name="picked%d" % i) for i in range(N // P)]
+        result = [keep.tile([P, T], F32, name="result%d" % i) for i in range(N // P)]
+
+        def list_cols(half):
+            return slice(half * HALF // LIST_ROWS, (half + 1) * HALF // LIST_ROWS)
+
+        def gather_table(half):
+            cols = slice(half * HALF, (half + 1) * HALF)
+            s, d = src[:, list_cols(half)], dst[:, list_cols(half)]
+            nc.vector.tensor_copy(src_sc[:, cols], both_planes[:].bitcast(U8).indirect(s))
+            nc.vector.tensor_copy(dst_sc[0][:, cols], both_planes[:].bitcast(U8).indirect(d))
+            nc.vector.tensor_copy(dst_sc[1][:, cols], second_plane[:].bitcast(U8).indirect(d))
+            for a in range(PASSES):
+                nc.vector.tensor_copy(src_words[a][:, cols], table[a][:].bitcast(U32).indirect(s))
+                nc.vector.tensor_copy(dst_words[a][:, cols], table[a][:].bitcast(U32).indirect(d))
+
+        def first_product(jt):
+            cols = slice(P * jt, P * (jt + 1))
+            acc = [psum.tile([P, BANK], F32, name="acc%d" % b) for b in range(PASSES)]
+            for a in range(PASSES):
+                for b in range(PASSES):
+                    nc.tensor.matmul_mx(
+                        out=acc[b][:],
+                        lhsT=src_words[a][:, cols].bitcast(FP8X4),
+                        lhsT_scale=src_sc[ROWS * a :, cols],
+                        rhs=ws[:, a, BANK * b : BANK * (b + 1)].bitcast(FP8X4),
+                        rhs_scale=ws_sc[:].bitcast(U8)[ROWS * a :, BANK * b : BANK * (b + 1)],
+                        start=(a == 0),
+                        stop=False,
+                    )
+            for a in range(PASSES):
+                for b in range(PASSES):
+                    nc.tensor.matmul_mx(
+                        out=acc[b][:],
+                        lhsT=dst_words[a][:, cols].bitcast(FP8X4),
+                        lhsT_scale=dst_sc[a][:, cols],
+                        rhs=wt[:, a, BANK // 2 * b : BANK // 2 * (b + 1)].bitcast(U8).bitcast(FP4X4),
+                        rhs_scale=wt_sc[:, a, :].bitcast(U8)[:, BANK * b : BANK * (b + 1)],
+                        start=False,
+                        stop=(a == PASSES - 1),
+                    )
+            rows = ring.tile([P, PASSES, 2, P, 2], BF16, name="rows", align_bytes=64)
+            for b in range(PASSES):
+                nc.scalar.copy(rows[:, b], acc[b][:].rearrange("j (p u e) -> j u p e", u=2, e=2))
+            return rows
+
+        def turn(jt, rows):
+            half, at = divmod(P * jt, HALF)
+            words = rows[:].rearrange("j b u p e -> j (b u p e)").bitcast(F32)
+            turned = psum.tile([P, PASSES, 2, P], F32, name="turned")
+            for b in range(PASSES):
+                for u in range(2):
+                    c = P * (2 * b + u)
+                    nc.tensor.transpose(turned[:, b, u, :], words[:, c : c + P], ident[:])
+            nc.scalar.copy(
+                h_bf[:, half, :, at : at + P, :].bitcast(F32),
+                turned[:].rearrange("p b u j -> p b j u"),
+            )
+
+        def quantize_h(half):
+            nc.vector.quantize_mx(
+                out=h_codes[:, half].rearrange("p b j -> p (b j)").bitcast(FP8X4),
+                scales=h_sc[:, half].rearrange("p b j -> p (b j)"),
+                in_=h_bf[:, half].rearrange("p b j t -> p (b j t)"),
+            )
+
+        def finish(i, half):
+            cols = slice(half * HALF, (half + 1) * HALF)
+            y = psum.tile([P, BANK], F32, name="y")
+            for b in range(PASSES):
+                nc.tensor.matmul_mx(
+                    out=y[:],
+                    lhsT=wd_codes[:, b, P * i : P * (i + 1)].bitcast(FP8X4),
+                    lhsT_scale=wd_sc[:, b, P * i : P * (i + 1)],
+                    rhs=h_codes[:, half, b, :].bitcast(FP8X4),
+                    rhs_scale=h_sc[:, half, b, :],
+                    start=(b == 0),
+                    stop=(b == PASSES - 1),
+                )
+            total = ring.tile([P, HALF], F32, name="total")
+            nc.vector.tensor_tensor(total[:], y[:], picked[i][:, cols], ADD)
+            return total
+
+        def scatter(i, half, total):
+            cols = slice(half * HALF, (half + 1) * HALF)
+            nc.vector.tensor_tensor(result[i][:].indirect(dst[:, list_cols(half)]), total[:], weight[:, cols], MULT)
+
+        tiles_a_half = HALF // P
+        waiting = None
+        for half in range(HALVES):
+            gather_table(half)
+        for half in range(HALVES):
+            for jt in range(half * tiles_a_half, (half + 1) * tiles_a_half):
+                rows = first_product(jt)
+                if waiting is not None:
+                    turn(*waiting)
+                    if waiting[0] == tiles_a_half - 1:
+                        quantize_h(0)
+                waiting = (jt, rows)
+            if half == 0:
+                for b in range(PASSES):
+                    nc.scalar.copy(wd_bf[:, b], wd_raw[b][:].rearrange("p t n -> p n t"))
+                nc.vector.quantize_mx(
+                    out=wd_codes[:].rearrange("p b n -> p (b n)").bitcast(FP8X4),
+                    scales=wd_sc[:].rearrange("p b n -> p (b n)"),
+                    in_=wd_bf[:].rearrange("p b n t -> p (b n t)"),
+                )
+        turn(*waiting)
+        quantize_h(1)
+
+        for i in range(N // P):
+            nc.vector.tensor_copy(picked[i][:], state[i][:].indirect(dst[:]))
+        for i in range(N // P):
+            nc.vector.memset(result[i][:], 0.0)
+
+        order = [(i, half) for half in range(HALVES) for i in range(N // P)]
+        total = finish(*order[0])
+        for n, (i, half) in enumerate(order):
+            ahead = finish(*order[n + 1]) if n + 1 < len(order) else None
+            scatter(i, half, total)
+            total = ahead
+            if half == HALVES - 1:
+                nc.sync.dma_start(out[P * i : P * (i + 1), :], result[i][:])

@@ -14,8 +14,7 @@ U16 = mybir.dt.uint16
 U8 = mybir.dt.uint8
 FP8X4 = mybir.dt.float8_e4m3fn_x4
 FP4X4 = mybir.dt.float4_e2m1fn_x4
-ADD = mybir.AluOpType.add
-MULT = mybir.AluOpType.mult
+COPY = mybir.ActivationFunctionType.Copy
 
 P = 128
 PACK = 4
@@ -35,8 +34,11 @@ def tile_list_msg_none_resL_kernel(
     nc = tc.nc
     with ExitStack() as ctx:
         keep = ctx.enter_context(tc.tile_pool(name="keep", bufs=1))
+        reused = ctx.enter_context(tc.tile_pool(name="reused", bufs=1))
         ring = ctx.enter_context(tc.tile_pool(name="ring", bufs=3))
-        psum = ctx.enter_context(tc.psum_pool(name="psum", bufs=2))
+        totals = ctx.enter_context(tc.tile_pool(name="totals", bufs=6))
+        sums = ctx.enter_context(tc.psum_pool(name="sums", bufs=3))
+        banks = ctx.enter_context(tc.psum_pool(name="banks", bufs=5))
 
         src = keep.tile([P, J // LIST_ROWS], U16, name="src")
         dst = keep.tile([P, J // LIST_ROWS], U16, name="dst")
@@ -44,12 +46,15 @@ def tile_list_msg_none_resL_kernel(
         second_plane = keep.tile([P, T // 4], I32, name="second_plane", align_bytes=64)
         ws_sc = keep.tile([P, R // 4], I32, name="ws_sc", align_bytes=64)
         wt_sc = keep.tile([P, PASSES, R // 4], I32, name="wt_sc", align_bytes=64)
-        table = [keep.tile([P, T], I32, name="table%d" % a, align_bytes=64) for a in range(PASSES)]
+        table = [reused.tile([P, T], I32, name="wide%d" % a, align_bytes=64) for a in range(PASSES)]
         ws = keep.tile([P, PASSES, R], I32, name="ws", align_bytes=64)
         wt = keep.tile([P, PASSES, R // 2], I32, name="wt", align_bytes=64)
         ident = keep.tile([P, P], F32, name="ident")
+        weight_rows = reused.tile([P, P], F32, name="late", align_bytes=64)
+        weight = keep.tile([P, J // P], F32, name="weight")
 
         nc.sync.dma_start(src[:], offs)
+        nc.sync.dma_start(dst[:], offs2)
         nc.vector.memset(both_planes[:], 0)
         nc.vector.memset(second_plane[:], 0)
         nc.vector.memset(ws_sc[:], 0)
@@ -61,14 +66,17 @@ def tile_list_msg_none_resL_kernel(
                 both_planes[QUAD * q : QUAD * q + PASSES * ROWS, :],
                 tab_scales[:, ROWS * q : ROWS * (q + 1), :].bitcast(I32),
             )
-        nc.sync.dma_start(dst[:], offs2)
+        for a in range(PASSES):
+            nc.sync.dma_start(table[a][:], tab_words[a].rearrange("p t i -> p (t i)").bitcast(I32))
         for q in range(QUADS):
             nc.sync.dma_start(
                 second_plane[QUAD * q : QUAD * q + ROWS, :],
                 tab_scales[1, ROWS * q : ROWS * (q + 1), :].bitcast(I32),
             )
+        nc.sync.dma_start(weight_rows[:], wgo[0 : P * P // J, :].rearrange("a (c j) -> (a c) j", j=P))
         for a in range(PASSES):
-            nc.sync.dma_start(table[a][:], tab_words[a].rearrange("p t i -> p (t i)").bitcast(I32))
+            nc.sync.dma_start(ws[:, a, :], ws_words[a].rearrange("p r i -> p (r i)").bitcast(I32))
+        nc.sync.dma_start(wt[:], wt_words.rearrange("a p c -> p a c").bitcast(I32))
         for q in range(QUADS):
             nc.sync.dma_start(
                 ws_sc[QUAD * q : QUAD * q + PASSES * ROWS, :],
@@ -79,148 +87,188 @@ def tile_list_msg_none_resL_kernel(
                 wt_sc[QUAD * q : QUAD * q + ROWS, :, :],
                 wt_scales[:, ROWS * q : ROWS * (q + 1), :].rearrange("a q r -> q a r").bitcast(I32),
             )
-        nc.sync.dma_start(ws[:], ws_words.rearrange("a p r i -> p a (r i)").bitcast(I32))
-        nc.sync.dma_start(wt[:], wt_words.rearrange("a p c -> p a c").bitcast(I32))
 
         wd_raw = [keep.tile([P, PACK, N], F32, name="wd_raw%d" % b) for b in range(PASSES)]
         for b in range(PASSES):
             nc.sync.dma_start(wd_raw[b][:], wd[BANK * b : BANK * (b + 1), :].rearrange("(p t) n -> p t n", t=PACK))
         state = [keep.tile([P, T], F32, name="state%d" % i) for i in range(N // P)]
-        weight = keep.tile([P, J], F32, name="weight")
         for i in range(N // P):
             nc.sync.dma_start(state[i][:], rT[P * i : P * (i + 1), :])
-        nc.sync.dma_start(weight[:], wgo)
 
-        src_words = [keep.tile([P, J], U32, name="src_words%d" % a, align_bytes=64) for a in range(PASSES)]
-        dst_words = [keep.tile([P, J], U32, name="dst_words%d" % a, align_bytes=64) for a in range(PASSES)]
-        src_sc = keep.tile([P, J], U8, name="src_sc", align_bytes=64)
-        dst_sc = [keep.tile([P, J], U8, name="dst_sc%d" % a, align_bytes=64) for a in range(PASSES)]
-        h_bf = keep.tile([P, HALVES, PASSES, HALF, PACK], BF16, name="h_bf", align_bytes=64)
         h_codes = keep.tile([P, HALVES, PASSES, HALF], U32, name="h_codes", align_bytes=64)
         h_sc = keep.tile([P, HALVES, PASSES, HALF], U8, name="h_sc", align_bytes=64)
-        wd_bf = keep.tile([P, PASSES, N, PACK], BF16, name="wd_bf", align_bytes=64)
+        wd_bf = reused.tile([P, PASSES, N, PACK], BF16, name="staged_wd", align_bytes=64)
         wd_codes = keep.tile([P, PASSES, N], U32, name="wd_codes", align_bytes=64)
         wd_sc = keep.tile([P, PASSES, N], U8, name="wd_sc", align_bytes=64)
-        picked = [keep.tile([P, J], F32, name="picked%d" % i) for i in range(N // P)]
-        result = [keep.tile([P, T], F32, name="result%d" % i) for i in range(N // P)]
+        message = [keep.tile([P, HALF // P, N], F32, name="message%d" % half) for half in range(HALVES)]
 
         def list_cols(half):
             return slice(half * HALF // LIST_ROWS, (half + 1) * HALF // LIST_ROWS)
 
-        def gather_table(half):
-            cols = slice(half * HALF, (half + 1) * HALF)
+        def gather_table(half, looked_up):
             s, d = src[:, list_cols(half)], dst[:, list_cols(half)]
-            nc.vector.tensor_copy(src_sc[:, cols], both_planes[:].bitcast(U8).indirect(s))
-            nc.vector.tensor_copy(dst_sc[0][:, cols], both_planes[:].bitcast(U8).indirect(d))
-            nc.vector.tensor_copy(dst_sc[1][:, cols], second_plane[:].bitcast(U8).indirect(d))
+            words = [looked_up[:, HALF * w : HALF * (w + 1)] for w in range(2 * PASSES)]
+            first = 2 * PASSES * HALF
+            planes = [looked_up[:, first + HALF // 4 * w : first + HALF // 4 * (w + 1)].bitcast(U8) for w in range(3)]
+            nc.vector.tensor_copy(planes[0], both_planes[:].bitcast(U8).indirect(s))
+            nc.vector.tensor_copy(planes[1], both_planes[:].bitcast(U8).indirect(d))
             for a in range(PASSES):
-                nc.vector.tensor_copy(src_words[a][:, cols], table[a][:].bitcast(U32).indirect(s))
-                nc.vector.tensor_copy(dst_words[a][:, cols], table[a][:].bitcast(U32).indirect(d))
+                nc.vector.tensor_copy(words[a], table[a][:].bitcast(U32).indirect(s))
+                nc.vector.tensor_copy(words[PASSES + a], table[a][:].bitcast(U32).indirect(d))
+            nc.vector.tensor_copy(planes[2], second_plane[:].bitcast(U8).indirect(d))
+            return words, planes
 
-        def first_product(jt):
-            cols = slice(P * jt, P * (jt + 1))
-            acc = [psum.tile([P, BANK], F32, name="acc%d" % b) for b in range(PASSES)]
-            for a in range(PASSES):
-                for b in range(PASSES):
+        def first_product(c, words, planes):
+            cols = slice(P * c, P * (c + 1))
+            rows = ring.tile([P, PASSES, 2, P, 2], BF16, name="rows", align_bytes=64)
+            for b in range(PASSES):
+                acc = sums.tile([P, BANK], F32, name="acc")
+                for a in range(PASSES):
                     nc.tensor.matmul_mx(
-                        out=acc[b][:],
-                        lhsT=src_words[a][:, cols].bitcast(FP8X4),
-                        lhsT_scale=src_sc[ROWS * a :, cols],
+                        out=acc[:],
+                        lhsT=words[a][:, cols].bitcast(FP8X4),
+                        lhsT_scale=planes[0][ROWS * a :, cols],
                         rhs=ws[:, a, BANK * b : BANK * (b + 1)].bitcast(FP8X4),
                         rhs_scale=ws_sc[:].bitcast(U8)[ROWS * a :, BANK * b : BANK * (b + 1)],
                         start=(a == 0),
                         stop=False,
                     )
-            for a in range(PASSES):
-                for b in range(PASSES):
+                for a in range(PASSES):
                     nc.tensor.matmul_mx(
-                        out=acc[b][:],
-                        lhsT=dst_words[a][:, cols].bitcast(FP8X4),
-                        lhsT_scale=dst_sc[a][:, cols],
+                        out=acc[:],
+                        lhsT=words[PASSES + a][:, cols].bitcast(FP8X4),
+                        lhsT_scale=planes[1 + a][:, cols],
                         rhs=wt[:, a, BANK // 2 * b : BANK // 2 * (b + 1)].bitcast(U8).bitcast(FP4X4),
                         rhs_scale=wt_sc[:, a, :].bitcast(U8)[:, BANK * b : BANK * (b + 1)],
                         start=False,
                         stop=(a == PASSES - 1),
                     )
-            rows = ring.tile([P, PASSES, 2, P, 2], BF16, name="rows", align_bytes=64)
-            for b in range(PASSES):
-                nc.scalar.copy(rows[:, b], acc[b][:].rearrange("j (p u e) -> j u p e", u=2, e=2))
+                nc.scalar.copy(rows[:, b], acc[:].rearrange("j (p u e) -> j u p e", u=2, e=2))
             return rows
 
-        def turn(jt, rows):
-            half, at = divmod(P * jt, HALF)
+        def turn(c, rows, h_bf):
             words = rows[:].rearrange("j b u p e -> j (b u p e)").bitcast(F32)
-            turned = psum.tile([P, PASSES, 2, P], F32, name="turned")
+            turned = banks.tile([P, PASSES, 2, P], F32, name="bank")
             for b in range(PASSES):
                 for u in range(2):
-                    c = P * (2 * b + u)
-                    nc.tensor.transpose(turned[:, b, u, :], words[:, c : c + P], ident[:])
+                    at = P * (2 * b + u)
+                    nc.tensor.transpose(turned[:, b, u, :], words[:, at : at + P], ident[:])
             nc.scalar.copy(
-                h_bf[:, half, :, at : at + P, :].bitcast(F32),
+                h_bf[:, :, P * c : P * (c + 1), :].bitcast(F32),
                 turned[:].rearrange("p b u j -> p b j u"),
             )
 
-        def quantize_h(half):
+        def quantize_h(half, h_bf):
             nc.vector.quantize_mx(
                 out=h_codes[:, half].rearrange("p b j -> p (b j)").bitcast(FP8X4),
                 scales=h_sc[:, half].rearrange("p b j -> p (b j)"),
-                in_=h_bf[:, half].rearrange("p b j t -> p (b j t)"),
+                in_=h_bf[:].rearrange("p b j t -> p (b j t)"),
             )
 
-        def finish(i, half):
-            cols = slice(half * HALF, (half + 1) * HALF)
-            y = psum.tile([P, BANK], F32, name="y")
-            for b in range(PASSES):
-                nc.tensor.matmul_mx(
-                    out=y[:],
-                    lhsT=wd_codes[:, b, P * i : P * (i + 1)].bitcast(FP8X4),
-                    lhsT_scale=wd_sc[:, b, P * i : P * (i + 1)],
-                    rhs=h_codes[:, half, b, :].bitcast(FP8X4),
-                    rhs_scale=h_sc[:, half, b, :],
-                    start=(b == 0),
-                    stop=(b == PASSES - 1),
-                )
-            total = ring.tile([P, HALF], F32, name="total")
-            nc.vector.tensor_tensor(total[:], y[:], picked[i][:, cols], ADD)
+        def gather_state(i, picked):
+            nc.vector.tensor_copy(picked[:], state[i][:].indirect(dst[:]))
+            return picked
+
+        def turn_state(half, picked):
+            own = totals.tile([P, HALF // P, P], F32, name="own")
+            bank = banks.tile([P, HALF // P, P], F32, name="bank")
+            for c in range(HALF // P):
+                at = half * HALF + P * c
+                nc.tensor.transpose(bank[:, c, :], picked[:, at : at + P], ident[:])
+            for c in range(HALF // P):
+                jt = half * HALF // P + c
+                nc.scalar.activation(own[:, c, :], bank[:, c, :], COPY, scale=weight[:, jt : jt + 1])
+            return own
+
+        def second_product(half):
+            for c in range(HALF // P):
+                jt = half * HALF // P + c
+                bank = banks.tile([P, N], F32, name="bank")
+                for b in range(PASSES):
+                    nc.tensor.matmul_mx(
+                        out=bank[:],
+                        lhsT=h_codes[:, half, b, P * c : P * (c + 1)].bitcast(FP8X4),
+                        lhsT_scale=h_sc[:, half, b, P * c : P * (c + 1)],
+                        rhs=wd_codes[:, b, :].bitcast(FP8X4),
+                        rhs_scale=wd_sc[:, b, :],
+                        start=(b == 0),
+                        stop=(b == PASSES - 1),
+                    )
+                nc.scalar.activation(message[half][:, c, :], bank[:], COPY, scale=weight[:, jt : jt + 1])
+
+        def add_back(i, half, own):
+            bank = banks.tile([P, HALF // P, P], F32, name="bank")
+            for c in range(HALF // P):
+                for first, part in ((True, own[:, c, :]), (False, message[half][:, c, P * i : P * (i + 1)])):
+                    nc.tensor.matmul(
+                        bank[:, c, :],
+                        part,
+                        ident[:],
+                        start=first,
+                        stop=not first,
+                        is_transpose=True,
+                    )
+            total = totals.tile([P, HALF], F32, name="total")
+            nc.scalar.copy(total[:], bank[:].rearrange("n c j -> n (c j)"))
             return total
 
         def scatter(i, half, total):
-            cols = slice(half * HALF, (half + 1) * HALF)
-            nc.vector.tensor_tensor(result[i][:].indirect(dst[:, list_cols(half)]), total[:], weight[:, cols], MULT)
+            nc.vector.tensor_copy(result[i][:].indirect(dst[:, list_cols(half)]), total[:])
 
-        tiles_a_half = HALF // P
-        waiting = None
-        for half in range(HALVES):
-            gather_table(half)
-        for half in range(HALVES):
-            for jt in range(half * tiles_a_half, (half + 1) * tiles_a_half):
-                rows = first_product(jt)
-                if waiting is not None:
-                    turn(*waiting)
-                    if waiting[0] == tiles_a_half - 1:
-                        quantize_h(0)
-                waiting = (jt, rows)
-            if half == 0:
-                for b in range(PASSES):
-                    nc.scalar.copy(wd_bf[:, b], wd_raw[b][:].rearrange("p t n -> p n t"))
-                nc.vector.quantize_mx(
-                    out=wd_codes[:].rearrange("p b n -> p (b n)").bitcast(FP8X4),
-                    scales=wd_sc[:].rearrange("p b n -> p (b n)"),
-                    in_=wd_bf[:].rearrange("p b n t -> p (b n t)"),
-                )
-        turn(*waiting)
-        quantize_h(1)
+        looked_up_width = 2 * PASSES * HALF + 3 * HALF // 4
+        h_shape = [P, PASSES, HALF, PACK]
+        first_half = gather_table(0, keep.tile([P, looked_up_width], U32, name="early", align_bytes=64))
+        weight_bank = banks.tile([P, P], F32, name="bank")
+        nc.tensor.transpose(weight_bank[:], weight_rows[:], ident[:])
+        nc.scalar.copy(weight[:], weight_bank[:, 0 : J // P])
+        second_half = gather_table(1, reused.tile([P, looked_up_width], U32, name="late", align_bytes=64))
 
-        for i in range(N // P):
-            nc.vector.tensor_copy(picked[i][:], state[i][:].indirect(dst[:]))
-        for i in range(N // P):
+        h_first = reused.tile(h_shape, BF16, name="staged_h", align_bytes=64)
+        rows = first_product(0, *first_half)
+        for c in range(HALF // P):
+            ahead = first_product(c + 1, *first_half) if c + 1 < HALF // P else first_product(0, *second_half)
+            turn(c, rows, h_first)
+            rows = ahead
+            b, n = divmod(c * N // 2, N)
+            nc.scalar.copy(
+                wd_bf[:, b, n : n + N // 2, :], wd_raw[b][:, :, n : n + N // 2].rearrange("p t n -> p n t")
+            )
+        nc.vector.quantize_mx(
+            out=wd_codes[:].rearrange("p b n -> p (b n)").bitcast(FP8X4),
+            scales=wd_sc[:].rearrange("p b n -> p (b n)"),
+            in_=wd_bf[:].rearrange("p b n t -> p (b n t)"),
+        )
+        quantize_h(0, h_first)
+        picked = [gather_state(i, keep.tile([P, J], F32, name="picked%d" % i)) for i in range(2)]
+        picked.append(gather_state(2, reused.tile([P, J], F32, name="staged_h", align_bytes=64)))
+        picked.append(gather_state(3, reused.tile([P, J], F32, name="staged_wd", align_bytes=64)))
+
+        h_second = reused.tile(h_shape, BF16, name="wide1", align_bytes=64)
+        ahead = first_product(1, *second_half)
+        turn(0, rows, h_second)
+        rows = ahead
+        second_product(0)
+        first_totals = [add_back(i, 0, turn_state(0, picked[i])) for i in range(2)]
+        for c in range(1, HALF // P):
+            ahead = first_product(c + 1, *second_half) if c + 1 < HALF // P else None
+            turn(c, rows, h_second)
+            rows = ahead
+            if c + 1 < HALF // P:
+                first_totals.append(add_back(c + 1, 0, turn_state(0, picked[c + 1])))
+        own = [turn_state(1, picked[i]) for i in range(N // P)]
+
+        result = [keep.tile([P, T], F32, name="result%d" % i) for i in range(2)]
+        result.append(reused.tile([P, T], F32, name="wide0", align_bytes=64))
+        for i in range(3):
             nc.vector.memset(result[i][:], 0.0)
-
-        order = [(i, half) for half in range(HALVES) for i in range(N // P)]
-        total = finish(*order[0])
-        for n, (i, half) in enumerate(order):
-            ahead = finish(*order[n + 1]) if n + 1 < len(order) else None
-            scatter(i, half, total)
-            total = ahead
-            if half == HALVES - 1:
-                nc.sync.dma_start(out[P * i : P * (i + 1), :], result[i][:])
+        for i in range(3):
+            scatter(i, 0, first_totals[i])
+        quantize_h(1, h_second)
+        result.append(reused.tile([P, T], F32, name="wide1", align_bytes=64))
+        nc.vector.memset(result[3][:], 0.0)
+        second_product(1)
+        second_totals = [add_back(i, 1, own[i]) for i in range(N // P)]
+        scatter(3, 0, first_totals[3])
+        for i in range(N // P):
+            scatter(i, 1, second_totals[i])
+            nc.sync.dma_start(out[P * i : P * (i + 1), :], result[i][:])

@@ -14,18 +14,25 @@ U16 = mybir.dt.uint16
 U8 = mybir.dt.uint8
 FP8X4 = mybir.dt.float8_e4m3fn_x4
 FP4X4 = mybir.dt.float4_e2m1fn_x4
+ADD = mybir.AluOpType.add
+MULT = mybir.AluOpType.mult
 COPY = mybir.ActivationFunctionType.Copy
 
 P = 128
 PACK = 4
-PASSES = 2
-BANK = 512
-HALF = 512
-HALVES = J // HALF
+SPAN = P * PACK
+PASSES = K // SPAN
+WORD = 4
+QUADS, QUAD, ROWS = 4, 32, 4
 LIST_ROWS = 16
-QUADS = 4
-QUAD = 32
-ROWS = 4
+HALF = J // 2
+PART = J // 4
+PARTS = J // PART
+EDGE_TILES = J // P
+HALF_TILES = HALF // P
+ROW_TILES = N // P
+DIRECT = 2
+TURNED = [(2, 0), (0, 1), (1, 1), (2, 1), (3, 0), (3, 1)]
 
 
 def tile_list_msg_none_resL_kernel(
@@ -34,241 +41,233 @@ def tile_list_msg_none_resL_kernel(
     nc = tc.nc
     with ExitStack() as ctx:
         keep = ctx.enter_context(tc.tile_pool(name="keep", bufs=1))
-        reused = ctx.enter_context(tc.tile_pool(name="reused", bufs=1))
-        ring = ctx.enter_context(tc.tile_pool(name="ring", bufs=3))
-        totals = ctx.enter_context(tc.tile_pool(name="totals", bufs=6))
+        rounded = ctx.enter_context(tc.tile_pool(name="rounded", bufs=3))
+        pieces = ctx.enter_context(tc.tile_pool(name="pieces", bufs=len(TURNED)))
         sums = ctx.enter_context(tc.psum_pool(name="sums", bufs=3))
         banks = ctx.enter_context(tc.psum_pool(name="banks", bufs=5))
 
         src = keep.tile([P, J // LIST_ROWS], U16, name="src")
         dst = keep.tile([P, J // LIST_ROWS], U16, name="dst")
-        both_planes = keep.tile([P, T // 4], I32, name="both_planes", align_bytes=64)
-        second_plane = keep.tile([P, T // 4], I32, name="second_plane", align_bytes=64)
-        ws_sc = keep.tile([P, R // 4], I32, name="ws_sc", align_bytes=64)
-        wt_sc = keep.tile([P, PASSES, R // 4], I32, name="wt_sc", align_bytes=64)
-        table = [reused.tile([P, T], I32, name="wide%d" % a, align_bytes=64) for a in range(PASSES)]
+        table_sc = keep.tile([P, T // WORD], I32, name="table_sc", align_bytes=64)
+        dst_sc = keep.tile([P, J], U8, name="dst_sc", align_bytes=64)
+        moved_sc = keep.tile([P, J // WORD], I32, name="moved_sc", align_bytes=64)
+        w_sc = keep.tile([P, PASSES, R // WORD], I32, name="w_sc", align_bytes=64)
+        src_sc = keep.tile([P, J], U8, name="src_sc", align_bytes=64)
+        table = keep.tile([P, PASSES, T], I32, name="table", align_bytes=64)
         ws = keep.tile([P, PASSES, R], I32, name="ws", align_bytes=64)
         wt = keep.tile([P, PASSES, R // 2], I32, name="wt", align_bytes=64)
         ident = keep.tile([P, P], F32, name="ident")
-        weight_rows = reused.tile([P, P], F32, name="late", align_bytes=64)
-        weight = keep.tile([P, J // P], F32, name="weight")
+        edge_w = keep.tile([P, HALF], F32, name="edge_w")
+        edge_w_rows = keep.tile([P, P], F32, name="edge_w_rows")
+        edge_w_cols = keep.tile([P, EDGE_TILES], F32, name="edge_w_cols")
 
         nc.sync.dma_start(src[:], offs)
         nc.sync.dma_start(dst[:], offs2)
-        nc.vector.memset(both_planes[:], 0)
-        nc.vector.memset(second_plane[:], 0)
-        nc.vector.memset(ws_sc[:], 0)
-        nc.vector.memset(wt_sc[:], 0)
+        nc.vector.memset(table_sc[:], 0)
+        nc.vector.memset(w_sc[:], 0)
+        nc.vector.memset(moved_sc[:], 0)
         make_identity(nc, ident[:])
 
         for q in range(QUADS):
             nc.sync.dma_start(
-                both_planes[QUAD * q : QUAD * q + PASSES * ROWS, :],
+                table_sc[QUAD * q : QUAD * q + PASSES * ROWS, :],
                 tab_scales[:, ROWS * q : ROWS * (q + 1), :].bitcast(I32),
             )
-        for a in range(PASSES):
-            nc.sync.dma_start(table[a][:], tab_words[a].rearrange("p t i -> p (t i)").bitcast(I32))
-        for q in range(QUADS):
-            nc.sync.dma_start(
-                second_plane[QUAD * q : QUAD * q + ROWS, :],
-                tab_scales[1, ROWS * q : ROWS * (q + 1), :].bitcast(I32),
-            )
-        nc.sync.dma_start(weight_rows[:], wgo[0 : P * P // J, :].rearrange("a (c j) -> (a c) j", j=P))
+        nc.sync.dma_start(table[:], tab_words.rearrange("a p t i -> p a (t i)").bitcast(I32))
         for a in range(PASSES):
             nc.sync.dma_start(ws[:, a, :], ws_words[a].rearrange("p r i -> p (r i)").bitcast(I32))
         nc.sync.dma_start(wt[:], wt_words.rearrange("a p c -> p a c").bitcast(I32))
-        for q in range(QUADS):
-            nc.sync.dma_start(
-                ws_sc[QUAD * q : QUAD * q + PASSES * ROWS, :],
-                ws_scales[:, ROWS * q : ROWS * (q + 1), :].bitcast(I32),
-            )
-        for q in range(QUADS):
-            nc.sync.dma_start(
-                wt_sc[QUAD * q : QUAD * q + ROWS, :, :],
-                wt_scales[:, ROWS * q : ROWS * (q + 1), :].rearrange("a q r -> q a r").bitcast(I32),
-            )
+        for first_row, scales in ((ROWS, ws_scales), (0, wt_scales)):
+            for q in range(QUADS):
+                nc.scalar.dma_start(
+                    w_sc[QUAD * q + first_row : QUAD * q + first_row + ROWS, :, :],
+                    scales[:, ROWS * q : ROWS * (q + 1), :].rearrange("a q r -> q a r").bitcast(I32),
+                )
 
         wd_raw = [keep.tile([P, PACK, N], F32, name="wd_raw%d" % b) for b in range(PASSES)]
         for b in range(PASSES):
-            nc.sync.dma_start(wd_raw[b][:], wd[BANK * b : BANK * (b + 1), :].rearrange("(p t) n -> p t n", t=PACK))
-        state = [keep.tile([P, T], F32, name="state%d" % i) for i in range(N // P)]
-        for i in range(N // P):
+            nc.sync.dma_start(wd_raw[b][:], wd[SPAN * b : SPAN * (b + 1), :].rearrange("(p t) n -> p t n", t=PACK))
+        state = [keep.tile([P, T], F32, name="state%d" % i) for i in range(ROW_TILES)]
+        for i in range(ROW_TILES):
             nc.sync.dma_start(state[i][:], rT[P * i : P * (i + 1), :])
+        nc.sync.dma_start(edge_w[:], wgo[:, :HALF])
+        nc.sync.dma_start(edge_w_rows[:], wgo[0 : P // EDGE_TILES, :].rearrange("a (c j) -> (a c) j", j=P))
 
-        h_codes = keep.tile([P, HALVES, PASSES, HALF], U32, name="h_codes", align_bytes=64)
-        h_sc = keep.tile([P, HALVES, PASSES, HALF], U8, name="h_sc", align_bytes=64)
-        wd_bf = reused.tile([P, PASSES, N, PACK], BF16, name="staged_wd", align_bytes=64)
+        h_codes = keep.tile([P, PARTS, PASSES, PART], U32, name="h_codes", align_bytes=64)
+        h_sc = keep.tile([P, PARTS, PASSES, PART], U8, name="h_sc", align_bytes=64)
+        wd_bf = keep.tile([P, PASSES, N, PACK], BF16, name="wd_bf", align_bytes=64)
         wd_codes = keep.tile([P, PASSES, N], U32, name="wd_codes", align_bytes=64)
         wd_sc = keep.tile([P, PASSES, N], U8, name="wd_sc", align_bytes=64)
-        message = [keep.tile([P, HALF // P, N], F32, name="message%d" % half) for half in range(HALVES)]
+        h_bf = [keep.tile([P, PASSES, PART, PACK], BF16, name="h_bf%d" % q, align_bytes=64) for q in range(PARTS)]
+        src_words = [keep.tile([P, J], U32, name="src_words%d" % a, align_bytes=64) for a in range(PASSES)]
+        dst_words = [keep.tile([P, J], U32, name="dst_words%d" % a, align_bytes=64) for a in range(PASSES)]
+        picked = [keep.tile([P, J], F32, name="picked%d" % i) for i in range(ROW_TILES)]
+        message = keep.tile([P, EDGE_TILES, N], F32, name="message")
+        result = [keep.tile([P, T], F32, name="result%d" % i) for i in range(DIRECT)]
 
-        def list_cols(half):
-            return slice(half * HALF // LIST_ROWS, (half + 1) * HALF // LIST_ROWS)
+        def half_list(offsets, half):
+            return offsets[:, half * HALF // LIST_ROWS : (half + 1) * HALF // LIST_ROWS]
 
-        def gather_table(half, looked_up):
-            s, d = src[:, list_cols(half)], dst[:, list_cols(half)]
-            words = [looked_up[:, HALF * w : HALF * (w + 1)] for w in range(2 * PASSES)]
-            first = 2 * PASSES * HALF
-            planes = [looked_up[:, first + HALF // 4 * w : first + HALF // 4 * (w + 1)].bitcast(U8) for w in range(3)]
-            nc.vector.tensor_copy(planes[0], both_planes[:].bitcast(U8).indirect(s))
-            nc.vector.tensor_copy(planes[1], both_planes[:].bitcast(U8).indirect(d))
+        def gather_words(half):
+            cols = slice(half * HALF, (half + 1) * HALF)
             for a in range(PASSES):
-                nc.vector.tensor_copy(words[a], table[a][:].bitcast(U32).indirect(s))
-                nc.vector.tensor_copy(words[PASSES + a], table[a][:].bitcast(U32).indirect(d))
-            nc.vector.tensor_copy(planes[2], second_plane[:].bitcast(U8).indirect(d))
-            return words, planes
+                window = table[:, a, :].bitcast(U32)
+                nc.vector.tensor_copy(src_words[a][:, cols], window.indirect(half_list(src, half)))
+                nc.vector.tensor_copy(dst_words[a][:, cols], window.indirect(half_list(dst, half)))
 
-        def first_product(c, words, planes):
-            cols = slice(P * c, P * (c + 1))
-            rows = ring.tile([P, PASSES, 2, P, 2], BF16, name="rows", align_bytes=64)
+        def first_product(jt):
+            cols = slice(P * jt, P * (jt + 1))
+            dst_planes = [dst_sc[:, cols], moved_sc[:].bitcast(U8)[:, cols]]
+            rows = rounded.tile([P, PASSES, 2, P, 2], BF16, name="rows", align_bytes=64)
             for b in range(PASSES):
-                acc = sums.tile([P, BANK], F32, name="acc")
+                r_cols = slice(SPAN * b, SPAN * (b + 1))
+                acc = sums.tile([P, SPAN], F32, name="acc")
                 for a in range(PASSES):
                     nc.tensor.matmul_mx(
                         out=acc[:],
-                        lhsT=words[a][:, cols].bitcast(FP8X4),
-                        lhsT_scale=planes[0][ROWS * a :, cols],
-                        rhs=ws[:, a, BANK * b : BANK * (b + 1)].bitcast(FP8X4),
-                        rhs_scale=ws_sc[:].bitcast(U8)[ROWS * a :, BANK * b : BANK * (b + 1)],
+                        lhsT=src_words[a][:, cols].bitcast(FP8X4),
+                        lhsT_scale=src_sc[ROWS * a :, cols],
+                        rhs=ws[:, a, r_cols].bitcast(FP8X4),
+                        rhs_scale=w_sc[:, a, :].bitcast(U8)[ROWS:, r_cols],
                         start=(a == 0),
                         stop=False,
                     )
                 for a in range(PASSES):
                     nc.tensor.matmul_mx(
                         out=acc[:],
-                        lhsT=words[PASSES + a][:, cols].bitcast(FP8X4),
-                        lhsT_scale=planes[1 + a][:, cols],
-                        rhs=wt[:, a, BANK // 2 * b : BANK // 2 * (b + 1)].bitcast(U8).bitcast(FP4X4),
-                        rhs_scale=wt_sc[:, a, :].bitcast(U8)[:, BANK * b : BANK * (b + 1)],
+                        lhsT=dst_words[a][:, cols].bitcast(FP8X4),
+                        lhsT_scale=dst_planes[a],
+                        rhs=wt[:, a, SPAN // 2 * b : SPAN // 2 * (b + 1)].bitcast(U8).bitcast(FP4X4),
+                        rhs_scale=w_sc[:, a, :].bitcast(U8)[:, r_cols],
                         start=False,
                         stop=(a == PASSES - 1),
                     )
                 nc.scalar.copy(rows[:, b], acc[:].rearrange("j (p u e) -> j u p e", u=2, e=2))
             return rows
 
-        def turn(c, rows, h_bf):
-            words = rows[:].rearrange("j b u p e -> j (b u p e)").bitcast(F32)
-            turned = banks.tile([P, PASSES, 2, P], F32, name="bank")
+        def turn_h(jt, rows):
+            q, c = divmod(jt, PART // P)
+            pairs = rows[:].rearrange("j b u p e -> j (b u p e)").bitcast(F32)
+            bank = banks.tile([P, PASSES, 2, P], F32, name="bank")
             for b in range(PASSES):
                 for u in range(2):
                     at = P * (2 * b + u)
-                    nc.tensor.transpose(turned[:, b, u, :], words[:, at : at + P], ident[:])
+                    nc.tensor.transpose(bank[:, b, u, :], pairs[:, at : at + P], ident[:])
             nc.scalar.copy(
-                h_bf[:, :, P * c : P * (c + 1), :].bitcast(F32),
-                turned[:].rearrange("p b u j -> p b j u"),
+                h_bf[q][:, :, P * c : P * (c + 1), :].bitcast(F32),
+                bank[:].rearrange("p b u j -> p b j u"),
             )
 
-        def quantize_h(half, h_bf):
+        def quantize_h(q):
             nc.vector.quantize_mx(
-                out=h_codes[:, half].rearrange("p b j -> p (b j)").bitcast(FP8X4),
-                scales=h_sc[:, half].rearrange("p b j -> p (b j)"),
-                in_=h_bf[:].rearrange("p b j t -> p (b j t)"),
+                out=h_codes[:, q].rearrange("p b j -> p (b j)").bitcast(FP8X4),
+                scales=h_sc[:, q].rearrange("p b j -> p (b j)"),
+                in_=h_bf[q][:].rearrange("p b j t -> p (b j t)"),
             )
 
-        def gather_state(i, picked):
-            nc.vector.tensor_copy(picked[:], state[i][:].indirect(dst[:]))
-            return picked
-
-        def turn_state(half, picked):
-            own = totals.tile([P, HALF // P, P], F32, name="own")
-            bank = banks.tile([P, HALF // P, P], F32, name="bank")
-            for c in range(HALF // P):
-                at = half * HALF + P * c
-                nc.tensor.transpose(bank[:, c, :], picked[:, at : at + P], ident[:])
-            for c in range(HALF // P):
-                jt = half * HALF // P + c
-                nc.scalar.activation(own[:, c, :], bank[:, c, :], COPY, scale=weight[:, jt : jt + 1])
-            return own
-
-        def second_product(half):
-            for c in range(HALF // P):
-                jt = half * HALF // P + c
-                bank = banks.tile([P, N], F32, name="bank")
+        def direct_sum(i):
+            bank = banks.tile([P, HALF], F32, name="bank")
+            for q in range(HALF // PART):
                 for b in range(PASSES):
                     nc.tensor.matmul_mx(
-                        out=bank[:],
-                        lhsT=h_codes[:, half, b, P * c : P * (c + 1)].bitcast(FP8X4),
-                        lhsT_scale=h_sc[:, half, b, P * c : P * (c + 1)],
-                        rhs=wd_codes[:, b, :].bitcast(FP8X4),
-                        rhs_scale=wd_sc[:, b, :],
+                        out=bank[:, q * PART : (q + 1) * PART],
+                        lhsT=wd_codes[:, b, P * i : P * (i + 1)].bitcast(FP8X4),
+                        lhsT_scale=wd_sc[:, b, P * i : P * (i + 1)],
+                        rhs=h_codes[:, q, b, :].bitcast(FP8X4),
+                        rhs_scale=h_sc[:, q, b, :],
                         start=(b == 0),
                         stop=(b == PASSES - 1),
                     )
-                nc.scalar.activation(message[half][:, c, :], bank[:], COPY, scale=weight[:, jt : jt + 1])
+            total = pieces.tile([P, HALF], F32, name="total")
+            nc.vector.tensor_tensor(total[:], bank[:], picked[i][:, :HALF], ADD)
+            return total
 
-        def add_back(i, half, own):
-            bank = banks.tile([P, HALF // P, P], F32, name="bank")
-            for c in range(HALF // P):
-                for first, part in ((True, own[:, c, :]), (False, message[half][:, c, P * i : P * (i + 1)])):
-                    nc.tensor.matmul(
-                        bank[:, c, :],
-                        part,
-                        ident[:],
-                        start=first,
-                        stop=not first,
-                        is_transpose=True,
+        def turn_state(i, half):
+            own = pieces.tile([P, HALF_TILES, P], F32, name="own")
+            bank = banks.tile([P, HALF_TILES, P], F32, name="bank")
+            for c in range(HALF_TILES):
+                jt = half * HALF_TILES + c
+                nc.tensor.transpose(bank[:, c, :], picked[i][:, P * jt : P * (jt + 1)], ident[:])
+            for c in range(HALF_TILES):
+                jt = half * HALF_TILES + c
+                nc.scalar.activation(own[:, c, :], bank[:, c, :], COPY, scale=edge_w_cols[:, jt : jt + 1])
+            return own
+
+        def turned_message(half, first_n):
+            for jt in range(half * HALF_TILES, (half + 1) * HALF_TILES):
+                q, at = divmod(P * jt, PART)
+                bank = banks.tile([P, N - first_n], F32, name="bank")
+                for b in range(PASSES):
+                    nc.tensor.matmul_mx(
+                        out=bank[:],
+                        lhsT=h_codes[:, q, b, at : at + P].bitcast(FP8X4),
+                        lhsT_scale=h_sc[:, q, b, at : at + P],
+                        rhs=wd_codes[:, b, first_n:].bitcast(FP8X4),
+                        rhs_scale=wd_sc[:, b, first_n:],
+                        start=(b == 0),
+                        stop=(b == PASSES - 1),
                     )
-            total = totals.tile([P, HALF], F32, name="total")
+                nc.scalar.activation(message[:, jt, first_n:], bank[:], COPY, scale=edge_w_cols[:, jt : jt + 1])
+
+        def turned_sum(i, half, own):
+            bank = banks.tile([P, HALF_TILES, P], F32, name="bank")
+            for c in range(HALF_TILES):
+                jt = half * HALF_TILES + c
+                for first, term in ((True, own[:, c, :]), (False, message[:, jt, P * i : P * (i + 1)])):
+                    nc.tensor.matmul(bank[:, c, :], term, ident[:], start=first, stop=not first, is_transpose=True)
+            total = pieces.tile([P, HALF], F32, name="total")
             nc.scalar.copy(total[:], bank[:].rearrange("n c j -> n (c j)"))
             return total
 
-        def scatter(i, half, total):
-            nc.vector.tensor_copy(result[i][:].indirect(dst[:, list_cols(half)]), total[:])
-
-        looked_up_width = 2 * PASSES * HALF + 3 * HALF // 4
-        h_shape = [P, PASSES, HALF, PACK]
-        first_half = gather_table(0, keep.tile([P, looked_up_width], U32, name="early", align_bytes=64))
-        weight_bank = banks.tile([P, P], F32, name="bank")
-        nc.tensor.transpose(weight_bank[:], weight_rows[:], ident[:])
-        nc.scalar.copy(weight[:], weight_bank[:, 0 : J // P])
-        second_half = gather_table(1, reused.tile([P, looked_up_width], U32, name="late", align_bytes=64))
-
-        h_first = reused.tile(h_shape, BF16, name="staged_h", align_bytes=64)
-        rows = first_product(0, *first_half)
-        for c in range(HALF // P):
-            ahead = first_product(c + 1, *first_half) if c + 1 < HALF // P else first_product(0, *second_half)
-            turn(c, rows, h_first)
-            rows = ahead
-            b, n = divmod(c * N // 2, N)
-            nc.scalar.copy(
-                wd_bf[:, b, n : n + N // 2, :], wd_raw[b][:, :, n : n + N // 2].rearrange("p t n -> p n t")
+        nc.vector.tensor_copy(dst_sc[:], table_sc[:].bitcast(U8).indirect(dst[:]))
+        for q in range(QUADS):
+            nc.scalar.dma_start(
+                moved_sc[QUAD * q : QUAD * q + ROWS, :],
+                dst_sc[QUAD * q + ROWS : QUAD * q + 2 * ROWS, :].bitcast(I32),
             )
-        nc.vector.quantize_mx(
-            out=wd_codes[:].rearrange("p b n -> p (b n)").bitcast(FP8X4),
-            scales=wd_sc[:].rearrange("p b n -> p (b n)"),
-            in_=wd_bf[:].rearrange("p b n t -> p (b n t)"),
-        )
-        quantize_h(0, h_first)
-        picked = [gather_state(i, keep.tile([P, J], F32, name="picked%d" % i)) for i in range(2)]
-        picked.append(gather_state(2, reused.tile([P, J], F32, name="staged_h", align_bytes=64)))
-        picked.append(gather_state(3, reused.tile([P, J], F32, name="staged_wd", align_bytes=64)))
+        nc.vector.tensor_copy(src_sc[:], table_sc[:].bitcast(U8).indirect(src[:]))
+        for half in range(J // HALF):
+            gather_words(half)
 
-        h_second = reused.tile(h_shape, BF16, name="wide1", align_bytes=64)
-        ahead = first_product(1, *second_half)
-        turn(0, rows, h_second)
-        rows = ahead
-        second_product(0)
-        first_totals = [add_back(i, 0, turn_state(0, picked[i])) for i in range(2)]
-        for c in range(1, HALF // P):
-            ahead = first_product(c + 1, *second_half) if c + 1 < HALF // P else None
-            turn(c, rows, h_second)
+        rows = first_product(0)
+        for jt in range(EDGE_TILES):
+            ahead = first_product(jt + 1) if jt + 1 < EDGE_TILES else None
+            turn_h(jt, rows)
             rows = ahead
-            if c + 1 < HALF // P:
-                first_totals.append(add_back(c + 1, 0, turn_state(0, picked[c + 1])))
-        own = [turn_state(1, picked[i]) for i in range(N // P)]
+            if jt < HALF_TILES:
+                b, n = divmod(jt * N // 2, N)
+                nc.scalar.copy(
+                    wd_bf[:, b, n : n + N // 2, :], wd_raw[b][:, :, n : n + N // 2].rearrange("p t n -> p n t")
+                )
+            if (jt + 1) * P % PART == 0:
+                quantize_h(jt * P // PART)
+            if jt == HALF_TILES - 1:
+                nc.vector.quantize_mx(
+                    out=wd_codes[:].rearrange("p b n -> p (b n)").bitcast(FP8X4),
+                    scales=wd_sc[:].rearrange("p b n -> p (b n)"),
+                    in_=wd_bf[:].rearrange("p b n t -> p (b n t)"),
+                )
+                for i in range(ROW_TILES):
+                    nc.vector.tensor_copy(picked[i][:], state[i][:].indirect(dst[:]))
+                bank = banks.tile([P, P], F32, name="bank")
+                nc.tensor.transpose(bank[:], edge_w_rows[:], ident[:])
+                nc.scalar.copy(edge_w_cols[:], bank[:, :EDGE_TILES])
+            if jt == HALF_TILES:
+                for i in range(DIRECT):
+                    nc.vector.memset(result[i][:].bitcast(I32), 0)
+                totals = [direct_sum(i) for i in range(DIRECT)]
+                for i in range(DIRECT):
+                    nc.vector.tensor_tensor(result[i][:].indirect(half_list(dst, 0)), totals[i][:], edge_w[:], MULT)
 
-        result = [keep.tile([P, T], F32, name="result%d" % i) for i in range(2)]
-        result.append(reused.tile([P, T], F32, name="wide0", align_bytes=64))
-        for i in range(3):
-            nc.vector.memset(result[i][:], 0.0)
-        for i in range(3):
-            scatter(i, 0, first_totals[i])
-        quantize_h(1, h_second)
-        result.append(reused.tile([P, T], F32, name="wide1", align_bytes=64))
-        nc.vector.memset(result[3][:], 0.0)
-        second_product(1)
-        second_totals = [add_back(i, 1, own[i]) for i in range(N // P)]
-        scatter(3, 0, first_totals[3])
-        for i in range(N // P):
-            scatter(i, 1, second_totals[i])
-            nc.sync.dma_start(out[P * i : P * (i + 1), :], result[i][:])
+        result.append(keep.tile([P, T], F32, name="h_bf%d" % (PARTS - 1), align_bytes=64))
+        nc.vector.memset(result[DIRECT][:].bitcast(I32), 0)
+        result.append(result[0])
+        turned_message(0, P * DIRECT)
+        owns = [turn_state(i, half) for i, half in TURNED]
+        for place, (i, half) in enumerate(TURNED):
+            total = turned_sum(i, half, owns[place])
+            nc.vector.tensor_copy(result[i][:].indirect(half_list(dst, half)), total[:])
+            if place == 0:
+                turned_message(1, 0)
+            if half == 1:
+                nc.sync.dma_start(out[P * i : P * (i + 1), :], result[i][:])

@@ -31,8 +31,7 @@ PARTS = J // PART
 EDGE_TILES = J // P
 HALF_TILES = HALF // P
 ROW_TILES = N // P
-DIRECT = 2
-TURNED = [(2, 0), (0, 1), (1, 1), (2, 1), (3, 0), (3, 1)]
+PAIR = 2
 
 
 def tile_list_msg_none_resL_kernel(
@@ -42,9 +41,10 @@ def tile_list_msg_none_resL_kernel(
     with ExitStack() as ctx:
         keep = ctx.enter_context(tc.tile_pool(name="keep", bufs=1))
         rounded = ctx.enter_context(tc.tile_pool(name="rounded", bufs=3))
-        pieces = ctx.enter_context(tc.tile_pool(name="pieces", bufs=len(TURNED)))
+        pieces = ctx.enter_context(tc.tile_pool(name="pieces", bufs=4))
         sums = ctx.enter_context(tc.psum_pool(name="sums", bufs=3))
-        banks = ctx.enter_context(tc.psum_pool(name="banks", bufs=5))
+        banks = ctx.enter_context(tc.psum_pool(name="banks", bufs=2))
+        ys = ctx.enter_context(tc.psum_pool(name="ys", bufs=3))
 
         src = keep.tile([P, J // LIST_ROWS], U16, name="src")
         dst = keep.tile([P, J // LIST_ROWS], U16, name="dst")
@@ -57,9 +57,7 @@ def tile_list_msg_none_resL_kernel(
         ws = keep.tile([P, PASSES, R], I32, name="ws", align_bytes=64)
         wt = keep.tile([P, PASSES, R // 2], I32, name="wt", align_bytes=64)
         ident = keep.tile([P, P], F32, name="ident")
-        edge_w = keep.tile([P, HALF], F32, name="edge_w")
-        edge_w_rows = keep.tile([P, P], F32, name="edge_w_rows")
-        edge_w_cols = keep.tile([P, EDGE_TILES], F32, name="edge_w_cols")
+        edge_w = keep.tile([P, J], F32, name="edge_w")
 
         nc.sync.dma_start(src[:], offs)
         nc.sync.dma_start(dst[:], offs2)
@@ -90,30 +88,33 @@ def tile_list_msg_none_resL_kernel(
         state = [keep.tile([P, T], F32, name="state%d" % i) for i in range(ROW_TILES)]
         for i in range(ROW_TILES):
             nc.sync.dma_start(state[i][:], rT[P * i : P * (i + 1), :])
-        nc.sync.dma_start(edge_w[:], wgo[:, :HALF])
-        nc.sync.dma_start(edge_w_rows[:], wgo[0 : P // EDGE_TILES, :].rearrange("a (c j) -> (a c) j", j=P))
+            if i == PAIR - 1:
+                nc.sync.dma_start(edge_w[:], wgo)
 
         h_codes = keep.tile([P, PARTS, PASSES, PART], U32, name="h_codes", align_bytes=64)
         h_sc = keep.tile([P, PARTS, PASSES, PART], U8, name="h_sc", align_bytes=64)
-        wd_bf = keep.tile([P, PASSES, N, PACK], BF16, name="wd_bf", align_bytes=64)
-        wd_codes = keep.tile([P, PASSES, N], U32, name="wd_codes", align_bytes=64)
-        wd_sc = keep.tile([P, PASSES, N], U8, name="wd_sc", align_bytes=64)
+        wd_bf = [keep.tile([P, PASSES, PAIR * P, PACK], BF16, name="wd_bf%d" % g, align_bytes=64) for g in range(PAIR)]
+        wd_codes = keep.tile([P, PAIR, PASSES, PAIR * P], U32, name="wd_codes", align_bytes=64)
+        wd_sc = keep.tile([P, PAIR, PASSES, PAIR * P], U8, name="wd_sc", align_bytes=64)
         h_bf = [keep.tile([P, PASSES, PART, PACK], BF16, name="h_bf%d" % q, align_bytes=64) for q in range(PARTS)]
         src_words = [keep.tile([P, J], U32, name="src_words%d" % a, align_bytes=64) for a in range(PASSES)]
         dst_words = [keep.tile([P, J], U32, name="dst_words%d" % a, align_bytes=64) for a in range(PASSES)]
-        picked = [keep.tile([P, J], F32, name="picked%d" % i) for i in range(ROW_TILES)]
-        message = keep.tile([P, EDGE_TILES, N], F32, name="message")
-        result = [keep.tile([P, T], F32, name="result%d" % i) for i in range(DIRECT)]
+        message = [keep.tile([P, PAIR, J], F32, name="message%d" % g) for g in range(PAIR)]
+        last_total = keep.tile([P, J], F32, name="last_total")
+        result = [keep.tile([P, T], F32, name="result%d" % i) for i in range(ROW_TILES - 1)]
+        for tile in result:
+            nc.vector.memset(tile[:].bitcast(I32), 0)
+        result.append(result[0])
 
-        def half_list(offsets, half):
-            return offsets[:, half * HALF // LIST_ROWS : (half + 1) * HALF // LIST_ROWS]
+        def entries(offsets, first, count):
+            return offsets[:, first // LIST_ROWS : (first + count) // LIST_ROWS]
 
-        def gather_words(half):
-            cols = slice(half * HALF, (half + 1) * HALF)
+        def gather_words(q):
+            cols = slice(q * PART, (q + 1) * PART)
             for a in range(PASSES):
                 window = table[:, a, :].bitcast(U32)
-                nc.vector.tensor_copy(src_words[a][:, cols], window.indirect(half_list(src, half)))
-                nc.vector.tensor_copy(dst_words[a][:, cols], window.indirect(half_list(dst, half)))
+                nc.vector.tensor_copy(src_words[a][:, cols], window.indirect(entries(src, q * PART, PART)))
+                nc.vector.tensor_copy(dst_words[a][:, cols], window.indirect(entries(dst, q * PART, PART)))
 
         def first_product(jt):
             cols = slice(P * jt, P * (jt + 1))
@@ -165,59 +166,72 @@ def tile_list_msg_none_resL_kernel(
                 in_=h_bf[q][:].rearrange("p b j t -> p (b j t)"),
             )
 
-        def direct_sum(i):
-            bank = banks.tile([P, HALF], F32, name="bank")
-            for q in range(HALF // PART):
+        def round_wd(g, b):
+            nc.scalar.copy(
+                wd_bf[g][:, b], wd_raw[b][:, :, PAIR * P * g : PAIR * P * (g + 1)].rearrange("p t n -> p n t")
+            )
+
+        def quantize_wd(g):
+            nc.vector.quantize_mx(
+                out=wd_codes[:, g].rearrange("p b n -> p (b n)").bitcast(FP8X4),
+                scales=wd_sc[:, g].rearrange("p b n -> p (b n)"),
+                in_=wd_bf[g][:].rearrange("p b n t -> p (b n t)"),
+            )
+
+        def second_product(g, q):
+            bank = ys.tile([P, PAIR, PART], F32, name="y")
+            for c in range(PAIR):
                 for b in range(PASSES):
                     nc.tensor.matmul_mx(
-                        out=bank[:, q * PART : (q + 1) * PART],
-                        lhsT=wd_codes[:, b, P * i : P * (i + 1)].bitcast(FP8X4),
-                        lhsT_scale=wd_sc[:, b, P * i : P * (i + 1)],
+                        out=bank[:, c, :],
+                        lhsT=wd_codes[:, g, b, P * c : P * (c + 1)].bitcast(FP8X4),
+                        lhsT_scale=wd_sc[:, g, b, P * c : P * (c + 1)],
                         rhs=h_codes[:, q, b, :].bitcast(FP8X4),
                         rhs_scale=h_sc[:, q, b, :],
                         start=(b == 0),
                         stop=(b == PASSES - 1),
                     )
-            total = pieces.tile([P, HALF], F32, name="total")
-            nc.vector.tensor_tensor(total[:], bank[:], picked[i][:, :HALF], ADD)
-            return total
+            return bank
 
-        def turn_state(i, half):
-            own = pieces.tile([P, HALF_TILES, P], F32, name="own")
-            bank = banks.tile([P, HALF_TILES, P], F32, name="bank")
-            for c in range(HALF_TILES):
-                jt = half * HALF_TILES + c
-                nc.tensor.transpose(bank[:, c, :], picked[i][:, P * jt : P * (jt + 1)], ident[:])
-            for c in range(HALF_TILES):
-                jt = half * HALF_TILES + c
-                nc.scalar.activation(own[:, c, :], bank[:, c, :], COPY, scale=edge_w_cols[:, jt : jt + 1])
-            return own
+        def add_state(total, i, first, count):
+            g, c = divmod(i, PAIR)
+            nc.vector.tensor_tensor(
+                total, state[i][:].indirect(entries(dst, first, count)), message[g][:, c, first : first + count], ADD
+            )
 
-        def turned_message(half, first_n):
-            for jt in range(half * HALF_TILES, (half + 1) * HALF_TILES):
-                q, at = divmod(P * jt, PART)
-                bank = banks.tile([P, N - first_n], F32, name="bank")
-                for b in range(PASSES):
-                    nc.tensor.matmul_mx(
-                        out=bank[:],
-                        lhsT=h_codes[:, q, b, at : at + P].bitcast(FP8X4),
-                        lhsT_scale=h_sc[:, q, b, at : at + P],
-                        rhs=wd_codes[:, b, first_n:].bitcast(FP8X4),
-                        rhs_scale=wd_sc[:, b, first_n:],
-                        start=(b == 0),
-                        stop=(b == PASSES - 1),
-                    )
-                nc.scalar.activation(message[:, jt, first_n:], bank[:], COPY, scale=edge_w_cols[:, jt : jt + 1])
+        def put(i, first, count, total):
+            nc.vector.tensor_tensor(
+                result[i][:].indirect(entries(dst, first, count)), total, edge_w[:, first : first + count], MULT
+            )
 
-        def turned_sum(i, half, own):
-            bank = banks.tile([P, HALF_TILES, P], F32, name="bank")
-            for c in range(HALF_TILES):
-                jt = half * HALF_TILES + c
-                for first, term in ((True, own[:, c, :]), (False, message[:, jt, P * i : P * (i + 1)])):
-                    nc.tensor.matmul(bank[:, c, :], term, ident[:], start=first, stop=not first, is_transpose=True)
-            total = pieces.tile([P, HALF], F32, name="total")
-            nc.scalar.copy(total[:], bank[:].rearrange("n c j -> n (c j)"))
-            return total
+        def store(i):
+            nc.sync.dma_start(out[P * i : P * (i + 1), :], result[i][:])
+
+        picked = []
+
+        def first_pair(q):
+            cols = slice(q * PART, (q + 1) * PART)
+            bank = second_product(0, q)
+            totals = [pieces.tile([P, PART], F32, name="total") for c in range(PAIR)]
+            if q * PART < HALF:
+                for c in range(PAIR):
+                    nc.vector.tensor_tensor(totals[c][:], bank[:, c, :], picked[c][:, cols], ADD)
+            else:
+                nc.scalar.copy(message[0][:, :, cols], bank[:])
+                for c in range(PAIR):
+                    add_state(totals[c][:], c, q * PART, PART)
+            for c in range(PAIR):
+                put(c, q * PART, PART, totals[c][:])
+                if q == PARTS - 1:
+                    store(c)
+
+        def second_pair_message(q):
+            bank = second_product(1, q)
+            nc.scalar.copy(message[1][:, :, q * PART : (q + 1) * PART], bank[:])
+
+        def third_row_tile(q, total):
+            add_state(total[:], PAIR, q * PART, PART)
+            put(PAIR, q * PART, PART, total[:])
 
         nc.vector.tensor_copy(dst_sc[:], table_sc[:].bitcast(U8).indirect(dst[:]))
         for q in range(QUADS):
@@ -226,48 +240,38 @@ def tile_list_msg_none_resL_kernel(
                 dst_sc[QUAD * q + ROWS : QUAD * q + 2 * ROWS, :].bitcast(I32),
             )
         nc.vector.tensor_copy(src_sc[:], table_sc[:].bitcast(U8).indirect(src[:]))
-        for half in range(J // HALF):
-            gather_words(half)
+        for q in range(PARTS):
+            gather_words(q)
 
         rows = first_product(0)
         for jt in range(EDGE_TILES):
             ahead = first_product(jt + 1) if jt + 1 < EDGE_TILES else None
             turn_h(jt, rows)
             rows = ahead
-            if jt < HALF_TILES:
-                b, n = divmod(jt * N // 2, N)
-                nc.scalar.copy(
-                    wd_bf[:, b, n : n + N // 2, :], wd_raw[b][:, :, n : n + N // 2].rearrange("p t n -> p n t")
-                )
+            if jt < PAIR * PASSES:
+                g, b = divmod(jt, PASSES)
+                round_wd(g, b)
+                if b == PASSES - 1:
+                    quantize_wd(g)
             if (jt + 1) * P % PART == 0:
-                quantize_h(jt * P // PART)
-            if jt == HALF_TILES - 1:
-                nc.vector.quantize_mx(
-                    out=wd_codes[:].rearrange("p b n -> p (b n)").bitcast(FP8X4),
-                    scales=wd_sc[:].rearrange("p b n -> p (b n)"),
-                    in_=wd_bf[:].rearrange("p b n t -> p (b n t)"),
-                )
-                for i in range(ROW_TILES):
-                    nc.vector.tensor_copy(picked[i][:], state[i][:].indirect(dst[:]))
-                bank = banks.tile([P, P], F32, name="bank")
-                nc.tensor.transpose(bank[:], edge_w_rows[:], ident[:])
-                nc.scalar.copy(edge_w_cols[:], bank[:, :EDGE_TILES])
-            if jt == HALF_TILES:
-                for i in range(DIRECT):
-                    nc.vector.memset(result[i][:].bitcast(I32), 0)
-                totals = [direct_sum(i) for i in range(DIRECT)]
-                for i in range(DIRECT):
-                    nc.vector.tensor_tensor(result[i][:].indirect(half_list(dst, 0)), totals[i][:], edge_w[:], MULT)
-
-        result.append(keep.tile([P, T], F32, name="h_bf%d" % (PARTS - 1), align_bytes=64))
-        nc.vector.memset(result[DIRECT][:].bitcast(I32), 0)
-        result.append(result[0])
-        turned_message(0, P * DIRECT)
-        owns = [turn_state(i, half) for i, half in TURNED]
-        for place, (i, half) in enumerate(TURNED):
-            total = turned_sum(i, half, owns[place])
-            nc.vector.tensor_copy(result[i][:].indirect(half_list(dst, half)), total[:])
-            if place == 0:
-                turned_message(1, 0)
-            if half == 1:
-                nc.sync.dma_start(out[P * i : P * (i + 1), :], result[i][:])
+                q = jt * P // PART
+                quantize_h(q)
+                if q == 0:
+                    picked.append(keep.tile([P, HALF], F32, name="picked"))
+                    picked.append(keep.tile([P, HALF], F32, name="h_bf0", align_bytes=64))
+                    for c in range(PAIR):
+                        nc.vector.tensor_copy(picked[c][:], state[c][:].indirect(entries(dst, 0, HALF)))
+                else:
+                    if q == 1:
+                        second_pair_message(0)
+                    third_row_tile(q - 1, keep.tile([P, PART], F32, name="h_bf%d" % q, align_bytes=64))
+                first_pair(q)
+                if q > 0:
+                    second_pair_message(q)
+                if q % 2 == 1:
+                    first = (q - 1) * PART
+                    add_state(last_total[:, first : first + HALF], ROW_TILES - 1, first, HALF)
+        third_row_tile(PARTS - 1, pieces.tile([P, PART], F32, name="total"))
+        store(PAIR)
+        put(ROW_TILES - 1, 0, J, last_total[:])
+        store(ROW_TILES - 1)

@@ -31,6 +31,7 @@ PARTS = J // PART
 EDGE_TILES = J // P
 HALF_TILES = HALF // P
 ROW_TILES = N // P
+SHIFTED = 112
 PAIR = 2
 
 
@@ -49,44 +50,59 @@ def tile_list_msg_none_resL_kernel(
         src = keep.tile([P, J // LIST_ROWS], U16, name="src")
         dst = keep.tile([P, J // LIST_ROWS], U16, name="dst")
         table_sc = keep.tile([P, T // WORD], I32, name="table_sc", align_bytes=64)
+        ws_sc = keep.tile([P, R // WORD], I32, name="ws_sc", align_bytes=64)
+        e2m1_sc = keep.tile([P, PASSES + 1, R // WORD], I32, name="e2m1_sc", align_bytes=64)
         dst_sc = keep.tile([P, J], U8, name="dst_sc", align_bytes=64)
-        moved_sc = keep.tile([P, J // WORD], I32, name="moved_sc", align_bytes=64)
-        w_sc = keep.tile([P, PASSES, R // WORD], I32, name="w_sc", align_bytes=64)
         src_sc = keep.tile([P, J], U8, name="src_sc", align_bytes=64)
         table = keep.tile([P, PASSES, T], I32, name="table", align_bytes=64)
         ws = keep.tile([P, PASSES, R], I32, name="ws", align_bytes=64)
         wt = keep.tile([P, PASSES, R // 2], I32, name="wt", align_bytes=64)
         ident = keep.tile([P, P], F32, name="ident")
         edge_w = keep.tile([P, J], F32, name="edge_w")
+        result = [keep.tile([P, T], F32, name="result%d" % i) for i in range(ROW_TILES - 1)]
 
-        nc.sync.dma_start(src[:], offs)
         nc.sync.dma_start(dst[:], offs2)
+        nc.sync.dma_start(src[:], offs)
         nc.vector.memset(table_sc[:], 0)
-        nc.vector.memset(w_sc[:], 0)
-        nc.vector.memset(moved_sc[:], 0)
+        nc.vector.memset(ws_sc[:], 0)
+        nc.vector.memset(e2m1_sc[:], 0)
+        for tile in result:
+            nc.gpsimd.memset(tile[:].bitcast(I32), 0)
+        result.append(result[0])
         make_identity(nc, ident[:])
 
-        for q in range(QUADS):
-            nc.sync.dma_start(
-                table_sc[QUAD * q : QUAD * q + PASSES * ROWS, :],
-                tab_scales[:, ROWS * q : ROWS * (q + 1), :].bitcast(I32),
-            )
-        nc.sync.dma_start(table[:], tab_words.rearrange("a p t i -> p a (t i)").bitcast(I32))
-        for a in range(PASSES):
-            nc.sync.dma_start(ws[:, a, :], ws_words[a].rearrange("p r i -> p (r i)").bitcast(I32))
-        nc.sync.dma_start(wt[:], wt_words.rearrange("a p c -> p a c").bitcast(I32))
-        for first_row, scales in ((ROWS, ws_scales), (0, wt_scales)):
+        def load_packed_planes(tile, scales):
             for q in range(QUADS):
-                nc.scalar.dma_start(
-                    w_sc[QUAD * q + first_row : QUAD * q + first_row + ROWS, :, :],
-                    scales[:, ROWS * q : ROWS * (q + 1), :].rearrange("a q r -> q a r").bitcast(I32),
+                nc.sync.dma_start(
+                    tile[QUAD * q : QUAD * q + PASSES * ROWS, :], scales[:, ROWS * q : ROWS * (q + 1), :].bitcast(I32)
                 )
 
+        def load_wt_planes(quads):
+            for q in quads:
+                nc.sync.dma_start(
+                    e2m1_sc[QUAD * q : QUAD * q + ROWS, :PASSES, :],
+                    wt_scales[:, ROWS * q : ROWS * (q + 1), :].rearrange("a q r -> q a r").bitcast(I32),
+                )
+
+        load_packed_planes(table_sc, tab_scales)
+        table_words = tab_words.rearrange("a p t i -> p a (t i)").bitcast(I32)
+        for cols in (slice(0, T // 2), slice(T // 2, T)):
+            nc.sync.dma_start(table[:, :, cols], table_words[:, :, cols])
+        load_packed_planes(ws_sc, ws_scales)
+        load_wt_planes(range(QUADS // 2))
+        nc.sync.dma_start(ws[:], ws_words.rearrange("a p r i -> p a (r i)").bitcast(I32))
+        load_wt_planes(range(QUADS // 2, QUADS))
+        nc.vector.tensor_copy(dst_sc[:], table_sc[:].bitcast(U8).indirect(dst[:]))
+        nc.sync.dma_start(e2m1_sc[:SHIFTED, PASSES, :], dst_sc[ROWS : ROWS + SHIFTED, :].bitcast(I32))
+        nc.vector.tensor_copy(src_sc[:], table_sc[:].bitcast(U8).indirect(src[:]))
+        nc.sync.dma_start(wt[:], wt_words.rearrange("a p c -> p a c").bitcast(I32))
+
         wd_raw = [keep.tile([P, PACK, N], F32, name="wd_raw%d" % b) for b in range(PASSES)]
+        state = [keep.tile([P, T], F32, name="state%d" % i) for i in range(ROW_TILES)]
+        nc.sync.dma_start(state[0][:], rT[:P, :])
         for b in range(PASSES):
             nc.sync.dma_start(wd_raw[b][:], wd[SPAN * b : SPAN * (b + 1), :].rearrange("(p t) n -> p t n", t=PACK))
-        state = [keep.tile([P, T], F32, name="state%d" % i) for i in range(ROW_TILES)]
-        for i in range(ROW_TILES):
+        for i in range(1, ROW_TILES):
             nc.sync.dma_start(state[i][:], rT[P * i : P * (i + 1), :])
             if i == PAIR - 1:
                 nc.sync.dma_start(edge_w[:], wgo)
@@ -101,10 +117,6 @@ def tile_list_msg_none_resL_kernel(
         dst_words = [keep.tile([P, J], U32, name="dst_words%d" % a, align_bytes=64) for a in range(PASSES)]
         message = [keep.tile([P, PAIR, J], F32, name="message%d" % g) for g in range(PAIR)]
         last_total = keep.tile([P, J], F32, name="last_total")
-        result = [keep.tile([P, T], F32, name="result%d" % i) for i in range(ROW_TILES - 1)]
-        for tile in result:
-            nc.vector.memset(tile[:].bitcast(I32), 0)
-        result.append(result[0])
 
         def entries(offsets, first, count):
             return offsets[:, first // LIST_ROWS : (first + count) // LIST_ROWS]
@@ -118,7 +130,7 @@ def tile_list_msg_none_resL_kernel(
 
         def first_product(jt):
             cols = slice(P * jt, P * (jt + 1))
-            dst_planes = [dst_sc[:, cols], moved_sc[:].bitcast(U8)[:, cols]]
+            dst_planes = [dst_sc[:, cols], e2m1_sc[:, PASSES, :].bitcast(U8)[:, cols]]
             rows = rounded.tile([P, PASSES, 2, P, 2], BF16, name="rows", align_bytes=64)
             for b in range(PASSES):
                 r_cols = slice(SPAN * b, SPAN * (b + 1))
@@ -129,7 +141,7 @@ def tile_list_msg_none_resL_kernel(
                         lhsT=src_words[a][:, cols].bitcast(FP8X4),
                         lhsT_scale=src_sc[ROWS * a :, cols],
                         rhs=ws[:, a, r_cols].bitcast(FP8X4),
-                        rhs_scale=w_sc[:, a, :].bitcast(U8)[ROWS:, r_cols],
+                        rhs_scale=ws_sc[:].bitcast(U8)[ROWS * a :, r_cols],
                         start=(a == 0),
                         stop=False,
                     )
@@ -139,7 +151,7 @@ def tile_list_msg_none_resL_kernel(
                         lhsT=dst_words[a][:, cols].bitcast(FP8X4),
                         lhsT_scale=dst_planes[a],
                         rhs=wt[:, a, SPAN // 2 * b : SPAN // 2 * (b + 1)].bitcast(U8).bitcast(FP4X4),
-                        rhs_scale=w_sc[:, a, :].bitcast(U8)[:, r_cols],
+                        rhs_scale=e2m1_sc[:, a, :].bitcast(U8)[:, r_cols],
                         start=False,
                         stop=(a == PASSES - 1),
                     )
@@ -233,13 +245,6 @@ def tile_list_msg_none_resL_kernel(
             add_state(total[:], PAIR, q * PART, PART)
             put(PAIR, q * PART, PART, total[:])
 
-        nc.vector.tensor_copy(dst_sc[:], table_sc[:].bitcast(U8).indirect(dst[:]))
-        for q in range(QUADS):
-            nc.scalar.dma_start(
-                moved_sc[QUAD * q : QUAD * q + ROWS, :],
-                dst_sc[QUAD * q + ROWS : QUAD * q + 2 * ROWS, :].bitcast(I32),
-            )
-        nc.vector.tensor_copy(src_sc[:], table_sc[:].bitcast(U8).indirect(src[:]))
         for q in range(PARTS):
             gather_words(q)
 

@@ -67,7 +67,7 @@ def tile_list_msg_none_resL_kernel(
         nc.vector.memset(ws_sc[:], 0)
         nc.vector.memset(e2m1_sc[:], 0)
         for tile in result:
-            nc.gpsimd.memset(tile[:].bitcast(I32), 0)
+            nc.vector.memset(tile[:].bitcast(I32), 0)
         result.append(result[0])
         make_identity(nc, ident[:])
 

@@ -41,96 +41,90 @@ def tile_list_msg_none_resL_kernel(
     nc = tc.nc
     with ExitStack() as ctx:
         keep = ctx.enter_context(tc.tile_pool(name="keep", bufs=1))
-        rounded = ctx.enter_context(tc.tile_pool(name="rounded", bufs=3))
+        rounded = ctx.enter_context(tc.tile_pool(name="rounded", bufs=4))
         pieces = ctx.enter_context(tc.tile_pool(name="pieces", bufs=4))
-        sums = ctx.enter_context(tc.psum_pool(name="sums", bufs=3))
+        sums = ctx.enter_context(tc.psum_pool(name="sums", bufs=4))
         banks = ctx.enter_context(tc.psum_pool(name="banks", bufs=2))
-        ys = ctx.enter_context(tc.psum_pool(name="ys", bufs=3))
+        ys = ctx.enter_context(tc.psum_pool(name="ys", bufs=1))
 
         src = keep.tile([P, J // LIST_ROWS], U16, name="src")
         dst = keep.tile([P, J // LIST_ROWS], U16, name="dst")
         table_sc = keep.tile([P, T // WORD], I32, name="table_sc", align_bytes=64)
-        ws_sc = keep.tile([P, R // WORD], I32, name="ws_sc", align_bytes=64)
-        e2m1_sc = keep.tile([P, PASSES + 1, R // WORD], I32, name="e2m1_sc", align_bytes=64)
+        w_sc = keep.tile([P, PASSES + 1, R // WORD], I32, name="w_sc", align_bytes=64)
         dst_sc = keep.tile([P, J], U8, name="dst_sc", align_bytes=64)
         src_sc = keep.tile([P, J], U8, name="src_sc", align_bytes=64)
         table = keep.tile([P, PASSES, T], I32, name="table", align_bytes=64)
-        ws = keep.tile([P, PASSES, R], I32, name="ws", align_bytes=64)
+        ws = [keep.tile([P, PASSES, SPAN], I32, name="ws%d" % b, align_bytes=64) for b in range(PASSES)]
         wt = keep.tile([P, PASSES, R // 2], I32, name="wt", align_bytes=64)
         ident = keep.tile([P, P], F32, name="ident")
         edge_w = keep.tile([P, J], F32, name="edge_w")
-        result = [keep.tile([P, T], F32, name="result%d" % i) for i in range(ROW_TILES - 1)]
+        result = [keep.tile([P, T], F32, name="result")]
 
         nc.sync.dma_start(dst[:], offs2)
         nc.sync.dma_start(src[:], offs)
         nc.vector.memset(table_sc[:], 0)
-        nc.vector.memset(ws_sc[:], 0)
-        nc.vector.memset(e2m1_sc[:], 0)
-        for tile in result:
-            nc.vector.memset(tile[:].bitcast(I32), 0)
-        result.append(result[0])
+        nc.vector.memset(w_sc[:], 0)
+        nc.vector.memset(result[0][:].bitcast(I32), 0)
         make_identity(nc, ident[:])
 
-        def load_packed_planes(tile, scales):
+        def load_weight_planes(scales, first_row):
             for q in range(QUADS):
                 nc.sync.dma_start(
-                    tile[QUAD * q : QUAD * q + PASSES * ROWS, :], scales[:, ROWS * q : ROWS * (q + 1), :].bitcast(I32)
+                    w_sc[QUAD * q + first_row : QUAD * q + first_row + ROWS, :PASSES, :],
+                    scales[:, ROWS * q : ROWS * (q + 1), :].rearrange("a q r -> q a r").bitcast(I32),
                 )
 
-        def load_wt_planes(quads):
-            for q in quads:
-                nc.sync.dma_start(
-                    e2m1_sc[QUAD * q : QUAD * q + ROWS, :PASSES, :],
-                    wt_scales[:, ROWS * q : ROWS * (q + 1), :].rearrange("a q r -> q a r").bitcast(I32),
-                )
-
-        load_packed_planes(table_sc, tab_scales)
+        for q in range(QUADS):
+            nc.sync.dma_start(
+                table_sc[QUAD * q : QUAD * q + PASSES * ROWS, :],
+                tab_scales[:, ROWS * q : ROWS * (q + 1), :].bitcast(I32),
+            )
         table_words = tab_words.rearrange("a p t i -> p a (t i)").bitcast(I32)
         for cols in (slice(0, T // 2), slice(T // 2, T)):
             nc.sync.dma_start(table[:, :, cols], table_words[:, :, cols])
-        load_packed_planes(ws_sc, ws_scales)
-        load_wt_planes(range(QUADS // 2))
-        nc.sync.dma_start(ws[:], ws_words.rearrange("a p r i -> p a (r i)").bitcast(I32))
-        load_wt_planes(range(QUADS // 2, QUADS))
-        nc.vector.tensor_copy(dst_sc[:], table_sc[:].bitcast(U8).indirect(dst[:]))
-        nc.sync.dma_start(e2m1_sc[:SHIFTED, PASSES, :], dst_sc[ROWS : ROWS + SHIFTED, :].bitcast(I32))
-        nc.vector.tensor_copy(src_sc[:], table_sc[:].bitcast(U8).indirect(src[:]))
+        ws_rows = ws_words.rearrange("a p r i -> p a (r i)").bitcast(I32)
+        load_weight_planes(ws_scales, ROWS)
+        nc.sync.dma_start(ws[0][:], ws_rows[:, :, :SPAN])
         nc.sync.dma_start(wt[:], wt_words.rearrange("a p c -> p a c").bitcast(I32))
+        load_weight_planes(wt_scales, 0)
+        nc.vector.tensor_copy(dst_sc[:], table_sc[:].bitcast(U8).indirect(dst[:]))
+        nc.sync.dma_start(w_sc[:SHIFTED, PASSES, :], dst_sc[ROWS : ROWS + SHIFTED, :].bitcast(I32))
+        nc.vector.tensor_copy(src_sc[:], table_sc[:].bitcast(U8).indirect(src[:]))
+        nc.sync.dma_start(ws[1][:], ws_rows[:, :, SPAN:])
 
         wd_raw = [keep.tile([P, PACK, N], F32, name="wd_raw%d" % b) for b in range(PASSES)]
         state = [keep.tile([P, T], F32, name="state%d" % i) for i in range(ROW_TILES)]
-        nc.sync.dma_start(state[0][:], rT[:P, :])
         for b in range(PASSES):
             nc.sync.dma_start(wd_raw[b][:], wd[SPAN * b : SPAN * (b + 1), :].rearrange("(p t) n -> p t n", t=PACK))
-        for i in range(1, ROW_TILES):
+        for i in range(ROW_TILES):
             nc.sync.dma_start(state[i][:], rT[P * i : P * (i + 1), :])
-            if i == PAIR - 1:
+            if i == 0:
                 nc.sync.dma_start(edge_w[:], wgo)
 
         h_codes = keep.tile([P, PARTS, PASSES, PART], U32, name="h_codes", align_bytes=64)
         h_sc = keep.tile([P, PARTS, PASSES, PART], U8, name="h_sc", align_bytes=64)
-        wd_bf = [keep.tile([P, PASSES, PAIR * P, PACK], BF16, name="wd_bf%d" % g, align_bytes=64) for g in range(PAIR)]
-        wd_codes = keep.tile([P, PAIR, PASSES, PAIR * P], U32, name="wd_codes", align_bytes=64)
-        wd_sc = keep.tile([P, PAIR, PASSES, PAIR * P], U8, name="wd_sc", align_bytes=64)
+        wd_bf = keep.tile([P, ROW_TILES, PASSES, P, PACK], BF16, name="wd_bf", align_bytes=64)
+        wd_codes = keep.tile([P, ROW_TILES, PASSES, P], U32, name="wd_codes", align_bytes=64)
+        wd_sc = keep.tile([P, ROW_TILES, PASSES, P], U8, name="wd_sc", align_bytes=64)
         h_bf = [keep.tile([P, PASSES, PART, PACK], BF16, name="h_bf%d" % q, align_bytes=64) for q in range(PARTS)]
         src_words = [keep.tile([P, J], U32, name="src_words%d" % a, align_bytes=64) for a in range(PASSES)]
         dst_words = [keep.tile([P, J], U32, name="dst_words%d" % a, align_bytes=64) for a in range(PASSES)]
-        message = [keep.tile([P, PAIR, J], F32, name="message%d" % g) for g in range(PAIR)]
+        message = keep.tile([P, ROW_TILES, J], F32, name="message")
         last_total = keep.tile([P, J], F32, name="last_total")
 
         def entries(offsets, first, count):
             return offsets[:, first // LIST_ROWS : (first + count) // LIST_ROWS]
 
-        def gather_words(q):
-            cols = slice(q * PART, (q + 1) * PART)
-            for a in range(PASSES):
-                window = table[:, a, :].bitcast(U32)
-                nc.vector.tensor_copy(src_words[a][:, cols], window.indirect(entries(src, q * PART, PART)))
-                nc.vector.tensor_copy(dst_words[a][:, cols], window.indirect(entries(dst, q * PART, PART)))
+        def gather_words(first, count):
+            cols = slice(first, first + count)
+            for words, offsets in ((src_words, src), (dst_words, dst)):
+                for a in range(PASSES):
+                    window = table[:, a, :].bitcast(U32)
+                    nc.vector.tensor_copy(words[a][:, cols], window.indirect(entries(offsets, first, count)))
 
         def first_product(jt):
             cols = slice(P * jt, P * (jt + 1))
-            dst_planes = [dst_sc[:, cols], e2m1_sc[:, PASSES, :].bitcast(U8)[:, cols]]
+            dst_planes = [dst_sc[:, cols], w_sc[:, PASSES, :].bitcast(U8)[:, cols]]
             rows = rounded.tile([P, PASSES, 2, P, 2], BF16, name="rows", align_bytes=64)
             for b in range(PASSES):
                 r_cols = slice(SPAN * b, SPAN * (b + 1))
@@ -140,8 +134,8 @@ def tile_list_msg_none_resL_kernel(
                         out=acc[:],
                         lhsT=src_words[a][:, cols].bitcast(FP8X4),
                         lhsT_scale=src_sc[ROWS * a :, cols],
-                        rhs=ws[:, a, r_cols].bitcast(FP8X4),
-                        rhs_scale=ws_sc[:].bitcast(U8)[ROWS * a :, r_cols],
+                        rhs=ws[b][:, a, :].bitcast(FP8X4),
+                        rhs_scale=w_sc[:, a, :].bitcast(U8)[ROWS:, r_cols],
                         start=(a == 0),
                         stop=False,
                     )
@@ -151,7 +145,7 @@ def tile_list_msg_none_resL_kernel(
                         lhsT=dst_words[a][:, cols].bitcast(FP8X4),
                         lhsT_scale=dst_planes[a],
                         rhs=wt[:, a, SPAN // 2 * b : SPAN // 2 * (b + 1)].bitcast(U8).bitcast(FP4X4),
-                        rhs_scale=e2m1_sc[:, a, :].bitcast(U8)[:, r_cols],
+                        rhs_scale=w_sc[:, a, :].bitcast(U8)[:, r_cols],
                         start=False,
                         stop=(a == PASSES - 1),
                     )
@@ -178,37 +172,33 @@ def tile_list_msg_none_resL_kernel(
                 in_=h_bf[q][:].rearrange("p b j t -> p (b j t)"),
             )
 
-        def round_wd(g, b):
-            nc.scalar.copy(
-                wd_bf[g][:, b], wd_raw[b][:, :, PAIR * P * g : PAIR * P * (g + 1)].rearrange("p t n -> p n t")
-            )
-
-        def quantize_wd(g):
+        def quantize_wd(first, count):
+            for i in range(first, first + count):
+                for b in range(PASSES):
+                    nc.scalar.copy(wd_bf[:, i, b], wd_raw[b][:, :, P * i : P * (i + 1)].rearrange("p t n -> p n t"))
+            tiles_i = slice(first, first + count)
             nc.vector.quantize_mx(
-                out=wd_codes[:, g].rearrange("p b n -> p (b n)").bitcast(FP8X4),
-                scales=wd_sc[:, g].rearrange("p b n -> p (b n)"),
-                in_=wd_bf[g][:].rearrange("p b n t -> p (b n t)"),
+                out=wd_codes[:, tiles_i].rearrange("p i b n -> p (i b n)").bitcast(FP8X4),
+                scales=wd_sc[:, tiles_i].rearrange("p i b n -> p (i b n)"),
+                in_=wd_bf[:, tiles_i].rearrange("p i b n t -> p (i b n t)"),
             )
 
-        def second_product(g, q):
-            bank = ys.tile([P, PAIR, PART], F32, name="y")
-            for c in range(PAIR):
+        def messages(bank, pairs):
+            for c, (i, q) in enumerate(pairs):
                 for b in range(PASSES):
                     nc.tensor.matmul_mx(
                         out=bank[:, c, :],
-                        lhsT=wd_codes[:, g, b, P * c : P * (c + 1)].bitcast(FP8X4),
-                        lhsT_scale=wd_sc[:, g, b, P * c : P * (c + 1)],
+                        lhsT=wd_codes[:, i, b, :].bitcast(FP8X4),
+                        lhsT_scale=wd_sc[:, i, b, :],
                         rhs=h_codes[:, q, b, :].bitcast(FP8X4),
                         rhs_scale=h_sc[:, q, b, :],
                         start=(b == 0),
                         stop=(b == PASSES - 1),
                     )
-            return bank
 
         def add_state(total, i, first, count):
-            g, c = divmod(i, PAIR)
             nc.vector.tensor_tensor(
-                total, state[i][:].indirect(entries(dst, first, count)), message[g][:, c, first : first + count], ADD
+                total, state[i][:].indirect(entries(dst, first, count)), message[:, i, first : first + count], ADD
             )
 
         def put(i, first, count, total):
@@ -219,64 +209,58 @@ def tile_list_msg_none_resL_kernel(
         def store(i):
             nc.sync.dma_start(out[P * i : P * (i + 1), :], result[i][:])
 
-        picked = []
-
-        def first_pair(q):
-            cols = slice(q * PART, (q + 1) * PART)
-            bank = second_product(0, q)
-            totals = [pieces.tile([P, PART], F32, name="total") for c in range(PAIR)]
-            if q * PART < HALF:
-                for c in range(PAIR):
-                    nc.vector.tensor_tensor(totals[c][:], bank[:, c, :], picked[c][:, cols], ADD)
-            else:
-                nc.scalar.copy(message[0][:, :, cols], bank[:])
-                for c in range(PAIR):
-                    add_state(totals[c][:], c, q * PART, PART)
-            for c in range(PAIR):
-                put(c, q * PART, PART, totals[c][:])
-                if q == PARTS - 1:
-                    store(c)
-
-        def second_pair_message(q):
-            bank = second_product(1, q)
-            nc.scalar.copy(message[1][:, :, q * PART : (q + 1) * PART], bank[:])
-
-        def third_row_tile(q, total):
+        def third_piece(q, total):
             add_state(total[:], PAIR, q * PART, PART)
             put(PAIR, q * PART, PART, total[:])
 
-        for q in range(PARTS):
-            gather_words(q)
+        for first, count in ((0, PART), (PART, PART), (HALF, HALF)):
+            gather_words(first, count)
+        third = keep.tile([P, T], F32, name="table", align_bytes=64)
+        nc.vector.memset(third[:].bitcast(I32), 0)
 
-        rows = first_product(0)
-        for jt in range(EDGE_TILES):
-            ahead = first_product(jt + 1) if jt + 1 < EDGE_TILES else None
-            turn_h(jt, rows)
-            rows = ahead
-            if jt < PAIR * PASSES:
-                g, b = divmod(jt, PASSES)
-                round_wd(g, b)
-                if b == PASSES - 1:
-                    quantize_wd(g)
-            if (jt + 1) * P % PART == 0:
-                q = jt * P // PART
-                quantize_h(q)
-                if q == 0:
-                    picked.append(keep.tile([P, HALF], F32, name="picked"))
-                    picked.append(keep.tile([P, HALF], F32, name="h_bf0", align_bytes=64))
-                    for c in range(PAIR):
-                        nc.vector.tensor_copy(picked[c][:], state[c][:].indirect(entries(dst, 0, HALF)))
-                else:
-                    if q == 1:
-                        second_pair_message(0)
-                    third_row_tile(q - 1, keep.tile([P, PART], F32, name="h_bf%d" % q, align_bytes=64))
-                first_pair(q)
-                if q > 0:
-                    second_pair_message(q)
-                if q % 2 == 1:
-                    first = (q - 1) * PART
-                    add_state(last_total[:, first : first + HALF], ROW_TILES - 1, first, HALF)
-        third_row_tile(PARTS - 1, pieces.tile([P, PART], F32, name="total"))
+        tiles = PART // P
+        rows = [first_product(jt) for jt in range(tiles)]
+        for q in range(PARTS):
+            last = q == PARTS - 1
+            cols = slice(q * PART, (q + 1) * PART)
+            if not last:
+                rows.append(first_product(tiles * (q + 1)))
+            if q == 0:
+                quantize_wd(0, PAIR)
+            for jt in range(tiles * q, tiles * (q + 1)):
+                turn_h(jt, rows[jt])
+            quantize_h(q)
+            if q == 0:
+                result.append(keep.tile([P, T], F32, name="h_bf0", align_bytes=64))
+                nc.vector.memset(result[1][:].bitcast(I32), 0)
+                result.extend([third, result[0]])
+                quantize_wd(PAIR, 1)
+            else:
+                third_piece(q - 1, keep.tile([P, PART], F32, name="h_bf%d" % q, align_bytes=64))
+            if not last:
+                rows.append(first_product(tiles * (q + 1) + 1))
+            bank = ys.tile([P, PAIR, PART], F32, name="y_pair")
+            messages(bank, [(c, q) for c in range(PAIR)])
+            nc.scalar.copy(message[:, :PAIR, cols], bank[:])
+            bank = ys.tile([P, 1, PART], F32, name="y_third")
+            messages(bank, [(PAIR, q)])
+            nc.scalar.copy(message[:, PAIR, cols], bank[:, 0, :])
+            totals = [pieces.tile([P, PART], F32, name="total") for c in range(PAIR)]
+            for c in range(PAIR):
+                add_state(totals[c][:], c, q * PART, PART)
+            for c in range(PAIR):
+                put(c, q * PART, PART, totals[c][:])
+                if last:
+                    store(c)
+        third_piece(PARTS - 1, pieces.tile([P, PART], F32, name="total"))
         store(PAIR)
-        put(ROW_TILES - 1, 0, J, last_total[:])
-        store(ROW_TILES - 1)
+        quantize_wd(PAIR + 1, 1)
+        for half in range(J // HALF):
+            bank = sums.tile([P, PAIR, PART], F32, name="acc")
+            messages(bank, [(PAIR + 1, PAIR * half + c) for c in range(PAIR)])
+            nc.scalar.copy(
+                message[:, PAIR + 1, half * HALF : (half + 1) * HALF], bank[:].rearrange("n c j -> n (c j)")
+            )
+        add_state(last_total[:], PAIR + 1, 0, J)
+        put(PAIR + 1, 0, J, last_total[:])
+        store(PAIR + 1)

@@ -58,7 +58,7 @@ def tile_list_msg_none_resL_kernel(
         wt = keep.tile([P, PASSES, R // 2], I32, name="wt", align_bytes=64)
         ident = keep.tile([P, P], F32, name="ident")
         edge_w = keep.tile([P, J], F32, name="edge_w")
-        result = [keep.tile([P, T], F32, name="result")]
+        result = [keep.tile([P, T], F32, name="result%d" % i) for i in range(PAIR)]
 
         nc.sync.dma_start(dst[:], offs2)
         nc.sync.dma_start(src[:], offs)
@@ -66,6 +66,8 @@ def tile_list_msg_none_resL_kernel(
         nc.vector.memset(w_sc[:], 0)
         nc.vector.memset(result[0][:].bitcast(I32), 0)
         make_identity(nc, ident[:])
+        for tile in result[1:]:
+            nc.vector.memset(tile[:].bitcast(I32), 0)
 
         def load_weight_planes(scales, first_row):
             for q in range(QUADS):
@@ -90,16 +92,32 @@ def tile_list_msg_none_resL_kernel(
         nc.vector.tensor_copy(dst_sc[:], table_sc[:].bitcast(U8).indirect(dst[:]))
         nc.sync.dma_start(w_sc[:SHIFTED, PASSES, :], dst_sc[ROWS : ROWS + SHIFTED, :].bitcast(I32))
         nc.vector.tensor_copy(src_sc[:], table_sc[:].bitcast(U8).indirect(src[:]))
-        nc.sync.dma_start(ws[1][:], ws_rows[:, :, SPAN:])
 
-        wd_raw = [keep.tile([P, PACK, N], F32, name="wd_raw%d" % b) for b in range(PASSES)]
+        wd_raw = [
+            [keep.tile([P, PACK, PAIR * P], F32, name="wd_raw%d%d" % (g, b)) for b in range(PASSES)] for g in range(PAIR)
+        ]
         state = [keep.tile([P, T], F32, name="state%d" % i) for i in range(ROW_TILES)]
-        for b in range(PASSES):
-            nc.sync.dma_start(wd_raw[b][:], wd[SPAN * b : SPAN * (b + 1), :].rearrange("(p t) n -> p t n", t=PACK))
-        for i in range(ROW_TILES):
+
+        def load_wd(g):
+            for b in range(PASSES):
+                rows = wd[SPAN * b : SPAN * (b + 1), PAIR * P * g : PAIR * P * (g + 1)]
+                nc.sync.dma_start(wd_raw[g][b][:], rows.rearrange("(p t) n -> p t n", t=PACK))
+
+        def load_state(i):
             nc.sync.dma_start(state[i][:], rT[P * i : P * (i + 1), :])
-            if i == 0:
-                nc.sync.dma_start(edge_w[:], wgo)
+
+        def load_edge_w(first, count):
+            nc.sync.dma_start(edge_w[:, first : first + count], wgo[:, first : first + count])
+
+        load_wd(0)
+        nc.sync.dma_start(ws[1][:], ws_rows[:, :, SPAN:])
+        load_state(3)
+        load_wd(1)
+        load_state(0)
+        load_edge_w(0, PART)
+        load_state(1)
+        load_edge_w(PART, J - PART)
+        load_state(2)
 
         h_codes = keep.tile([P, PARTS, PASSES, PART], U32, name="h_codes", align_bytes=64)
         h_sc = keep.tile([P, PARTS, PASSES, PART], U8, name="h_sc", align_bytes=64)
@@ -109,7 +127,7 @@ def tile_list_msg_none_resL_kernel(
         h_bf = [keep.tile([P, PASSES, PART, PACK], BF16, name="h_bf%d" % q, align_bytes=64) for q in range(PARTS)]
         src_words = [keep.tile([P, J], U32, name="src_words%d" % a, align_bytes=64) for a in range(PASSES)]
         dst_words = [keep.tile([P, J], U32, name="dst_words%d" % a, align_bytes=64) for a in range(PASSES)]
-        message = keep.tile([P, ROW_TILES, J], F32, name="message")
+        message = keep.tile([P, ROW_TILES - 1, J], F32, name="message")
         last_total = keep.tile([P, J], F32, name="last_total")
 
         def entries(offsets, first, count):
@@ -122,11 +140,10 @@ def tile_list_msg_none_resL_kernel(
                     window = table[:, a, :].bitcast(U32)
                     nc.vector.tensor_copy(words[a][:, cols], window.indirect(entries(offsets, first, count)))
 
-        def first_product(jt):
+        def first_product(jt, passes):
             cols = slice(P * jt, P * (jt + 1))
             dst_planes = [dst_sc[:, cols], w_sc[:, PASSES, :].bitcast(U8)[:, cols]]
-            rows = rounded.tile([P, PASSES, 2, P, 2], BF16, name="rows", align_bytes=64)
-            for b in range(PASSES):
+            for b in passes:
                 r_cols = slice(SPAN * b, SPAN * (b + 1))
                 acc = sums.tile([P, SPAN], F32, name="acc")
                 for a in range(PASSES):
@@ -149,12 +166,11 @@ def tile_list_msg_none_resL_kernel(
                         start=False,
                         stop=(a == PASSES - 1),
                     )
-                nc.scalar.copy(rows[:, b], acc[:].rearrange("j (p u e) -> j u p e", u=2, e=2))
-            return rows
+                nc.scalar.copy(rows[jt][:, b], acc[:].rearrange("j (p u e) -> j u p e", u=2, e=2))
 
-        def turn_h(jt, rows):
+        def turn_h(jt):
             q, c = divmod(jt, PART // P)
-            pairs = rows[:].rearrange("j b u p e -> j (b u p e)").bitcast(F32)
+            pairs = rows[jt][:].rearrange("j b u p e -> j (b u p e)").bitcast(F32)
             bank = banks.tile([P, PASSES, 2, P], F32, name="bank")
             for b in range(PASSES):
                 for u in range(2):
@@ -174,8 +190,10 @@ def tile_list_msg_none_resL_kernel(
 
         def quantize_wd(first, count):
             for i in range(first, first + count):
+                g, c = divmod(i, PAIR)
                 for b in range(PASSES):
-                    nc.scalar.copy(wd_bf[:, i, b], wd_raw[b][:, :, P * i : P * (i + 1)].rearrange("p t n -> p n t"))
+                    raw = wd_raw[g][b][:, :, P * c : P * (c + 1)]
+                    nc.scalar.copy(wd_bf[:, i, b], raw.rearrange("p t n -> p n t"))
             tiles_i = slice(first, first + count)
             nc.vector.quantize_mx(
                 out=wd_codes[:, tiles_i].rearrange("p i b n -> p (i b n)").bitcast(FP8X4),
@@ -215,52 +233,105 @@ def tile_list_msg_none_resL_kernel(
 
         for first, count in ((0, PART), (PART, PART), (HALF, HALF)):
             gather_words(first, count)
-        third = keep.tile([P, T], F32, name="table", align_bytes=64)
-        nc.vector.memset(third[:].bitcast(I32), 0)
+        picked = keep.tile([P, J], F32, name="picked")
+        nc.vector.tensor_copy(picked[:], state[PAIR + 1][:].indirect(dst[:]))
 
-        tiles = PART // P
-        rows = [first_product(jt) for jt in range(tiles)]
-        for q in range(PARTS):
-            last = q == PARTS - 1
-            cols = slice(q * PART, (q + 1) * PART)
-            if not last:
-                rows.append(first_product(tiles * (q + 1)))
-            if q == 0:
-                quantize_wd(0, PAIR)
-            for jt in range(tiles * q, tiles * (q + 1)):
-                turn_h(jt, rows[jt])
-            quantize_h(q)
-            if q == 0:
-                result.append(keep.tile([P, T], F32, name="h_bf0", align_bytes=64))
-                nc.vector.memset(result[1][:].bitcast(I32), 0)
-                result.extend([third, result[0]])
-                quantize_wd(PAIR, 1)
-            else:
-                third_piece(q - 1, keep.tile([P, PART], F32, name="h_bf%d" % q, align_bytes=64))
-            if not last:
-                rows.append(first_product(tiles * (q + 1) + 1))
-            bank = ys.tile([P, PAIR, PART], F32, name="y_pair")
-            messages(bank, [(c, q) for c in range(PAIR)])
-            nc.scalar.copy(message[:, :PAIR, cols], bank[:])
+        def third_message(q):
             bank = ys.tile([P, 1, PART], F32, name="y_third")
             messages(bank, [(PAIR, q)])
-            nc.scalar.copy(message[:, PAIR, cols], bank[:, 0, :])
+            nc.scalar.copy(message[:, PAIR, q * PART : (q + 1) * PART], bank[:, 0, :])
+
+        def whole_tile(jt):
+            rows.append(rounded.tile([P, PASSES, 2, P, 2], BF16, name="rows", align_bytes=64))
+            first_product(jt, range(PASSES))
+
+        def new_rows():
+            rows.append(rounded.tile([P, PASSES, 2, P, 2], BF16, name="rows", align_bytes=64))
+
+        def turn_part(q):
+            for jt in range(tiles * q, tiles * (q + 1)):
+                turn_h(jt)
+
+        def first_pair(q):
             totals = [pieces.tile([P, PART], F32, name="total") for c in range(PAIR)]
             for c in range(PAIR):
                 add_state(totals[c][:], c, q * PART, PART)
             for c in range(PAIR):
                 put(c, q * PART, PART, totals[c][:])
-                if last:
+                if q == PARTS - 1:
                     store(c)
+
+        def pair_message(q):
+            bank = ys.tile([P, PAIR, PART], F32, name="y_pair")
+            messages(bank, [(c, q) for c in range(PAIR)])
+            nc.scalar.copy(message[:, :PAIR, q * PART : (q + 1) * PART], bank[:])
+
+        tiles = PART // P
+        rows = []
+        quantize_wd(0, PAIR)
+        new_rows()
+        new_rows()
+        for b in range(PASSES):
+            for jt in range(tiles):
+                first_product(jt, [b])
+        turn_part(0)
+        quantize_h(0)
+        result.append(keep.tile([P, T], F32, name="h_bf0", align_bytes=64))
+        nc.vector.memset(result[PAIR][:].bitcast(I32), 0)
+        result.append(result[0])
+        quantize_wd(PAIR, 1)
+        whole_tile(2)
+        new_rows()
+        first_product(3, [0])
+        pair_message(0)
+        third_message(0)
+        first_pair(0)
+        first_product(3, [1])
+        turn_part(1)
+        for q in range(1, PARTS):
+            quantize_h(q)
+            third_piece(q - 1, keep.tile([P, PART], F32, name="h_bf%d" % q, align_bytes=64))
+            if q + 1 < PARTS:
+                for jt in range(tiles * (q + 1), tiles * (q + 2)):
+                    whole_tile(jt)
+                turn_part(q + 1)
+            pair_message(q)
+            third_message(q)
+            first_pair(q)
         third_piece(PARTS - 1, pieces.tile([P, PART], F32, name="total"))
         store(PAIR)
         quantize_wd(PAIR + 1, 1)
+        own = keep.tile([P, EDGE_TILES, P], F32, name="own")
+        turned = keep.tile([P, EDGE_TILES, P], F32, name="turned")
         for half in range(J // HALF):
-            bank = sums.tile([P, PAIR, PART], F32, name="acc")
-            messages(bank, [(PAIR + 1, PAIR * half + c) for c in range(PAIR)])
-            nc.scalar.copy(
-                message[:, PAIR + 1, half * HALF : (half + 1) * HALF], bank[:].rearrange("n c j -> n (c j)")
-            )
-        add_state(last_total[:], PAIR + 1, 0, J)
+            jts = slice(half * HALF_TILES, (half + 1) * HALF_TILES)
+            bank = sums.tile([P, HALF_TILES, P], F32, name="acc")
+            for c in range(HALF_TILES):
+                jt = half * HALF_TILES + c
+                nc.tensor.transpose(bank[:, c, :], picked[:, P * jt : P * (jt + 1)], ident[:])
+            nc.scalar.copy(own[:, jts, :], bank[:])
+        for half in range(J // HALF):
+            jts = slice(half * HALF_TILES, (half + 1) * HALF_TILES)
+            bank = sums.tile([P, HALF_TILES, P], F32, name="acc")
+            for c in range(HALF_TILES):
+                q, at = divmod(P * (half * HALF_TILES + c), PART)
+                for b in range(PASSES):
+                    nc.tensor.matmul_mx(
+                        out=bank[:, c, :],
+                        lhsT=h_codes[:, q, b, at : at + P].bitcast(FP8X4),
+                        lhsT_scale=h_sc[:, q, b, at : at + P],
+                        rhs=wd_codes[:, PAIR + 1, b, :].bitcast(FP8X4),
+                        rhs_scale=wd_sc[:, PAIR + 1, b, :],
+                        start=(b == 0),
+                        stop=(b == PASSES - 1),
+                    )
+            nc.scalar.copy(turned[:, jts, :], bank[:])
+        for half in range(J // HALF):
+            bank = sums.tile([P, HALF_TILES, P], F32, name="acc")
+            for c in range(HALF_TILES):
+                jt = half * HALF_TILES + c
+                for first, term in ((True, own[:, jt, :]), (False, turned[:, jt, :])):
+                    nc.tensor.matmul(bank[:, c, :], term, ident[:], start=first, stop=not first, is_transpose=True)
+            nc.scalar.copy(last_total[:, half * HALF : (half + 1) * HALF], bank[:].rearrange("n c j -> n (c j)"))
         put(PAIR + 1, 0, J, last_total[:])
         store(PAIR + 1)

@@ -31,7 +31,7 @@ PARTS = J // PART
 EDGE_TILES = J // P
 HALF_TILES = HALF // P
 ROW_TILES = N // P
-SHIFTED = 112
+SHIFTED = 100
 PAIR = 2
 
 
@@ -71,7 +71,7 @@ def tile_list_msg_none_resL_kernel(
 
         def load_weight_planes(scales, first_row):
             for q in range(QUADS):
-                nc.sync.dma_start(
+                nc.scalar.dma_start(
                     w_sc[QUAD * q + first_row : QUAD * q + first_row + ROWS, :PASSES, :],
                     scales[:, ROWS * q : ROWS * (q + 1), :].rearrange("a q r -> q a r").bitcast(I32),
                 )
@@ -82,15 +82,14 @@ def tile_list_msg_none_resL_kernel(
                 tab_scales[:, ROWS * q : ROWS * (q + 1), :].bitcast(I32),
             )
         table_words = tab_words.rearrange("a p t i -> p a (t i)").bitcast(I32)
-        for cols in (slice(0, T // 2), slice(T // 2, T)):
-            nc.sync.dma_start(table[:, :, cols], table_words[:, :, cols])
+        nc.sync.dma_start(table[:], table_words)
         ws_rows = ws_words.rearrange("a p r i -> p a (r i)").bitcast(I32)
         load_weight_planes(ws_scales, ROWS)
         nc.sync.dma_start(ws[0][:], ws_rows[:, :, :SPAN])
         nc.sync.dma_start(wt[:], wt_words.rearrange("a p c -> p a c").bitcast(I32))
         load_weight_planes(wt_scales, 0)
         nc.vector.tensor_copy(dst_sc[:], table_sc[:].bitcast(U8).indirect(dst[:]))
-        nc.sync.dma_start(w_sc[:SHIFTED, PASSES, :], dst_sc[ROWS : ROWS + SHIFTED, :].bitcast(I32))
+        nc.scalar.dma_start(w_sc[:SHIFTED, PASSES, :], dst_sc[ROWS : ROWS + SHIFTED, :].bitcast(I32))
         nc.vector.tensor_copy(src_sc[:], table_sc[:].bitcast(U8).indirect(src[:]))
 
         wd_raw = [
@@ -109,8 +108,8 @@ def tile_list_msg_none_resL_kernel(
         def load_edge_w(first, count):
             nc.sync.dma_start(edge_w[:, first : first + count], wgo[:, first : first + count])
 
-        load_wd(0)
         nc.sync.dma_start(ws[1][:], ws_rows[:, :, SPAN:])
+        load_wd(0)
         load_state(3)
         load_wd(1)
         load_state(0)
@@ -281,12 +280,10 @@ def tile_list_msg_none_resL_kernel(
         result.append(result[0])
         quantize_wd(PAIR, 1)
         whole_tile(2)
-        new_rows()
-        first_product(3, [0])
         pair_message(0)
         third_message(0)
         first_pair(0)
-        first_product(3, [1])
+        whole_tile(3)
         turn_part(1)
         for q in range(1, PARTS):
             quantize_h(q)

@@ -64,8 +64,9 @@ def tile_list_msg_none_resL_kernel(
         nc.sync.dma_start(src[:], offs)
         nc.vector.memset(table_sc[:], 0)
         nc.vector.memset(w_sc[:], 0)
+        nc.vector.memset(ident[:], 0.0)
+        make_identity(nc, ident[:], nomemset=True)
         nc.vector.memset(result[0][:].bitcast(I32), 0)
-        make_identity(nc, ident[:])
         for tile in result[1:]:
             nc.vector.memset(tile[:].bitcast(I32), 0)
 
@@ -86,6 +87,7 @@ def tile_list_msg_none_resL_kernel(
         ws_rows = ws_words.rearrange("a p r i -> p a (r i)").bitcast(I32)
         load_weight_planes(ws_scales, ROWS)
         nc.sync.dma_start(ws[0][:], ws_rows[:, :, :SPAN])
+        nc.sync.dma_start(ws[1][:], ws_rows[:, :, SPAN:])
         nc.sync.dma_start(wt[:], wt_words.rearrange("a p c -> p a c").bitcast(I32))
         load_weight_planes(wt_scales, 0)
         nc.vector.tensor_copy(dst_sc[:], table_sc[:].bitcast(U8).indirect(dst[:]))
@@ -108,7 +110,6 @@ def tile_list_msg_none_resL_kernel(
         def load_edge_w(first, count):
             nc.sync.dma_start(edge_w[:, first : first + count], wgo[:, first : first + count])
 
-        nc.sync.dma_start(ws[1][:], ws_rows[:, :, SPAN:])
         load_wd(0)
         load_state(3)
         load_wd(1)
@@ -139,33 +140,49 @@ def tile_list_msg_none_resL_kernel(
                     window = table[:, a, :].bitcast(U32)
                     nc.vector.tensor_copy(words[a][:, cols], window.indirect(entries(offsets, first, count)))
 
-        def first_product(jt, passes):
+        def first_pass(acc, jt, b, step):
             cols = slice(P * jt, P * (jt + 1))
-            dst_planes = [dst_sc[:, cols], w_sc[:, PASSES, :].bitcast(U8)[:, cols]]
+            r_cols = slice(SPAN * b, SPAN * (b + 1))
+            side, a = divmod(step, PASSES)
+            if side == 0:
+                lhsT, lhsT_scale = src_words[a][:, cols], src_sc[ROWS * a :, cols]
+                rhs, rhs_scale = ws[b][:, a, :].bitcast(FP8X4), w_sc[:, a, :].bitcast(U8)[ROWS:, r_cols]
+            else:
+                lhsT = dst_words[a][:, cols]
+                lhsT_scale = [dst_sc[:, cols], w_sc[:, PASSES, :].bitcast(U8)[:, cols]][a]
+                rhs = wt[:, a, SPAN // 2 * b : SPAN // 2 * (b + 1)].bitcast(U8).bitcast(FP4X4)
+                rhs_scale = w_sc[:, a, :].bitcast(U8)[:, r_cols]
+            nc.tensor.matmul_mx(
+                out=acc[:],
+                lhsT=lhsT.bitcast(FP8X4),
+                lhsT_scale=lhsT_scale,
+                rhs=rhs,
+                rhs_scale=rhs_scale,
+                start=(step == 0),
+                stop=(step == 2 * PASSES - 1),
+            )
+
+        def round_sum(acc, jt, b):
+            nc.scalar.copy(rows[jt][:, b], acc[:].rearrange("j (p u e) -> j u p e", u=2, e=2))
+
+        def first_product(jt, passes):
             for b in passes:
-                r_cols = slice(SPAN * b, SPAN * (b + 1))
                 acc = sums.tile([P, SPAN], F32, name="acc")
-                for a in range(PASSES):
-                    nc.tensor.matmul_mx(
-                        out=acc[:],
-                        lhsT=src_words[a][:, cols].bitcast(FP8X4),
-                        lhsT_scale=src_sc[ROWS * a :, cols],
-                        rhs=ws[b][:, a, :].bitcast(FP8X4),
-                        rhs_scale=w_sc[:, a, :].bitcast(U8)[ROWS:, r_cols],
-                        start=(a == 0),
-                        stop=False,
-                    )
-                for a in range(PASSES):
-                    nc.tensor.matmul_mx(
-                        out=acc[:],
-                        lhsT=dst_words[a][:, cols].bitcast(FP8X4),
-                        lhsT_scale=dst_planes[a],
-                        rhs=wt[:, a, SPAN // 2 * b : SPAN // 2 * (b + 1)].bitcast(U8).bitcast(FP4X4),
-                        rhs_scale=w_sc[:, a, :].bitcast(U8)[:, r_cols],
-                        start=False,
-                        stop=(a == PASSES - 1),
-                    )
-                nc.scalar.copy(rows[jt][:, b], acc[:].rearrange("j (p u e) -> j u p e", u=2, e=2))
+                for step in range(2 * PASSES):
+                    first_pass(acc, jt, b, step)
+                round_sum(acc, jt, b)
+
+        def first_part():
+            accs = {(jt, b): sums.tile([P, SPAN], F32, name="acc") for jt in range(tiles) for b in range(PASSES)}
+            for b in range(PASSES):
+                for step in range(PASSES):
+                    for jt in range(tiles):
+                        first_pass(accs[jt, b], jt, b, step)
+            for jt in range(tiles):
+                for b in range(PASSES):
+                    for step in range(PASSES, 2 * PASSES):
+                        first_pass(accs[jt, b], jt, b, step)
+                    round_sum(accs[jt, b], jt, b)
 
         def turn_h(jt):
             q, c = divmod(jt, PART // P)
@@ -270,9 +287,7 @@ def tile_list_msg_none_resL_kernel(
         quantize_wd(0, PAIR)
         new_rows()
         new_rows()
-        for b in range(PASSES):
-            for jt in range(tiles):
-                first_product(jt, [b])
+        first_part()
         turn_part(0)
         quantize_h(0)
         result.append(keep.tile([P, T], F32, name="h_bf0", align_bytes=64))
@@ -288,15 +303,25 @@ def tile_list_msg_none_resL_kernel(
         for q in range(1, PARTS):
             quantize_h(q)
             third_piece(q - 1, keep.tile([P, PART], F32, name="h_bf%d" % q, align_bytes=64))
-            if q + 1 < PARTS:
-                for jt in range(tiles * (q + 1), tiles * (q + 2)):
-                    whole_tile(jt)
-                turn_part(q + 1)
+            last = q + 1 == PARTS
+            if not last:
+                whole_tile(tiles * (q + 1))
             pair_message(q)
             third_message(q)
-            first_pair(q)
-        third_piece(PARTS - 1, pieces.tile([P, PART], F32, name="total"))
-        store(PAIR)
+            if not last:
+                first_pair(q)
+                whole_tile(tiles * (q + 1) + 1)
+                turn_part(q + 1)
+        at = J - PART
+        totals = [pieces.tile([P, PART], F32, name="total") for i in range(PAIR + 1)]
+        add_state(totals[0][:], 0, at, PART)
+        put(0, at, PART, totals[0][:])
+        store(0)
+        for i in (1, 2):
+            add_state(totals[i][:], i, at, PART)
+        for i in (1, 2):
+            put(i, at, PART, totals[i][:])
+            store(i)
         quantize_wd(PAIR + 1, 1)
         own = keep.tile([P, EDGE_TILES, P], F32, name="own")
         turned = keep.tile([P, EDGE_TILES, P], F32, name="turned")

@@ -58,7 +58,7 @@ def tile_list_msg_none_resL_kernel(
         wt = keep.tile([P, PASSES, R // 2], I32, name="wt", align_bytes=64)
         ident = keep.tile([P, P], F32, name="ident")
         edge_w = keep.tile([P, J], F32, name="edge_w")
-        result = [keep.tile([P, T], F32, name="result%d" % i) for i in range(PAIR)]
+        result = [keep.tile([P, T], F32, name="result%d" % i) for i in range(PAIR + 1)]
 
         nc.sync.dma_start(dst[:], offs2)
         nc.sync.dma_start(src[:], offs)
@@ -127,7 +127,7 @@ def tile_list_msg_none_resL_kernel(
         h_bf = [keep.tile([P, PASSES, PART, PACK], BF16, name="h_bf%d" % q, align_bytes=64) for q in range(PARTS)]
         src_words = [keep.tile([P, J], U32, name="src_words%d" % a, align_bytes=64) for a in range(PASSES)]
         dst_words = [keep.tile([P, J], U32, name="dst_words%d" % a, align_bytes=64) for a in range(PASSES)]
-        message = keep.tile([P, ROW_TILES - 1, J], F32, name="message")
+        message = keep.tile([P, PAIR, J], F32, name="message")
         last_total = keep.tile([P, J], F32, name="last_total")
 
         def entries(offsets, first, count):
@@ -231,9 +231,8 @@ def tile_list_msg_none_resL_kernel(
                     )
 
         def add_state(total, i, first, count):
-            nc.vector.tensor_tensor(
-                total, state[i][:].indirect(entries(dst, first, count)), message[:, i, first : first + count], ADD
-            )
+            y = third[first // PART][:] if i == PAIR else message[:, i, first : first + count]
+            nc.vector.tensor_tensor(total, state[i][:].indirect(entries(dst, first, count)), y, ADD)
 
         def put(i, first, count, total):
             nc.vector.tensor_tensor(
@@ -249,20 +248,24 @@ def tile_list_msg_none_resL_kernel(
 
         for first, count in ((0, PART), (PART, PART), (HALF, HALF)):
             gather_words(first, count)
-        picked = keep.tile([P, J], F32, name="picked")
-        nc.vector.tensor_copy(picked[:], state[PAIR + 1][:].indirect(dst[:]))
+        picked = [keep.tile([P, HALF], F32, name="picked")]
+        nc.vector.tensor_copy(picked[0][:], state[PAIR + 1][:].indirect(entries(dst, 0, HALF)))
 
         def third_message(q):
             bank = ys.tile([P, 1, PART], F32, name="y_third")
             messages(bank, [(PAIR, q)])
-            nc.scalar.copy(message[:, PAIR, q * PART : (q + 1) * PART], bank[:, 0, :])
+            third_banks.append(bank)
+
+        def take_third(q, name):
+            third.append(keep.tile([P, PART], F32, name=name, align_bytes=64))
+            nc.scalar.copy(third[q][:], third_banks[q][:, 0, :])
 
         def whole_tile(jt):
-            rows.append(rounded.tile([P, PASSES, 2, P, 2], BF16, name="rows", align_bytes=64))
+            rows.append(keep.tile([P, PASSES, 2, P, 2], BF16, name="rows%d" % len(rows), align_bytes=64))
             first_product(jt, range(PASSES))
 
         def new_rows():
-            rows.append(rounded.tile([P, PASSES, 2, P, 2], BF16, name="rows", align_bytes=64))
+            rows.append(keep.tile([P, PASSES, 2, P, 2], BF16, name="rows%d" % len(rows), align_bytes=64))
 
         def turn_part(q):
             for jt in range(tiles * q, tiles * (q + 1)):
@@ -284,14 +287,16 @@ def tile_list_msg_none_resL_kernel(
 
         tiles = PART // P
         rows = []
+        third_banks = []
+        third = []
         quantize_wd(0, PAIR)
         new_rows()
         new_rows()
         first_part()
         turn_part(0)
         quantize_h(0)
-        result.append(keep.tile([P, T], F32, name="h_bf0", align_bytes=64))
-        nc.vector.memset(result[PAIR][:].bitcast(I32), 0)
+        picked.append(keep.tile([P, HALF], F32, name="h_bf0", align_bytes=64))
+        nc.vector.tensor_copy(picked[1][:], state[PAIR + 1][:].indirect(entries(dst, HALF, HALF)))
         result.append(result[0])
         quantize_wd(PAIR, 1)
         whole_tile(2)
@@ -302,7 +307,8 @@ def tile_list_msg_none_resL_kernel(
         turn_part(1)
         for q in range(1, PARTS):
             quantize_h(q)
-            third_piece(q - 1, keep.tile([P, PART], F32, name="h_bf%d" % q, align_bytes=64))
+            take_third(q - 1, "rows%d" % (tiles * q + 1))
+            third_piece(q - 1, pieces.tile([P, PART], F32, name="total"))
             last = q + 1 == PARTS
             if not last:
                 whole_tile(tiles * (q + 1))
@@ -312,6 +318,7 @@ def tile_list_msg_none_resL_kernel(
                 first_pair(q)
                 whole_tile(tiles * (q + 1) + 1)
                 turn_part(q + 1)
+        take_third(PARTS - 1, "third_last")
         at = J - PART
         totals = [pieces.tile([P, PART], F32, name="total") for i in range(PAIR + 1)]
         add_state(totals[0][:], 0, at, PART)
@@ -330,7 +337,7 @@ def tile_list_msg_none_resL_kernel(
             bank = sums.tile([P, HALF_TILES, P], F32, name="acc")
             for c in range(HALF_TILES):
                 jt = half * HALF_TILES + c
-                nc.tensor.transpose(bank[:, c, :], picked[:, P * jt : P * (jt + 1)], ident[:])
+                nc.tensor.transpose(bank[:, c, :], picked[half][:, P * c : P * (c + 1)], ident[:])
             nc.scalar.copy(own[:, jts, :], bank[:])
         for half in range(J // HALF):
             jts = slice(half * HALF_TILES, (half + 1) * HALF_TILES)

@@ -70,6 +70,17 @@ def tile_list_msg_none_resL_kernel(
         for tile in result[1:]:
             nc.vector.memset(tile[:].bitcast(I32), 0)
 
+        groups = ((0, PAIR), (PAIR, 1), (PAIR + 1, 1))
+        wd_raw = {
+            first: [keep.tile([P, PACK, count * P], F32, name="wd_raw%d%d" % (first, b)) for b in range(PASSES)]
+            for first, count in groups
+        }
+
+        def load_wd(first, count, passes):
+            for b in passes:
+                rows = wd[SPAN * b : SPAN * (b + 1), P * first : P * (first + count)]
+                nc.sync.dma_start(wd_raw[first][b][:], rows.rearrange("(p t) n -> p t n", t=PACK))
+
         def load_weight_planes(scales, first_row):
             for q in range(QUADS):
                 nc.scalar.dma_start(
@@ -87,22 +98,15 @@ def tile_list_msg_none_resL_kernel(
         ws_rows = ws_words.rearrange("a p r i -> p a (r i)").bitcast(I32)
         load_weight_planes(ws_scales, ROWS)
         nc.sync.dma_start(ws[0][:], ws_rows[:, :, :SPAN])
+        load_wd(0, PAIR, [0])
         nc.sync.dma_start(ws[1][:], ws_rows[:, :, SPAN:])
-        nc.sync.dma_start(wt[:], wt_words.rearrange("a p c -> p a c").bitcast(I32))
         load_weight_planes(wt_scales, 0)
         nc.vector.tensor_copy(dst_sc[:], table_sc[:].bitcast(U8).indirect(dst[:]))
-        nc.scalar.dma_start(w_sc[:SHIFTED, PASSES, :], dst_sc[ROWS : ROWS + SHIFTED, :].bitcast(I32))
+        nc.sync.dma_start(w_sc[:SHIFTED, PASSES, :], dst_sc[ROWS : ROWS + SHIFTED, :].bitcast(I32))
+        nc.sync.dma_start(wt[:], wt_words.rearrange("a p c -> p a c").bitcast(I32))
         nc.vector.tensor_copy(src_sc[:], table_sc[:].bitcast(U8).indirect(src[:]))
 
-        wd_raw = [
-            [keep.tile([P, PACK, PAIR * P], F32, name="wd_raw%d%d" % (g, b)) for b in range(PASSES)] for g in range(PAIR)
-        ]
         state = [keep.tile([P, T], F32, name="state%d" % i) for i in range(ROW_TILES)]
-
-        def load_wd(g):
-            for b in range(PASSES):
-                rows = wd[SPAN * b : SPAN * (b + 1), PAIR * P * g : PAIR * P * (g + 1)]
-                nc.sync.dma_start(wd_raw[g][b][:], rows.rearrange("(p t) n -> p t n", t=PACK))
 
         def load_state(i):
             nc.sync.dma_start(state[i][:], rT[P * i : P * (i + 1), :])
@@ -110,20 +114,19 @@ def tile_list_msg_none_resL_kernel(
         def load_edge_w(first, count):
             nc.sync.dma_start(edge_w[:, first : first + count], wgo[:, first : first + count])
 
-        load_wd(0)
+        load_wd(0, PAIR, [1])
         load_state(3)
-        load_wd(1)
+        load_wd(PAIR, 1, [0, 1])
         load_state(0)
         load_edge_w(0, PART)
         load_state(1)
         load_edge_w(PART, J - PART)
         load_state(2)
+        load_wd(PAIR + 1, 1, [0, 1])
 
         h_codes = keep.tile([P, PARTS, PASSES, PART], U32, name="h_codes", align_bytes=64)
         h_sc = keep.tile([P, PARTS, PASSES, PART], U8, name="h_sc", align_bytes=64)
-        wd_bf = keep.tile([P, ROW_TILES, PASSES, P, PACK], BF16, name="wd_bf", align_bytes=64)
-        wd_codes = keep.tile([P, ROW_TILES, PASSES, P], U32, name="wd_codes", align_bytes=64)
-        wd_sc = keep.tile([P, ROW_TILES, PASSES, P], U8, name="wd_sc", align_bytes=64)
+        wd_mx = {}
         h_bf = [keep.tile([P, PASSES, PART, PACK], BF16, name="h_bf%d" % q, align_bytes=64) for q in range(PARTS)]
         src_words = [keep.tile([P, J], U32, name="src_words%d" % a, align_bytes=64) for a in range(PASSES)]
         dst_words = [keep.tile([P, J], U32, name="dst_words%d" % a, align_bytes=64) for a in range(PASSES)]
@@ -204,17 +207,22 @@ def tile_list_msg_none_resL_kernel(
                 in_=h_bf[q][:].rearrange("p b j t -> p (b j t)"),
             )
 
-        def quantize_wd(first, count):
-            for i in range(first, first + count):
-                g, c = divmod(i, PAIR)
-                for b in range(PASSES):
-                    raw = wd_raw[g][b][:, :, P * c : P * (c + 1)]
-                    nc.scalar.copy(wd_bf[:, i, b], raw.rearrange("p t n -> p n t"))
-            tiles_i = slice(first, first + count)
+        def quantize_wd(first, count, passes, name):
+            bf = keep.tile([P, len(passes), count * P, PACK], BF16, name=name, align_bytes=64)
+            codes = keep.tile([P, len(passes), count * P], U32, name="wd_codes%d%d" % (first, passes[0]), align_bytes=64)
+            scales = keep.tile([P, len(passes), count * P], U8, name="wd_sc%d%d" % (first, passes[0]), align_bytes=64)
+            for k, b in enumerate(passes):
+                nc.scalar.copy(
+                    bf[:, k].rearrange("p (c i) t -> p c t i", i=PACK),
+                    wd_raw[first][b][:].rearrange("p t (c i) -> p c t i", i=PACK),
+                )
+                for i in range(count):
+                    cols = slice(P * i, P * (i + 1))
+                    wd_mx[first + i, b] = (codes[:, k, cols].bitcast(FP8X4), scales[:, k, cols])
             nc.vector.quantize_mx(
-                out=wd_codes[:, tiles_i].rearrange("p i b n -> p (i b n)").bitcast(FP8X4),
-                scales=wd_sc[:, tiles_i].rearrange("p i b n -> p (i b n)"),
-                in_=wd_bf[:, tiles_i].rearrange("p i b n t -> p (i b n t)"),
+                out=codes[:].rearrange("p b n -> p (b n)").bitcast(FP8X4),
+                scales=scales[:].rearrange("p b n -> p (b n)"),
+                in_=bf[:].rearrange("p b n t -> p (b n t)"),
             )
 
         def messages(bank, pairs):
@@ -222,8 +230,8 @@ def tile_list_msg_none_resL_kernel(
                 for b in range(PASSES):
                     nc.tensor.matmul_mx(
                         out=bank[:, c, :],
-                        lhsT=wd_codes[:, i, b, :].bitcast(FP8X4),
-                        lhsT_scale=wd_sc[:, i, b, :],
+                        lhsT=wd_mx[i, b][0],
+                        lhsT_scale=wd_mx[i, b][1],
                         rhs=h_codes[:, q, b, :].bitcast(FP8X4),
                         rhs_scale=h_sc[:, q, b, :],
                         start=(b == 0),
@@ -289,7 +297,7 @@ def tile_list_msg_none_resL_kernel(
         rows = []
         third_banks = []
         third = []
-        quantize_wd(0, PAIR)
+        quantize_wd(0, PAIR, [0, 1], "wd_bf0")
         new_rows()
         new_rows()
         first_part()
@@ -298,12 +306,12 @@ def tile_list_msg_none_resL_kernel(
         picked.append(keep.tile([P, HALF], F32, name="h_bf0", align_bytes=64))
         nc.vector.tensor_copy(picked[1][:], state[PAIR + 1][:].indirect(entries(dst, HALF, HALF)))
         result.append(result[0])
-        quantize_wd(PAIR, 1)
+        quantize_wd(PAIR, 1, [0, 1], "rows1")
         whole_tile(2)
         pair_message(0)
-        third_message(0)
         first_pair(0)
         whole_tile(3)
+        third_message(0)
         turn_part(1)
         for q in range(1, PARTS):
             quantize_h(q)
@@ -313,10 +321,11 @@ def tile_list_msg_none_resL_kernel(
             if not last:
                 whole_tile(tiles * (q + 1))
             pair_message(q)
-            third_message(q)
             if not last:
                 first_pair(q)
                 whole_tile(tiles * (q + 1) + 1)
+            third_message(q)
+            if not last:
                 turn_part(q + 1)
         take_third(PARTS - 1, "third_last")
         at = J - PART
@@ -329,7 +338,7 @@ def tile_list_msg_none_resL_kernel(
         for i in (1, 2):
             put(i, at, PART, totals[i][:])
             store(i)
-        quantize_wd(PAIR + 1, 1)
+        quantize_wd(PAIR + 1, 1, [0, 1], "rows6")
         own = keep.tile([P, EDGE_TILES, P], F32, name="own")
         turned = keep.tile([P, EDGE_TILES, P], F32, name="turned")
         for half in range(J // HALF):
@@ -349,8 +358,8 @@ def tile_list_msg_none_resL_kernel(
                         out=bank[:, c, :],
                         lhsT=h_codes[:, q, b, at : at + P].bitcast(FP8X4),
                         lhsT_scale=h_sc[:, q, b, at : at + P],
-                        rhs=wd_codes[:, PAIR + 1, b, :].bitcast(FP8X4),
-                        rhs_scale=wd_sc[:, PAIR + 1, b, :],
+                        rhs=wd_mx[PAIR + 1, b][0],
+                        rhs_scale=wd_mx[PAIR + 1, b][1],
                         start=(b == 0),
                         stop=(b == PASSES - 1),
                     )

@@ -53,7 +53,7 @@ def tile_list_msg_none_resL_kernel(
         w_sc = keep.tile([P, PASSES + 1, R // WORD], I32, name="w_sc", align_bytes=64)
         dst_sc = keep.tile([P, J], U8, name="dst_sc", align_bytes=64)
         src_sc = keep.tile([P, J], U8, name="src_sc", align_bytes=64)
-        table = keep.tile([P, PASSES, T], I32, name="table", align_bytes=64)
+        table = keep.tile([P, PASSES * T], I32, name="table", align_bytes=64)
         ws = [keep.tile([P, PASSES, SPAN], I32, name="ws%d" % b, align_bytes=64) for b in range(PASSES)]
         wt = keep.tile([P, PASSES, R // 2], I32, name="wt", align_bytes=64)
         ident = keep.tile([P, P], F32, name="ident")
@@ -94,7 +94,8 @@ def tile_list_msg_none_resL_kernel(
                 tab_scales[:, ROWS * q : ROWS * (q + 1), :].bitcast(I32),
             )
         table_words = tab_words.rearrange("a p t i -> p a (t i)").bitcast(I32)
-        nc.sync.dma_start(table[:], table_words)
+        for a in range(PASSES):
+            nc.sync.dma_start(table[:, T * a : T * (a + 1)], table_words[:, a, :])
         ws_rows = ws_words.rearrange("a p r i -> p a (r i)").bitcast(I32)
         load_weight_planes(ws_scales, ROWS)
         nc.sync.dma_start(ws[0][:], ws_rows[:, :, :SPAN])
@@ -136,11 +137,11 @@ def tile_list_msg_none_resL_kernel(
         def entries(offsets, first, count):
             return offsets[:, first // LIST_ROWS : (first + count) // LIST_ROWS]
 
-        def gather_words(first, count):
+        def gather_words(first, count, spare):
             cols = slice(first, first + count)
-            for words, offsets in ((src_words, src), (dst_words, dst)):
-                for a in range(PASSES):
-                    window = table[:, a, :].bitcast(U32)
+            for a in range(PASSES):
+                window = table[:, T * a : min(T * (a + 1) + spare, PASSES * T)].bitcast(U32)
+                for words, offsets in ((src_words, src), (dst_words, dst)):
                     nc.vector.tensor_copy(words[a][:, cols], window.indirect(entries(offsets, first, count)))
 
         def first_pass(acc, jt, b, step):
@@ -254,8 +255,10 @@ def tile_list_msg_none_resL_kernel(
             add_state(total[:], PAIR, q * PART, PART)
             put(PAIR, q * PART, PART, total[:])
 
-        for first, count in ((0, PART), (PART, PART), (HALF, HALF)):
-            gather_words(first, count)
+        gather_words(0, PART, 0)
+        rest = (J - PART) // 2
+        for first in (PART, PART + rest):
+            gather_words(first, rest, T // 2)
         picked = [keep.tile([P, HALF], F32, name="picked")]
         nc.vector.tensor_copy(picked[0][:], state[PAIR + 1][:].indirect(entries(dst, 0, HALF)))
 
@@ -303,10 +306,10 @@ def tile_list_msg_none_resL_kernel(
         first_part()
         turn_part(0)
         quantize_h(0)
-        picked.append(keep.tile([P, HALF], F32, name="h_bf0", align_bytes=64))
-        nc.vector.tensor_copy(picked[1][:], state[PAIR + 1][:].indirect(entries(dst, HALF, HALF)))
         result.append(result[0])
         quantize_wd(PAIR, 1, [0, 1], "rows1")
+        picked.append(keep.tile([P, HALF], F32, name="wd_raw%d0" % PAIR))
+        nc.vector.tensor_copy(picked[1][:], state[PAIR + 1][:].indirect(entries(dst, HALF, HALF)))
         whole_tile(2)
         pair_message(0)
         first_pair(0)

@@ -82,10 +82,10 @@ def tile_list_msg_none_resL_kernel(
                 nc.sync.dma_start(wd_raw[first][b][:], rows.rearrange("(p t) n -> p t n", t=PACK))
 
         def load_weight_planes(scales, first_row):
-            for q in range(QUADS):
+            for row in range(ROWS):
                 nc.scalar.dma_start(
-                    w_sc[QUAD * q + first_row : QUAD * q + first_row + ROWS, :PASSES, :],
-                    scales[:, ROWS * q : ROWS * (q + 1), :].rearrange("a q r -> q a r").bitcast(I32),
+                    w_sc[first_row + row : P : QUAD, :PASSES, :],
+                    scales[:, row : QUADS * ROWS : ROWS, :].rearrange("a q r -> q a r").bitcast(I32),
                 )
 
         for q in range(QUADS):

@@ -306,7 +306,6 @@ def tile_list_msg_none_resL_kernel(
         first_part()
         turn_part(0)
         quantize_h(0)
-        result.append(result[0])
         quantize_wd(PAIR, 1, [0, 1], "rows1")
         picked.append(keep.tile([P, HALF], F32, name="wd_raw%d0" % PAIR))
         nc.vector.tensor_copy(picked[1][:], state[PAIR + 1][:].indirect(entries(dst, HALF, HALF)))
@@ -318,6 +317,9 @@ def tile_list_msg_none_resL_kernel(
         turn_part(1)
         for q in range(1, PARTS):
             quantize_h(q)
+            if q == 2:
+                result.append(keep.tile([P, T], F32, name="h_bf%d" % q, align_bytes=64))
+                nc.gpsimd.memset(result[PAIR + 1][:].bitcast(I32), 0)
             take_third(q - 1, "rows%d" % (tiles * q + 1))
             third_piece(q - 1, pieces.tile([P, PART], F32, name="total"))
             last = q + 1 == PARTS

@@ -58,13 +58,17 @@ def tile_list_msg_none_resL_kernel(
         wt = keep.tile([P, PASSES, R // 2], I32, name="wt", align_bytes=64)
         ident = keep.tile([P, P], F32, name="ident")
         edge_w = keep.tile([P, J], F32, name="edge_w")
-        result = [keep.tile([P, T], F32, name="result%d" % i) for i in range(PAIR + 1)]
+        w_rows = keep.tile([P, P], F32, name="w_rows")
+        w_cols = keep.tile([P, EDGE_TILES], F32, name="w_cols")
+        result = [keep.tile([P, T], F32, name="result%d" % i) for i in range(PAIR)]
 
         nc.sync.dma_start(dst[:], offs2)
         nc.sync.dma_start(src[:], offs)
         nc.vector.memset(table_sc[:], 0)
         nc.vector.memset(w_sc[:], 0)
         nc.vector.memset(ident[:], 0.0)
+        nc.vector.memset(w_rows[:], 0.0)
+        nc.gpsimd.dma_start(w_rows[:EDGE_TILES, :], wgo[0, :].rearrange("(c p) -> c p", p=P))
         make_identity(nc, ident[:], nomemset=True)
         nc.vector.memset(result[0][:].bitcast(I32), 0)
         for tile in result[1:]:
@@ -112,18 +116,23 @@ def tile_list_msg_none_resL_kernel(
         def load_state(i):
             nc.sync.dma_start(state[i][:], rT[P * i : P * (i + 1), :])
 
-        def load_edge_w(first, count):
-            nc.sync.dma_start(edge_w[:, first : first + count], wgo[:, first : first + count])
-
         load_wd(0, PAIR, [1])
         load_state(3)
         load_wd(PAIR, 1, [0, 1])
-        load_state(0)
-        load_edge_w(0, PART)
-        load_state(1)
-        load_edge_w(PART, J - PART)
         load_state(2)
+        load_state(0)
+        load_state(1)
         load_wd(PAIR + 1, 1, [0, 1])
+
+        bank = sums.tile([P, SPAN], F32, name="acc")
+        nc.tensor.transpose(bank[:, :P], w_rows[:], ident[:])
+        nc.scalar.copy(w_cols[:], bank[:, :EDGE_TILES])
+        for half in range(J // HALF):
+            bank = sums.tile([P, HALF_TILES, P], F32, name="acc")
+            for c in range(HALF_TILES):
+                jt = half * HALF_TILES + c
+                nc.tensor.transpose(bank[:, c, :], w_cols[:, jt : jt + 1].to_broadcast([P, P]), ident[:])
+            nc.scalar.copy(edge_w[:, half * HALF : (half + 1) * HALF], bank[:].rearrange("n c j -> n (c j)"))
 
         h_codes = keep.tile([P, PARTS, PASSES, PART], U32, name="h_codes", align_bytes=64)
         h_sc = keep.tile([P, PARTS, PASSES, PART], U8, name="h_sc", align_bytes=64)
@@ -132,7 +141,8 @@ def tile_list_msg_none_resL_kernel(
         src_words = [keep.tile([P, J], U32, name="src_words%d" % a, align_bytes=64) for a in range(PASSES)]
         dst_words = [keep.tile([P, J], U32, name="dst_words%d" % a, align_bytes=64) for a in range(PASSES)]
         message = keep.tile([P, PAIR, J], F32, name="message")
-        last_total = keep.tile([P, J], F32, name="last_total")
+        last_message = keep.tile([P, J], F32, name="last_message")
+        turned = keep.tile([P, EDGE_TILES, P], F32, name="turned")
 
         def entries(offsets, first, count):
             return offsets[:, first // LIST_ROWS : (first + count) // LIST_ROWS]
@@ -240,8 +250,35 @@ def tile_list_msg_none_resL_kernel(
                     )
 
         def add_state(total, i, first, count):
-            y = third[first // PART][:] if i == PAIR else message[:, i, first : first + count]
+            y = message[:, i, first : first + count]
             nc.vector.tensor_tensor(total, state[i][:].indirect(entries(dst, first, count)), y, ADD)
+
+        def weigh_state(i, name):
+            weighted[i] = keep.tile([P, J], F32, name=name)
+            nc.vector.tensor_tensor(weighted[i][:], state[i][:].indirect(dst[:]), edge_w[:], MULT)
+
+        def put_sum(i, first, count, y):
+            nc.vector.tensor_tensor(
+                result[i][:].indirect(entries(dst, first, count)), weighted[i][:, first : first + count], y, ADD
+            )
+
+        def weighted_message(i, jts, edge_major, row_major):
+            for c, jt in enumerate(jts):
+                q, at = divmod(P * jt, PART)
+                for b in range(PASSES):
+                    nc.tensor.matmul_mx(
+                        out=edge_major[:, c, :],
+                        lhsT=h_codes[:, q, b, at : at + P].bitcast(FP8X4),
+                        lhsT_scale=h_sc[:, q, b, at : at + P],
+                        rhs=wd_mx[i, b][0],
+                        rhs_scale=wd_mx[i, b][1],
+                        start=(b == 0),
+                        stop=(b == PASSES - 1),
+                    )
+            for c, jt in enumerate(jts):
+                nc.scalar.activation(turned[:, jt, :], edge_major[:, c, :], COPY, scale=w_cols[:, jt : jt + 1])
+            for c, jt in enumerate(jts):
+                nc.tensor.transpose(row_major[:, c, :], turned[:, jt, :], ident[:])
 
         def put(i, first, count, total):
             nc.vector.tensor_tensor(
@@ -251,25 +288,21 @@ def tile_list_msg_none_resL_kernel(
         def store(i):
             nc.sync.dma_start(out[P * i : P * (i + 1), :], result[i][:])
 
-        def third_piece(q, total):
-            add_state(total[:], PAIR, q * PART, PART)
-            put(PAIR, q * PART, PART, total[:])
-
         gather_words(0, PART, 0)
         rest = (J - PART) // 2
         for first in (PART, PART + rest):
             gather_words(first, rest, T // 2)
-        picked = [keep.tile([P, HALF], F32, name="picked")]
-        nc.vector.tensor_copy(picked[0][:], state[PAIR + 1][:].indirect(entries(dst, 0, HALF)))
+        weighted = {}
+        weigh_state(PAIR + 1, "weighted_last")
 
         def third_message(q):
-            bank = ys.tile([P, 1, PART], F32, name="y_third")
-            messages(bank, [(PAIR, q)])
+            bank = ys.tile([P, 2, tiles, P], F32, name="y_third")
+            weighted_message(PAIR, range(tiles * q, tiles * (q + 1)), bank[:, 0], bank[:, 1])
             third_banks.append(bank)
 
         def take_third(q, name):
             third.append(keep.tile([P, PART], F32, name=name, align_bytes=64))
-            nc.scalar.copy(third[q][:], third_banks[q][:, 0, :])
+            nc.scalar.copy(third[q][:], third_banks[q][:, 1].rearrange("n c j -> n (c j)"))
 
         def whole_tile(jt):
             rows.append(keep.tile([P, PASSES, 2, P, 2], BF16, name="rows%d" % len(rows), align_bytes=64))
@@ -292,9 +325,10 @@ def tile_list_msg_none_resL_kernel(
                     store(c)
 
         def pair_message(q):
-            bank = ys.tile([P, PAIR, PART], F32, name="y_pair")
-            messages(bank, [(c, q) for c in range(PAIR)])
-            nc.scalar.copy(message[:, :PAIR, q * PART : (q + 1) * PART], bank[:])
+            for c, (pool, name) in enumerate(((ys, "y_first"), (banks, "bank"))):
+                bank = pool.tile([P, 1, PART], F32, name=name)
+                messages(bank, [(c, q)])
+                nc.scalar.copy(message[:, c, q * PART : (q + 1) * PART], bank[:, 0, :])
 
         tiles = PART // P
         rows = []
@@ -307,8 +341,9 @@ def tile_list_msg_none_resL_kernel(
         turn_part(0)
         quantize_h(0)
         quantize_wd(PAIR, 1, [0, 1], "rows1")
-        picked.append(keep.tile([P, HALF], F32, name="wd_raw%d0" % PAIR))
-        nc.vector.tensor_copy(picked[1][:], state[PAIR + 1][:].indirect(entries(dst, HALF, HALF)))
+        weigh_state(PAIR, "wd_raw%d0" % PAIR)
+        result.append(keep.tile([P, T], F32, name="rows1", align_bytes=64))
+        nc.gpsimd.memset(result[PAIR][:].bitcast(I32), 0)
         whole_tile(2)
         pair_message(0)
         first_pair(0)
@@ -321,7 +356,7 @@ def tile_list_msg_none_resL_kernel(
                 result.append(keep.tile([P, T], F32, name="h_bf%d" % q, align_bytes=64))
                 nc.gpsimd.memset(result[PAIR + 1][:].bitcast(I32), 0)
             take_third(q - 1, "rows%d" % (tiles * q + 1))
-            third_piece(q - 1, pieces.tile([P, PART], F32, name="total"))
+            put_sum(PAIR, (q - 1) * PART, PART, third[q - 1][:])
             last = q + 1 == PARTS
             if not last:
                 whole_tile(tiles * (q + 1))
@@ -332,49 +367,17 @@ def tile_list_msg_none_resL_kernel(
             third_message(q)
             if not last:
                 turn_part(q + 1)
+        first_pair(PARTS - 1)
         take_third(PARTS - 1, "third_last")
-        at = J - PART
-        totals = [pieces.tile([P, PART], F32, name="total") for i in range(PAIR + 1)]
-        add_state(totals[0][:], 0, at, PART)
-        put(0, at, PART, totals[0][:])
-        store(0)
-        for i in (1, 2):
-            add_state(totals[i][:], i, at, PART)
-        for i in (1, 2):
-            put(i, at, PART, totals[i][:])
-            store(i)
+        put_sum(PAIR, J - PART, PART, third[PARTS - 1][:])
+        store(PAIR)
         quantize_wd(PAIR + 1, 1, [0, 1], "rows6")
-        own = keep.tile([P, EDGE_TILES, P], F32, name="own")
-        turned = keep.tile([P, EDGE_TILES, P], F32, name="turned")
         for half in range(J // HALF):
-            jts = slice(half * HALF_TILES, (half + 1) * HALF_TILES)
-            bank = sums.tile([P, HALF_TILES, P], F32, name="acc")
-            for c in range(HALF_TILES):
-                jt = half * HALF_TILES + c
-                nc.tensor.transpose(bank[:, c, :], picked[half][:, P * c : P * (c + 1)], ident[:])
-            nc.scalar.copy(own[:, jts, :], bank[:])
-        for half in range(J // HALF):
-            jts = slice(half * HALF_TILES, (half + 1) * HALF_TILES)
-            bank = sums.tile([P, HALF_TILES, P], F32, name="acc")
-            for c in range(HALF_TILES):
-                q, at = divmod(P * (half * HALF_TILES + c), PART)
-                for b in range(PASSES):
-                    nc.tensor.matmul_mx(
-                        out=bank[:, c, :],
-                        lhsT=h_codes[:, q, b, at : at + P].bitcast(FP8X4),
-                        lhsT_scale=h_sc[:, q, b, at : at + P],
-                        rhs=wd_mx[PAIR + 1, b][0],
-                        rhs_scale=wd_mx[PAIR + 1, b][1],
-                        start=(b == 0),
-                        stop=(b == PASSES - 1),
-                    )
-            nc.scalar.copy(turned[:, jts, :], bank[:])
-        for half in range(J // HALF):
-            bank = sums.tile([P, HALF_TILES, P], F32, name="acc")
-            for c in range(HALF_TILES):
-                jt = half * HALF_TILES + c
-                for first, term in ((True, own[:, jt, :]), (False, turned[:, jt, :])):
-                    nc.tensor.matmul(bank[:, c, :], term, ident[:], start=first, stop=not first, is_transpose=True)
-            nc.scalar.copy(last_total[:, half * HALF : (half + 1) * HALF], bank[:].rearrange("n c j -> n (c j)"))
-        put(PAIR + 1, 0, J, last_total[:])
+            edge_major = sums.tile([P, HALF_TILES, P], F32, name="acc")
+            row_major = sums.tile([P, HALF_TILES, P], F32, name="acc")
+            weighted_message(PAIR + 1, range(half * HALF_TILES, (half + 1) * HALF_TILES), edge_major, row_major)
+            nc.scalar.copy(
+                last_message[:, half * HALF : (half + 1) * HALF], row_major[:].rearrange("n c j -> n (c j)")
+            )
+        put_sum(PAIR + 1, 0, J, last_message[:])
         store(PAIR + 1)

@@ -68,7 +68,6 @@ def tile_list_msg_none_resL_kernel(
         nc.vector.memset(w_sc[:], 0)
         nc.vector.memset(ident[:], 0.0)
         nc.vector.memset(w_rows[:], 0.0)
-        nc.gpsimd.dma_start(w_rows[:EDGE_TILES, :], wgo[0, :].rearrange("(c p) -> c p", p=P))
         make_identity(nc, ident[:], nomemset=True)
         nc.vector.memset(result[0][:].bitcast(I32), 0)
         for tile in result[1:]:
@@ -97,6 +96,7 @@ def tile_list_msg_none_resL_kernel(
                 table_sc[QUAD * q : QUAD * q + PASSES * ROWS, :],
                 tab_scales[:, ROWS * q : ROWS * (q + 1), :].bitcast(I32),
             )
+        nc.sync.dma_start(w_rows[:EDGE_TILES, :], wgo[0, :].rearrange("(c p) -> c p", p=P))
         table_words = tab_words.rearrange("a p t i -> p a (t i)").bitcast(I32)
         for a in range(PASSES):
             nc.sync.dma_start(table[:, T * a : T * (a + 1)], table_words[:, a, :])
@@ -344,30 +344,23 @@ def tile_list_msg_none_resL_kernel(
         weigh_state(PAIR, "wd_raw%d0" % PAIR)
         result.append(keep.tile([P, T], F32, name="rows1", align_bytes=64))
         nc.gpsimd.memset(result[PAIR][:].bitcast(I32), 0)
-        whole_tile(2)
-        pair_message(0)
-        first_pair(0)
-        whole_tile(3)
-        third_message(0)
-        turn_part(1)
-        for q in range(1, PARTS):
-            quantize_h(q)
-            if q == 2:
-                result.append(keep.tile([P, T], F32, name="h_bf%d" % q, align_bytes=64))
-                nc.gpsimd.memset(result[PAIR + 1][:].bitcast(I32), 0)
-            take_third(q - 1, "rows%d" % (tiles * q + 1))
-            put_sum(PAIR, (q - 1) * PART, PART, third[q - 1][:])
+        for q in range(PARTS):
+            if q > 0:
+                quantize_h(q)
+                if q == 2:
+                    result.append(keep.tile([P, T], F32, name="h_bf%d" % q, align_bytes=64))
+                    nc.gpsimd.memset(result[PAIR + 1][:].bitcast(I32), 0)
+                take_third(q - 1, "rows%d" % (tiles * q + 1))
+                put_sum(PAIR, (q - 1) * PART, PART, third[q - 1][:])
             last = q + 1 == PARTS
             if not last:
                 whole_tile(tiles * (q + 1))
-            pair_message(q)
-            if not last:
-                first_pair(q)
                 whole_tile(tiles * (q + 1) + 1)
-            third_message(q)
+            pair_message(q)
+            first_pair(q)
             if not last:
                 turn_part(q + 1)
-        first_pair(PARTS - 1)
+            third_message(q)
         take_third(PARTS - 1, "third_last")
         put_sum(PAIR, J - PART, PART, third[PARTS - 1][:])
         store(PAIR)

@@ -65,11 +65,11 @@ def tile_list_msg_none_resL_kernel(
         nc.sync.dma_start(dst[:], offs2)
         nc.sync.dma_start(src[:], offs)
         nc.vector.memset(table_sc[:], 0)
-        nc.vector.memset(w_sc[:], 0)
         nc.vector.memset(ident[:], 0.0)
         nc.vector.memset(w_rows[:], 0.0)
         make_identity(nc, ident[:], nomemset=True)
         nc.vector.memset(result[0][:].bitcast(I32), 0)
+        nc.vector.memset(w_sc[:], 0)
         for tile in result[1:]:
             nc.vector.memset(tile[:].bitcast(I32), 0)
 
@@ -91,7 +91,7 @@ def tile_list_msg_none_resL_kernel(
                     scales[:, row : QUADS * ROWS : ROWS, :].rearrange("a q r -> q a r").bitcast(I32),
                 )
 
-        for q in range(QUADS):
+        for q in (2, 3, 0, 1):
             nc.sync.dma_start(
                 table_sc[QUAD * q : QUAD * q + PASSES * ROWS, :],
                 tab_scales[:, ROWS * q : ROWS * (q + 1), :].bitcast(I32),

@@ -60,7 +60,7 @@ def tile_list_msg_none_resL_kernel(
         edge_w = keep.tile([P, J], F32, name="edge_w")
         w_rows = keep.tile([P, P], F32, name="w_rows")
         w_cols = keep.tile([P, EDGE_TILES], F32, name="w_cols")
-        result = [keep.tile([P, T], F32, name="result%d" % i) for i in range(PAIR)]
+        result = [keep.tile([P, T], F32, name="result0")]
 
         nc.sync.dma_start(dst[:], offs2)
         nc.sync.dma_start(src[:], offs)
@@ -70,8 +70,6 @@ def tile_list_msg_none_resL_kernel(
         make_identity(nc, ident[:], nomemset=True)
         nc.vector.memset(result[0][:].bitcast(I32), 0)
         nc.vector.memset(w_sc[:], 0)
-        for tile in result[1:]:
-            nc.vector.memset(tile[:].bitcast(I32), 0)
 
         groups = ((0, PAIR), (PAIR, 1), (PAIR + 1, 1))
         wd_raw = {
@@ -149,9 +147,9 @@ def tile_list_msg_none_resL_kernel(
 
         def gather_words(first, count, spare):
             cols = slice(first, first + count)
-            for a in range(PASSES):
-                window = table[:, T * a : min(T * (a + 1) + spare, PASSES * T)].bitcast(U32)
-                for words, offsets in ((src_words, src), (dst_words, dst)):
+            for words, offsets in ((src_words, src), (dst_words, dst)):
+                for a in range(PASSES):
+                    window = table[:, T * a : min(T * (a + 1) + spare, PASSES * T)].bitcast(U32)
                     nc.vector.tensor_copy(words[a][:, cols], window.indirect(entries(offsets, first, count)))
 
         def first_pass(acc, jt, b, step):
@@ -289,10 +287,10 @@ def tile_list_msg_none_resL_kernel(
             nc.sync.dma_start(out[P * i : P * (i + 1), :], result[i][:])
 
         gather_words(0, PART, 0)
-        rest = (J - PART) // 2
-        for first in (PART, PART + rest):
-            gather_words(first, rest, T // 2)
+        gather_words(PART, J - PART, T // 2)
         weighted = {}
+        result.append(keep.tile([P, T], F32, name="table", align_bytes=64))
+        nc.gpsimd.memset(result[1][:].bitcast(I32), 0)
         weigh_state(PAIR + 1, "weighted_last")
 
         def third_message(q):

@@ -31,7 +31,8 @@ PARTS = J // PART
 EDGE_TILES = J // P
 HALF_TILES = HALF // P
 ROW_TILES = N // P
-SHIFTED = 100
+LIVE = P - QUAD
+STEPS = (0, 2, 1, 3)
 PAIR = 2
 
 
@@ -50,9 +51,9 @@ def tile_list_msg_none_resL_kernel(
         src = keep.tile([P, J // LIST_ROWS], U16, name="src")
         dst = keep.tile([P, J // LIST_ROWS], U16, name="dst")
         table_sc = keep.tile([P, T // WORD], I32, name="table_sc", align_bytes=64)
-        w_sc = keep.tile([P, PASSES + 1, R // WORD], I32, name="w_sc", align_bytes=64)
-        dst_sc = keep.tile([P, J], U8, name="dst_sc", align_bytes=64)
-        src_sc = keep.tile([P, J], U8, name="src_sc", align_bytes=64)
+        w_sc = keep.tile([P, PASSES, R // WORD], I32, name="w_sc", align_bytes=64)
+        picked_sc = keep.tile([P, 2, J], U8, name="picked_sc", align_bytes=64)
+        planes = [keep.tile([P, 2 * J // WORD], I32, name="planes%d" % a, align_bytes=64) for a in range(PASSES)]
         table = keep.tile([P, PASSES * T], I32, name="table", align_bytes=64)
         ws = [keep.tile([P, PASSES, SPAN], I32, name="ws%d" % b, align_bytes=64) for b in range(PASSES)]
         wt = keep.tile([P, PASSES, R // 2], I32, name="wt", align_bytes=64)
@@ -60,16 +61,18 @@ def tile_list_msg_none_resL_kernel(
         edge_w = keep.tile([P, J], F32, name="edge_w")
         w_rows = keep.tile([P, P], F32, name="w_rows")
         w_cols = keep.tile([P, EDGE_TILES], F32, name="w_cols")
-        result = [keep.tile([P, T], F32, name="result0")]
+        result = []
 
         nc.sync.dma_start(dst[:], offs2)
+        nc.sync.dma_start(table_sc[LIVE:, :], tab_scales.rearrange("a q t -> (a q) t").bitcast(I32))
         nc.sync.dma_start(src[:], offs)
-        nc.vector.memset(table_sc[:], 0)
-        nc.vector.memset(ident[:], 0.0)
         nc.vector.memset(w_rows[:], 0.0)
-        make_identity(nc, ident[:], nomemset=True)
-        nc.vector.memset(result[0][:].bitcast(I32), 0)
         nc.vector.memset(w_sc[:], 0)
+        nc.vector.memset(ident[:], 0.0)
+        nc.vector.memset(table_sc[:LIVE, :], 0)
+        make_identity(nc, ident[:], nomemset=True)
+        for a in range(PASSES):
+            nc.vector.memset(planes[a][:], 0)
 
         groups = ((0, PAIR), (PAIR, 1), (PAIR + 1, 1))
         wd_raw = {
@@ -84,30 +87,33 @@ def tile_list_msg_none_resL_kernel(
 
         def load_weight_planes(scales, first_row):
             for row in range(ROWS):
-                nc.scalar.dma_start(
-                    w_sc[first_row + row : P : QUAD, :PASSES, :],
+                nc.sync.dma_start(
+                    w_sc[first_row + row : P : QUAD],
                     scales[:, row : QUADS * ROWS : ROWS, :].rearrange("a q r -> q a r").bitcast(I32),
                 )
 
-        for q in (2, 3, 0, 1):
-            nc.sync.dma_start(
-                table_sc[QUAD * q : QUAD * q + PASSES * ROWS, :],
-                tab_scales[:, ROWS * q : ROWS * (q + 1), :].bitcast(I32),
-            )
-        nc.sync.dma_start(w_rows[:EDGE_TILES, :], wgo[0, :].rearrange("(c p) -> c p", p=P))
         table_words = tab_words.rearrange("a p t i -> p a (t i)").bitcast(I32)
-        for a in range(PASSES):
-            nc.sync.dma_start(table[:, T * a : T * (a + 1)], table_words[:, a, :])
         ws_rows = ws_words.rearrange("a p r i -> p a (r i)").bitcast(I32)
+        nc.sync.dma_start(table[:, :T], table_words[:, 0, :])
+        nc.sync.dma_start(w_rows[:EDGE_TILES, :], wgo[0, :].rearrange("(c p) -> c p", p=P))
         load_weight_planes(ws_scales, ROWS)
-        nc.sync.dma_start(ws[0][:], ws_rows[:, :, :SPAN])
-        load_wd(0, PAIR, [0])
-        nc.sync.dma_start(ws[1][:], ws_rows[:, :, SPAN:])
+        nc.sync.dma_start(table[:, T:], table_words[:, 1, :])
         load_weight_planes(wt_scales, 0)
-        nc.vector.tensor_copy(dst_sc[:], table_sc[:].bitcast(U8).indirect(dst[:]))
-        nc.sync.dma_start(w_sc[:SHIFTED, PASSES, :], dst_sc[ROWS : ROWS + SHIFTED, :].bitcast(I32))
+        nc.sync.dma_start(ws[0][:], ws_rows[:, :, :SPAN])
         nc.sync.dma_start(wt[:], wt_words.rearrange("a p c -> p a c").bitcast(I32))
-        nc.vector.tensor_copy(src_sc[:], table_sc[:].bitcast(U8).indirect(src[:]))
+        for side, offsets in ((1, dst), (0, src)):
+            nc.vector.tensor_copy(picked_sc[:, side, :], table_sc[:].bitcast(U8).indirect(offsets[:]))
+        picked_rows = picked_sc[:].rearrange("p s j -> p (s j)").bitcast(I32)
+
+        def move_planes(a):
+            first = LIVE + QUADS * ROWS * a
+            for row in range(ROWS):
+                nc.sync.dma_start(planes[a][row:P:QUAD, :], picked_rows[first + row : first + QUADS * ROWS : ROWS, :])
+
+        move_planes(0)
+        load_wd(0, PAIR, [0])
+        move_planes(1)
+        nc.sync.dma_start(ws[1][:], ws_rows[:, :, SPAN:])
 
         state = [keep.tile([P, T], F32, name="state%d" % i) for i in range(ROW_TILES)]
 
@@ -156,12 +162,12 @@ def tile_list_msg_none_resL_kernel(
             cols = slice(P * jt, P * (jt + 1))
             r_cols = slice(SPAN * b, SPAN * (b + 1))
             side, a = divmod(step, PASSES)
+            lhsT_scale = planes[a][:].bitcast(U8)[:, J * side + P * jt : J * side + P * (jt + 1)]
             if side == 0:
-                lhsT, lhsT_scale = src_words[a][:, cols], src_sc[ROWS * a :, cols]
+                lhsT = src_words[a][:, cols]
                 rhs, rhs_scale = ws[b][:, a, :].bitcast(FP8X4), w_sc[:, a, :].bitcast(U8)[ROWS:, r_cols]
             else:
                 lhsT = dst_words[a][:, cols]
-                lhsT_scale = [dst_sc[:, cols], w_sc[:, PASSES, :].bitcast(U8)[:, cols]][a]
                 rhs = wt[:, a, SPAN // 2 * b : SPAN // 2 * (b + 1)].bitcast(U8).bitcast(FP4X4)
                 rhs_scale = w_sc[:, a, :].bitcast(U8)[:, r_cols]
             nc.tensor.matmul_mx(
@@ -170,8 +176,8 @@ def tile_list_msg_none_resL_kernel(
                 lhsT_scale=lhsT_scale,
                 rhs=rhs,
                 rhs_scale=rhs_scale,
-                start=(step == 0),
-                stop=(step == 2 * PASSES - 1),
+                start=(step == STEPS[0]),
+                stop=(step == STEPS[-1]),
             )
 
         def round_sum(acc, jt, b):
@@ -180,19 +186,18 @@ def tile_list_msg_none_resL_kernel(
         def first_product(jt, passes):
             for b in passes:
                 acc = sums.tile([P, SPAN], F32, name="acc")
-                for step in range(2 * PASSES):
+                for step in STEPS:
                     first_pass(acc, jt, b, step)
                 round_sum(acc, jt, b)
 
         def first_part():
             accs = {(jt, b): sums.tile([P, SPAN], F32, name="acc") for jt in range(tiles) for b in range(PASSES)}
             for b in range(PASSES):
-                for step in range(PASSES):
+                for step in STEPS[:2]:
                     for jt in range(tiles):
                         first_pass(accs[jt, b], jt, b, step)
-            for jt in range(tiles):
-                for b in range(PASSES):
-                    for step in range(PASSES, 2 * PASSES):
+                for jt in range(tiles):
+                    for step in STEPS[2:]:
                         first_pass(accs[jt, b], jt, b, step)
                     round_sum(accs[jt, b], jt, b)
 
@@ -290,7 +295,7 @@ def tile_list_msg_none_resL_kernel(
         gather_words(PART, J - PART, T // 2)
         weighted = {}
         result.append(keep.tile([P, T], F32, name="table", align_bytes=64))
-        nc.gpsimd.memset(result[1][:].bitcast(I32), 0)
+        nc.gpsimd.memset(result[0][:].bitcast(I32), 0)
         weigh_state(PAIR + 1, "weighted_last")
 
         def third_message(q):
@@ -341,6 +346,8 @@ def tile_list_msg_none_resL_kernel(
         quantize_wd(PAIR, 1, [0, 1], "rows1")
         weigh_state(PAIR, "wd_raw%d0" % PAIR)
         result.append(keep.tile([P, T], F32, name="rows1", align_bytes=64))
+        nc.gpsimd.memset(result[1][:].bitcast(I32), 0)
+        result.append(keep.tile([P, T], F32, name="state%d" % PAIR))
         nc.gpsimd.memset(result[PAIR][:].bitcast(I32), 0)
         for q in range(PARTS):
             if q > 0:

@@ -55,7 +55,7 @@ def tile_list_msg_none_resL_kernel(
         picked_sc = keep.tile([P, 2, J], U8, name="picked_sc", align_bytes=64)
         planes = [keep.tile([P, 2 * J // WORD], I32, name="planes%d" % a, align_bytes=64) for a in range(PASSES)]
         table = keep.tile([P, PASSES * T], I32, name="table", align_bytes=64)
-        ws = [keep.tile([P, PASSES, SPAN], I32, name="ws%d" % b, align_bytes=64) for b in range(PASSES)]
+        ws = [keep.tile([P, R], I32, name="ws%d" % a, align_bytes=64) for a in range(PASSES)]
         wt = keep.tile([P, PASSES, R // 2], I32, name="wt", align_bytes=64)
         ident = keep.tile([P, P], F32, name="ident")
         edge_w = keep.tile([P, J], F32, name="edge_w")
@@ -76,7 +76,7 @@ def tile_list_msg_none_resL_kernel(
 
         groups = ((0, PAIR), (PAIR, 1), (PAIR + 1, 1))
         wd_raw = {
-            first: [keep.tile([P, PACK, count * P], F32, name="wd_raw%d%d" % (first, b)) for b in range(PASSES)]
+            first: [keep.tile([P, PACK, count * P], F32, name="wd_raw%d%d" % (first, b), align_bytes=64) for b in range(PASSES)]
             for first, count in groups
         }
 
@@ -99,8 +99,7 @@ def tile_list_msg_none_resL_kernel(
         load_weight_planes(ws_scales, ROWS)
         nc.sync.dma_start(table[:, T:], table_words[:, 1, :])
         load_weight_planes(wt_scales, 0)
-        nc.sync.dma_start(ws[0][:], ws_rows[:, :, :SPAN])
-        nc.sync.dma_start(wt[:], wt_words.rearrange("a p c -> p a c").bitcast(I32))
+        nc.sync.dma_start(ws[0][:], ws_rows[:, 0, :])
         for side, offsets in ((1, dst), (0, src)):
             nc.vector.tensor_copy(picked_sc[:, side, :], table_sc[:].bitcast(U8).indirect(offsets[:]))
         picked_rows = picked_sc[:].rearrange("p s j -> p (s j)").bitcast(I32)
@@ -111,17 +110,17 @@ def tile_list_msg_none_resL_kernel(
                 nc.sync.dma_start(planes[a][row:P:QUAD, :], picked_rows[first + row : first + QUADS * ROWS : ROWS, :])
 
         move_planes(0)
-        load_wd(0, PAIR, [0])
+        nc.sync.dma_start(wt[:], wt_words.rearrange("a p c -> p a c").bitcast(I32))
+        nc.sync.dma_start(ws[1][:], ws_rows[:, 1, :])
         move_planes(1)
-        nc.sync.dma_start(ws[1][:], ws_rows[:, :, SPAN:])
 
-        state = [keep.tile([P, T], F32, name="state%d" % i) for i in range(ROW_TILES)]
+        state = [keep.tile([P, T], F32, name="state%d" % i, align_bytes=64) for i in range(ROW_TILES)]
 
         def load_state(i):
             nc.sync.dma_start(state[i][:], rT[P * i : P * (i + 1), :])
 
-        load_wd(0, PAIR, [1])
         load_state(3)
+        load_wd(0, PAIR, [0, 1])
         load_wd(PAIR, 1, [0, 1])
         load_state(2)
         load_state(0)
@@ -153,8 +152,8 @@ def tile_list_msg_none_resL_kernel(
 
         def gather_words(first, count, spare):
             cols = slice(first, first + count)
-            for words, offsets in ((src_words, src), (dst_words, dst)):
-                for a in range(PASSES):
+            for a in range(PASSES):
+                for words, offsets in ((src_words, src), (dst_words, dst)):
                     window = table[:, T * a : min(T * (a + 1) + spare, PASSES * T)].bitcast(U32)
                     nc.vector.tensor_copy(words[a][:, cols], window.indirect(entries(offsets, first, count)))
 
@@ -165,7 +164,7 @@ def tile_list_msg_none_resL_kernel(
             lhsT_scale = planes[a][:].bitcast(U8)[:, J * side + P * jt : J * side + P * (jt + 1)]
             if side == 0:
                 lhsT = src_words[a][:, cols]
-                rhs, rhs_scale = ws[b][:, a, :].bitcast(FP8X4), w_sc[:, a, :].bitcast(U8)[ROWS:, r_cols]
+                rhs, rhs_scale = ws[a][:, r_cols].bitcast(FP8X4), w_sc[:, a, :].bitcast(U8)[ROWS:, r_cols]
             else:
                 lhsT = dst_words[a][:, cols]
                 rhs = wt[:, a, SPAN // 2 * b : SPAN // 2 * (b + 1)].bitcast(U8).bitcast(FP4X4)
@@ -192,11 +191,12 @@ def tile_list_msg_none_resL_kernel(
 
         def first_part():
             accs = {(jt, b): sums.tile([P, SPAN], F32, name="acc") for jt in range(tiles) for b in range(PASSES)}
-            for b in range(PASSES):
-                for step in STEPS[:2]:
+            for step in STEPS[:2]:
+                for b in range(PASSES):
                     for jt in range(tiles):
                         first_pass(accs[jt, b], jt, b, step)
-                for jt in range(tiles):
+            for jt in range(tiles):
+                for b in range(PASSES):
                     for step in STEPS[2:]:
                         first_pass(accs[jt, b], jt, b, step)
                     round_sum(accs[jt, b], jt, b)
@@ -221,9 +221,9 @@ def tile_list_msg_none_resL_kernel(
                 in_=h_bf[q][:].rearrange("p b j t -> p (b j t)"),
             )
 
-        def quantize_wd(first, count, passes, name):
+        def quantize_wd(first, count, passes, name, codes_name):
             bf = keep.tile([P, len(passes), count * P, PACK], BF16, name=name, align_bytes=64)
-            codes = keep.tile([P, len(passes), count * P], U32, name="wd_codes%d%d" % (first, passes[0]), align_bytes=64)
+            codes = keep.tile([P, len(passes), count * P], U32, name=codes_name, align_bytes=64)
             scales = keep.tile([P, len(passes), count * P], U8, name="wd_sc%d%d" % (first, passes[0]), align_bytes=64)
             for k, b in enumerate(passes):
                 nc.scalar.copy(
@@ -257,7 +257,7 @@ def tile_list_msg_none_resL_kernel(
             nc.vector.tensor_tensor(total, state[i][:].indirect(entries(dst, first, count)), y, ADD)
 
         def weigh_state(i, name):
-            weighted[i] = keep.tile([P, J], F32, name=name)
+            weighted[i] = keep.tile([P, J], F32, name=name, align_bytes=64)
             nc.vector.tensor_tensor(weighted[i][:], state[i][:].indirect(dst[:]), edge_w[:], MULT)
 
         def put_sum(i, first, count, y):
@@ -308,7 +308,11 @@ def tile_list_msg_none_resL_kernel(
             nc.scalar.copy(third[q][:], third_banks[q][:, 1].rearrange("n c j -> n (c j)"))
 
         def whole_tile(jt):
-            rows.append(keep.tile([P, PASSES, 2, P, 2], BF16, name="rows%d" % len(rows), align_bytes=64))
+            if jt == tiles:
+                both = keep.tile([P, tiles, PASSES, 2, P, 2], BF16, name="wd_raw01", align_bytes=64)
+                rows.extend(both[:, c] for c in range(tiles))
+            elif jt >= 2 * tiles:
+                rows.append(keep.tile([P, PASSES, 2, P, 2], BF16, name="rows%d" % jt, align_bytes=64))
             first_product(jt, range(PASSES))
 
         def new_rows():
@@ -337,17 +341,17 @@ def tile_list_msg_none_resL_kernel(
         rows = []
         third_banks = []
         third = []
-        quantize_wd(0, PAIR, [0, 1], "wd_bf0")
         new_rows()
         new_rows()
         first_part()
         turn_part(0)
         quantize_h(0)
-        quantize_wd(PAIR, 1, [0, 1], "rows1")
-        weigh_state(PAIR, "wd_raw%d0" % PAIR)
+        quantize_wd(0, PAIR, [0, 1], "rows1", "wd_codes0")
         result.append(keep.tile([P, T], F32, name="rows1", align_bytes=64))
         nc.gpsimd.memset(result[1][:].bitcast(I32), 0)
-        result.append(keep.tile([P, T], F32, name="state%d" % PAIR))
+        weigh_state(PAIR, "weighted_third")
+        quantize_wd(PAIR, 1, [0, 1], "h_bf0", "state%d" % PAIR)
+        result.append(keep.tile([P, T], F32, name="h_bf0", align_bytes=64))
         nc.gpsimd.memset(result[PAIR][:].bitcast(I32), 0)
         for q in range(PARTS):
             if q > 0:
@@ -355,7 +359,7 @@ def tile_list_msg_none_resL_kernel(
                 if q == 2:
                     result.append(keep.tile([P, T], F32, name="h_bf%d" % q, align_bytes=64))
                     nc.gpsimd.memset(result[PAIR + 1][:].bitcast(I32), 0)
-                take_third(q - 1, "rows%d" % (tiles * q + 1))
+                take_third(q - 1, "wd_raw01" if q == 1 else "rows%d" % (tiles * q + 1))
                 put_sum(PAIR, (q - 1) * PART, PART, third[q - 1][:])
             last = q + 1 == PARTS
             if not last:
@@ -369,7 +373,7 @@ def tile_list_msg_none_resL_kernel(
         take_third(PARTS - 1, "third_last")
         put_sum(PAIR, J - PART, PART, third[PARTS - 1][:])
         store(PAIR)
-        quantize_wd(PAIR + 1, 1, [0, 1], "rows6")
+        quantize_wd(PAIR + 1, 1, [0, 1], "rows6", "wd_codes3")
         for half in range(J // HALF):
             edge_major = sums.tile([P, HALF_TILES, P], F32, name="acc")
             row_major = sums.tile([P, HALF_TILES, P], F32, name="acc")

@@ -280,6 +280,10 @@ def tile_list_msg_none_resL_kernel(
                     )
             for c, jt in enumerate(jts):
                 nc.scalar.activation(turned[:, jt, :], edge_major[:, c, :], COPY, scale=w_cols[:, jt : jt + 1])
+            if row_major is not None:
+                turn_back(jts, row_major)
+
+        def turn_back(jts, row_major):
             for c, jt in enumerate(jts):
                 nc.tensor.transpose(row_major[:, c, :], turned[:, jt, :], ident[:])
 
@@ -300,7 +304,7 @@ def tile_list_msg_none_resL_kernel(
 
         def third_message(q):
             bank = ys.tile([P, 2, tiles, P], F32, name="y_third")
-            weighted_message(PAIR, range(tiles * q, tiles * (q + 1)), bank[:, 0], bank[:, 1])
+            weighted_message(PAIR, range(tiles * q, tiles * (q + 1)), bank[:, 0], None)
             third_banks.append(bank)
 
         def take_third(q, name):
@@ -367,9 +371,13 @@ def tile_list_msg_none_resL_kernel(
                 whole_tile(tiles * (q + 1) + 1)
             pair_message(q)
             first_pair(q)
+            if q > 0:
+                third_message(q)
             if not last:
                 turn_part(q + 1)
-            third_message(q)
+            if q == 0:
+                third_message(q)
+            turn_back(range(tiles * q, tiles * (q + 1)), third_banks[q][:, 1])
         take_third(PARTS - 1, "third_last")
         put_sum(PAIR, J - PART, PART, third[PARTS - 1][:])
         store(PAIR)

from contextlib import ExitStack

import concourse.mybir as mybir
from concourse.masks import make_identity

K, R, N, T, J = 1024, 1024, 512, 2048, 1024
FLOPS = 2 * (2 * K * R * J + R * N * J)

F32 = mybir.dt.float32
BF16 = mybir.dt.bfloat16
I32 = mybir.dt.int32
U32 = mybir.dt.uint32
U16 = mybir.dt.uint16
U8 = mybir.dt.uint8
FP8X4 = mybir.dt.float8_e4m3fn_x4
FP4X4 = mybir.dt.float4_e2m1fn_x4
ADD = mybir.AluOpType.add
MULT = mybir.AluOpType.mult
COPY = mybir.ActivationFunctionType.Copy

P = 128
PACK = 4
SPAN = P * PACK
PASSES = K // SPAN
WORD = 4
QUADS, QUAD, ROWS = 4, 32, 4
LIST_ROWS = 16
HALF = J // 2
PART = J // 4
PARTS = J // PART
EDGE_TILES = J // P
HALF_TILES = HALF // P
ROW_TILES = N // P
LIVE = P - QUAD
STEPS = (0, 2, 1, 3)
PAIR = 2


def tile_list_msg_none_resL_kernel(
    tc, tab_words, tab_scales, ws_words, ws_scales, wt_words, wt_scales, wd, rT, wgo, offs, offs2, out
):
    nc = tc.nc
    with ExitStack() as ctx:
        keep = ctx.enter_context(tc.tile_pool(name="keep", bufs=1))
        rounded = ctx.enter_context(tc.tile_pool(name="rounded", bufs=4))
        pieces = ctx.enter_context(tc.tile_pool(name="pieces", bufs=4))
        sums = ctx.enter_context(tc.psum_pool(name="sums", bufs=4))
        banks = ctx.enter_context(tc.psum_pool(name="banks", bufs=2))
        ys = ctx.enter_context(tc.psum_pool(name="ys", bufs=1))

        src = keep.tile([P, J // LIST_ROWS], U16, name="src")
        dst = keep.tile([P, J // LIST_ROWS], U16, name="dst")
        table_sc = keep.tile([P, T // WORD], I32, name="table_sc", align_bytes=64)
        w_sc = keep.tile([P, PASSES, R // WORD], I32, name="w_sc", align_bytes=64)
        picked_sc = keep.tile([P, 2, J], U8, name="picked_sc", align_bytes=64)
        planes = [keep.tile([P, 2 * J // WORD], I32, name="planes%d" % a, align_bytes=64) for a in range(PASSES)]
        table = keep.tile([P, PASSES * T], I32, name="table", align_bytes=64)
        ws = [keep.tile([P, R], I32, name="ws%d" % a, align_bytes=64) for a in range(PASSES)]
        wt = keep.tile([P, PASSES, R // 2], I32, name="wt", align_bytes=64)
        ident = keep.tile([P, P], F32, name="ident")
        edge_w = keep.tile([P, J], F32, name="edge_w")
        w_rows = keep.tile([P, P], F32, name="w_rows")
        w_cols = keep.tile([P, EDGE_TILES], F32, name="w_cols")
        result = []

        nc.sync.dma_start(dst[:], offs2)
        nc.sync.dma_start(table_sc[LIVE:, :], tab_scales.rearrange("a q t -> (a q) t").bitcast(I32))
        nc.sync.dma_start(src[:], offs)
        nc.vector.memset(w_rows[:], 0.0)
        nc.vector.memset(w_sc[:], 0)
        nc.vector.memset(ident[:], 0.0)
        nc.vector.memset(table_sc[:LIVE, :], 0)
        make_identity(nc, ident[:], nomemset=True)
        for a in range(PASSES):
            nc.vector.memset(planes[a][:], 0)

        groups = ((0, PAIR), (PAIR, 1), (PAIR + 1, 1))
        wd_raw = {
            first: [keep.tile([P, PACK, count * P], F32, name="wd_raw%d%d" % (first, b), align_bytes=64) for b in range(PASSES)]
            for first, count in groups
        }

        def load_wd(first, count, passes):
            for b in passes:
                rows = wd[SPAN * b : SPAN * (b + 1), P * first : P * (first + count)]
                nc.sync.dma_start(wd_raw[first][b][:], rows.rearrange("(p t) n -> p t n", t=PACK))

        def load_weight_planes(scales, first_row):
            for row in range(ROWS):
                nc.sync.dma_start(
                    w_sc[first_row + row : P : QUAD],
                    scales[:, row : QUADS * ROWS : ROWS, :].rearrange("a q r -> q a r").bitcast(I32),
                )

        table_words = tab_words.rearrange("a p t i -> p a (t i)").bitcast(I32)
        ws_rows = ws_words.rearrange("a p r i -> p a (r i)").bitcast(I32)
        nc.sync.dma_start(table[:, :T], table_words[:, 0, :])
        nc.sync.dma_start(w_rows[:EDGE_TILES, :], wgo[0, :].rearrange("(c p) -> c p", p=P))
        load_weight_planes(ws_scales, ROWS)
        nc.sync.dma_start(table[:, T:], table_words[:, 1, :])
        load_weight_planes(wt_scales, 0)
        nc.sync.dma_start(ws[0][:], ws_rows[:, 0, :])
        for side, offsets in ((1, dst), (0, src)):
            nc.vector.tensor_copy(picked_sc[:, side, :], table_sc[:].bitcast(U8).indirect(offsets[:]))
        picked_rows = picked_sc[:].rearrange("p s j -> p (s j)").bitcast(I32)

        def move_planes(a):
            first = LIVE + QUADS * ROWS * a
            for row in range(ROWS):
                nc.sync.dma_start(planes[a][row:P:QUAD, :], picked_rows[first + row : first + QUADS * ROWS : ROWS, :])

        move_planes(0)
        nc.sync.dma_start(wt[:], wt_words.rearrange("a p c -> p a c").bitcast(I32))
        nc.sync.dma_start(ws[1][:], ws_rows[:, 1, :])
        move_planes(1)

        state = [keep.tile([P, T], F32, name="state%d" % i, align_bytes=64) for i in range(ROW_TILES)]

        def load_state(i):
            nc.sync.dma_start(state[i][:], rT[P * i : P * (i + 1), :])

        load_state(3)
        load_wd(0, PAIR, [0, 1])
        load_wd(PAIR, 1, [0, 1])
        load_state(2)
        load_state(0)
        load_state(1)
        load_wd(PAIR + 1, 1, [0, 1])

        bank = sums.tile([P, SPAN], F32, name="acc")
        nc.tensor.transpose(bank[:, :P], w_rows[:], ident[:])
        nc.scalar.copy(w_cols[:], bank[:, :EDGE_TILES])
        for half in range(J // HALF):
            bank = sums.tile([P, HALF_TILES, P], F32, name="acc")
            for c in range(HALF_TILES):
                jt = half * HALF_TILES + c
                nc.tensor.transpose(bank[:, c, :], w_cols[:, jt : jt + 1].to_broadcast([P, P]), ident[:])
            nc.scalar.copy(edge_w[:, half * HALF : (half + 1) * HALF], bank[:].rearrange("n c j -> n (c j)"))

        h_codes = keep.tile([P, PARTS, PASSES, PART], U32, name="h_codes", align_bytes=64)
        h_sc = keep.tile([P, PARTS, PASSES, PART], U8, name="h_sc", align_bytes=64)
        wd_mx = {}
        h_bf = [keep.tile([P, PASSES, PART, PACK], BF16, name="h_bf%d" % q, align_bytes=64) for q in range(PARTS)]
        src_words = [keep.tile([P, J], U32, name="src_words%d" % a, align_bytes=64) for a in range(PASSES)]
        dst_words = [keep.tile([P, J], U32, name="dst_words%d" % a, align_bytes=64) for a in range(PASSES)]
        message = keep.tile([P, PAIR, J], F32, name="message")
        last_message = keep.tile([P, J], F32, name="last_message")
        turned = keep.tile([P, EDGE_TILES, P], F32, name="turned")

        def entries(offsets, first, count):
            return offsets[:, first // LIST_ROWS : (first + count) // LIST_ROWS]

        def gather_words(first, count, spare):
            cols = slice(first, first + count)
            for a in range(PASSES):
                for words, offsets in ((src_words, src), (dst_words, dst)):
                    window = table[:, T * a : min(T * (a + 1) + spare, PASSES * T)].bitcast(U32)
                    nc.vector.tensor_copy(words[a][:, cols], window.indirect(entries(offsets, first, count)))

        def first_pass(acc, jt, b, step):
            cols = slice(P * jt, P * (jt + 1))
            r_cols = slice(SPAN * b, SPAN * (b + 1))
            side, a = divmod(step, PASSES)
            lhsT_scale = planes[a][:].bitcast(U8)[:, J * side + P * jt : J * side + P * (jt + 1)]
            if side == 0:
                lhsT = src_words[a][:, cols]
                rhs, rhs_scale = ws[a][:, r_cols].bitcast(FP8X4), w_sc[:, a, :].bitcast(U8)[ROWS:, r_cols]
            else:
                lhsT = dst_words[a][:, cols]
                rhs = wt[:, a, SPAN // 2 * b : SPAN // 2 * (b + 1)].bitcast(U8).bitcast(FP4X4)
                rhs_scale = w_sc[:, a, :].bitcast(U8)[:, r_cols]
            nc.tensor.matmul_mx(
                out=acc[:],
                lhsT=lhsT.bitcast(FP8X4),
                lhsT_scale=lhsT_scale,
                rhs=rhs,
                rhs_scale=rhs_scale,
                start=(step == STEPS[0]),
                stop=(step == STEPS[-1]),
            )

        def round_sum(acc, jt, b):
            nc.scalar.copy(rows[jt][:, b], acc[:].rearrange("j (p u e) -> j u p e", u=2, e=2))

        def first_product(jt, passes):
            for b in passes:
                acc = sums.tile([P, SPAN], F32, name="acc")
                for step in STEPS:
                    first_pass(acc, jt, b, step)
                round_sum(acc, jt, b)

        def first_part():
            accs = {(jt, b): sums.tile([P, SPAN], F32, name="acc") for jt in range(tiles) for b in range(PASSES)}
            for step in STEPS[:2]:
                for b in range(PASSES):
                    for jt in range(tiles):
                        first_pass(accs[jt, b], jt, b, step)
            for jt in range(tiles):
                for b in range(PASSES):
                    for step in STEPS[2:]:
                        first_pass(accs[jt, b], jt, b, step)
                    round_sum(accs[jt, b], jt, b)

        def turn_h(jt):
            q, c = divmod(jt, PART // P)
            pairs = rows[jt][:].rearrange("j b u p e -> j (b u p e)").bitcast(F32)
            bank = banks.tile([P, PASSES, 2, P], F32, name="bank")
            for b in range(PASSES):
                for u in range(2):
                    at = P * (2 * b + u)
                    nc.tensor.transpose(bank[:, b, u, :], pairs[:, at : at + P], ident[:])
            nc.scalar.copy(
                h_bf[q][:, :, P * c : P * (c + 1), :].bitcast(F32),
                bank[:].rearrange("p b u j -> p b j u"),
            )

        def quantize_h(q):
            nc.vector.quantize_mx(
                out=h_codes[:, q].rearrange("p b j -> p (b j)").bitcast(FP8X4),
                scales=h_sc[:, q].rearrange("p b j -> p (b j)"),
                in_=h_bf[q][:].rearrange("p b j t -> p (b j t)"),
            )

        def quantize_wd(first, count, passes, name, codes_name):
            bf = keep.tile([P, len(passes), count * P, PACK], BF16, name=name, align_bytes=64)
            codes = keep.tile([P, len(passes), count * P], U32, name=codes_name, align_bytes=64)
            scales = keep.tile([P, len(passes), count * P], U8, name="wd_sc%d%d" % (first, passes[0]), align_bytes=64)
            for k, b in enumerate(passes):
                nc.scalar.copy(
                    bf[:, k].rearrange("p (c i) t -> p c t i", i=PACK),
                    wd_raw[first][b][:].rearrange("p t (c i) -> p c t i", i=PACK),
                )
                for i in range(count):
                    cols = slice(P * i, P * (i + 1))
                    wd_mx[first + i, b] = (codes[:, k, cols].bitcast(FP8X4), scales[:, k, cols])
            nc.vector.quantize_mx(
                out=codes[:].rearrange("p b n -> p (b n)").bitcast(FP8X4),
                scales=scales[:].rearrange("p b n -> p (b n)"),
                in_=bf[:].rearrange("p b n t -> p (b n t)"),
            )

        def messages(bank, pairs):
            for c, (i, q) in enumerate(pairs):
                for b in range(PASSES):
                    nc.tensor.matmul_mx(
                        out=bank[:, c, :],
                        lhsT=wd_mx[i, b][0],
                        lhsT_scale=wd_mx[i, b][1],
                        rhs=h_codes[:, q, b, :].bitcast(FP8X4),
                        rhs_scale=h_sc[:, q, b, :],
                        start=(b == 0),
                        stop=(b == PASSES - 1),
                    )

        def add_state(total, i, first, count):
            y = message[:, i, first : first + count]
            nc.vector.tensor_tensor(total, state[i][:].indirect(entries(dst, first, count)), y, ADD)

        def weigh_state(i, name):
            weighted[i] = keep.tile([P, J], F32, name=name, align_bytes=64)
            nc.vector.tensor_tensor(weighted[i][:], state[i][:].indirect(dst[:]), edge_w[:], MULT)

        def put_sum(i, first, count, y):
            nc.vector.tensor_tensor(
                result[i][:].indirect(entries(dst, first, count)), weighted[i][:, first : first + count], y, ADD
            )

        def weighted_message(i, jts, edge_major, row_major):
            for c, jt in enumerate(jts):
                q, at = divmod(P * jt, PART)
                for b in range(PASSES):
                    nc.tensor.matmul_mx(
                        out=edge_major[:, c, :],
                        lhsT=h_codes[:, q, b, at : at + P].bitcast(FP8X4),
                        lhsT_scale=h_sc[:, q, b, at : at + P],
                        rhs=wd_mx[i, b][0],
                        rhs_scale=wd_mx[i, b][1],
                        start=(b == 0),
                        stop=(b == PASSES - 1),
                    )
            for c, jt in enumerate(jts):
                nc.scalar.activation(turned[:, jt, :], edge_major[:, c, :], COPY, scale=w_cols[:, jt : jt + 1])
            if row_major is not None:
                turn_back(jts, row_major)

        def turn_back(jts, row_major):
            for c, jt in enumerate(jts):
                nc.tensor.transpose(row_major[:, c, :], turned[:, jt, :], ident[:])

        def put(i, first, count, total):
            nc.vector.tensor_tensor(
                result[i][:].indirect(entries(dst, first, count)), total, edge_w[:, first : first + count], MULT
            )

        def store(i):
            nc.sync.dma_start(out[P * i : P * (i + 1), :], result[i][:])

        gather_words(0, PART, 0)
        gather_words(PART, J - PART, T // 2)
        weighted = {}
        result.append(keep.tile([P, T], F32, name="table", align_bytes=64))
        nc.gpsimd.memset(result[0][:].bitcast(I32), 0)
        weigh_state(PAIR + 1, "weighted_last")

        def third_message(q):
            bank = ys.tile([P, 2, tiles, P], F32, name="y_third")
            weighted_message(PAIR, range(tiles * q, tiles * (q + 1)), bank[:, 0], None)
            third_banks.append(bank)

        def take_third(q, name):
            third.append(keep.tile([P, PART], F32, name=name, align_bytes=64))
            nc.scalar.copy(third[q][:], third_banks[q][:, 1].rearrange("n c j -> n (c j)"))

        def whole_tile(jt):
            if jt == tiles:
                both = keep.tile([P, tiles, PASSES, 2, P, 2], BF16, name="wd_raw01", align_bytes=64)
                rows.extend(both[:, c] for c in range(tiles))
            elif jt >= 2 * tiles:
                rows.append(keep.tile([P, PASSES, 2, P, 2], BF16, name="rows%d" % jt, align_bytes=64))
            first_product(jt, range(PASSES))

        def new_rows():
            rows.append(keep.tile([P, PASSES, 2, P, 2], BF16, name="rows%d" % len(rows), align_bytes=64))

        def turn_part(q):
            for jt in range(tiles * q, tiles * (q + 1)):
                turn_h(jt)

        def first_pair(q):
            totals = [pieces.tile([P, PART], F32, name="total") for c in range(PAIR)]
            for c in range(PAIR):
                add_state(totals[c][:], c, q * PART, PART)
            for c in range(PAIR):
                put(c, q * PART, PART, totals[c][:])
                if q == PARTS - 1:
                    store(c)

        def pair_message(q):
            for c, (pool, name) in enumerate(((ys, "y_first"), (banks, "bank"))):
                bank = pool.tile([P, 1, PART], F32, name=name)
                messages(bank, [(c, q)])
                nc.scalar.copy(message[:, c, q * PART : (q + 1) * PART], bank[:, 0, :])

        tiles = PART // P
        rows = []
        third_banks = []
        third = []
        new_rows()
        new_rows()
        first_part()
        turn_part(0)
        quantize_h(0)
        quantize_wd(0, PAIR, [0, 1], "rows1", "wd_codes0")
        result.append(keep.tile([P, T], F32, name="rows1", align_bytes=64))
        nc.gpsimd.memset(result[1][:].bitcast(I32), 0)
        weigh_state(PAIR, "weighted_third")
        quantize_wd(PAIR, 1, [0, 1], "h_bf0", "state%d" % PAIR)
        result.append(keep.tile([P, T], F32, name="h_bf0", align_bytes=64))
        nc.gpsimd.memset(result[PAIR][:].bitcast(I32), 0)
        for q in range(PARTS):
            if q > 0:
                quantize_h(q)
                if q == 2:
                    result.append(keep.tile([P, T], F32, name="h_bf%d" % q, align_bytes=64))
                    nc.gpsimd.memset(result[PAIR + 1][:].bitcast(I32), 0)
                take_third(q - 1, "wd_raw01" if q == 1 else "rows%d" % (tiles * q + 1))
                put_sum(PAIR, (q - 1) * PART, PART, third[q - 1][:])
            last = q + 1 == PARTS
            if not last:
                whole_tile(tiles * (q + 1))
                whole_tile(tiles * (q + 1) + 1)
            pair_message(q)
            first_pair(q)
            if q > 0:
                third_message(q)
            if not last:
                turn_part(q + 1)
            if q == 0:
                third_message(q)
            turn_back(range(tiles * q, tiles * (q + 1)), third_banks[q][:, 1])
        take_third(PARTS - 1, "third_last")
        put_sum(PAIR, J - PART, PART, third[PARTS - 1][:])
        store(PAIR)
        quantize_wd(PAIR + 1, 1, [0, 1], "rows6", "wd_codes3")
        for half in range(J // HALF):
            edge_major = sums.tile([P, HALF_TILES, P], F32, name="acc")
            row_major = sums.tile([P, HALF_TILES, P], F32, name="acc")
            weighted_message(PAIR + 1, range(half * HALF_TILES, (half + 1) * HALF_TILES), edge_major, row_major)
            nc.scalar.copy(
                last_message[:, half * HALF : (half + 1) * HALF], row_major[:].rearrange("n c j -> n (c j)")
            )
        put_sum(PAIR + 1, 0, J, last_message[:])
        store(PAIR + 1)
